import numpy as np
import ml_dtypes


def mxq(x, axis, fmt="e4m3"):
    dtype, down = {"e4m3": (ml_dtypes.float8_e4m3fn, 7), "e5m2": (ml_dtypes.float8_e5m2, 14)}[fmt]
    v = np.moveaxis(np.asarray(x, np.float32).astype(ml_dtypes.bfloat16).astype(np.float64), axis, -1)
    blocks = v.reshape(v.shape[:-1] + (-1, 32))
    amax = np.abs(blocks).max(-1, keepdims=True)
    byte = np.maximum(np.where(amax > 0, np.frexp(amax)[1] - 1 + 127, 0) - down, 1)
    scale = np.exp2(byte - 127.0)
    codes = (blocks / scale).astype(np.float32).astype(dtype).astype(np.float64)
    return np.moveaxis((codes * scale).reshape(v.shape), -1, axis)


WIDE = False


def mx_kscale(k):
    if not WIDE:
        return np.ones(k)
    levels = np.array([10, -10, 5, -5, 0])
    if k % 512:
        return np.exp2(np.random.permutation(np.resize(levels, k // 32))).repeat(32)
    a = np.empty((k // 512, 16))
    for p in range(k // 512):
        a[p, :8] = np.random.permutation(np.resize(levels, 8))
        for g in range(8):
            far = levels[np.abs(levels - a[p, g]) >= 10]
            a[p, g + 8] = far[np.random.randint(len(far))]
    return np.exp2(a.ravel()).repeat(32)


def f64(x):
    return np.asarray(x).astype(np.float64)


def striped(idx):
    return np.tile(idx.reshape(-1, 16).T, (8, 1)).astype(np.uint16)


def unstriped(offs):
    return offs[:16].T.reshape(-1).astype(np.int64)


E2M1 = np.array([0.0, 0.5, 1.0, 1.5, 2.0, 3.0, 4.0, 6.0, -0.0, -0.5, -1.0, -1.5, -2.0, -3.0, -4.0, -6.0])


def pack_weight(w, fmt):
    k, n = w.shape
    w = f64(np.asarray(w, np.float32).astype(ml_dtypes.bfloat16)).reshape(k // 32, 32, n)
    amax = np.abs(w).max(1)
    if fmt == "e4m3":
        byte = np.frexp(amax)[1] - 1 + 127 - 7
    else:
        mant, ex = np.frexp(amax / 6.0)
        byte = np.where(mant > 0.5, ex, ex - 1) + 127
    byte = np.clip(np.where(amax > 0, byte, 1), 1, 254)
    scaled = (w * np.exp2(127.0 - byte)[:, None, :]).reshape(k, n).astype(np.float32)
    by_word = np.ascontiguousarray(scaled.reshape(k // 512, 128, 4, n).transpose(0, 1, 3, 2))
    if fmt == "e4m3":
        words = by_word.astype(ml_dtypes.float8_e4m3fn).view(np.uint8)
    else:
        c = by_word.astype(ml_dtypes.float4_e2m1fn).view(np.uint8) & 0xF
        words = (c[..., 0::2] | (c[..., 1::2] << 4)).reshape(k // 512, 128, 2 * n)
    return np.ascontiguousarray(words), np.ascontiguousarray(byte.astype(np.uint8).reshape(k // 512, 16, n))


def unpack_weight(words, scales, fmt):
    g, _, n = scales.shape
    words = np.ascontiguousarray(words).reshape(g, 128, n, -1)
    if fmt == "e4m3":
        vals = words.view(ml_dtypes.float8_e4m3fn).astype(np.float64)
    else:
        nib = np.empty((g, 128, n, 4), np.uint8)
        nib[..., 0::2] = words & 0xF
        nib[..., 1::2] = words >> 4
        vals = E2M1[nib]
    vals = vals * np.repeat(np.exp2(scales.astype(np.float64) - 127.0), 8, axis=1)[..., None]
    return vals.transpose(0, 1, 3, 2).reshape(g * 512, n)


def gelu(v):
    return 0.5 * v * (1.0 + np.tanh(np.sqrt(2.0 / np.pi) * (v + 0.044715 * v**3)))


K, H, R, N, T, S, T2, P = 1024, 1024, 512, 512, 2048, 1024, 2048, 128

def setup_inputs():
    n = np.random.standard_normal
    s = mx_kscale(K)[:, None]
    u = mx_kscale(H)[:, None]
    tab_words, tab_scales = pack_weight(n((K, T)) * s, "e4m3")
    wg_words, wg_scales = pack_weight(n((K, N)) / np.sqrt(K) / s, "e4m3")
    w3_words, w3_scales = pack_weight(n((R, N)) * np.sqrt(2 / R) / u[:R], "e2m1")
    return {
        "tab_words": tab_words, "tab_scales": tab_scales,
        "offs": striped(np.random.permutation(T)[:S]),
        "w1": (n((K, H)) / np.sqrt(K) / s * u.T).astype(np.float32),
        "wg_words": wg_words, "wg_scales": wg_scales,
        "w3_words": w3_words, "w3_scales": w3_scales,
        "w4": (n((R, N)) * np.sqrt(2 / R) / u[R:]).astype(np.float32),
        "wgo": np.exp(0.3 * n((P, S))).astype(np.float32),
        "offs2": striped(np.random.permutation(T2)[:S]),
    }

def reference(tab_words, tab_scales, offs, w1, wg_words, wg_scales, w3_words, w3_scales, w4, wgo, offs2):
    v = unpack_weight(tab_words, tab_scales, "e4m3")[:, unstriped(offs)]
    wg = unpack_weight(wg_words, wg_scales, "e4m3")
    w3 = unpack_weight(w3_words, w3_scales, "e2m1")
    h = np.maximum(mxq(f64(w1), 0, "e4m3").T @ v, 0)
    hq = mxq(h, 0, "e4m3")
    e1 = w3.T @ hq[:R]
    e2 = mxq(f64(w4), 0, "e4m3").T @ hq[R:]
    g = 1 / (1 + np.exp(-(wg.T @ v)))
    y = e2 + g * (e1 - e2)
    out = np.zeros((N, T2))
    out[:, unstriped(offs2)] = np.tile(f64(wgo), (N // P, 1)) * y
    return out

@@ -1,0 +1,308 @@
+from contextlib import ExitStack
+
+import concourse.mybir as mybir
+
+K, H, R, N, T, S, T2, P = 1024, 1024, 512, 512, 2048, 1024, 2048, 128
+FLOPS = 2 * S * (K * H + K * N + 2 * R * N)
+
+F32 = mybir.dt.float32
+BF16 = mybir.dt.bfloat16
+I32 = mybir.dt.int32
+U32 = mybir.dt.uint32
+U16 = mybir.dt.uint16
+U8 = mybir.dt.uint8
+FP8X4 = mybir.dt.float8_e4m3fn_x4
+FP4X4 = mybir.dt.float4_e2m1fn_x4
+ACT = mybir.ActivationFunctionType
+ALU = mybir.AluOpType
+
+PACK = 4
+K_PASS = P * PACK
+PASSES = K // K_PASS
+QUADS = 4
+LIST_ROWS = 16
+H_CHUNK = 128
+
+
+def tile_list_candidate_expert_blend_kernel(
+    tc, tab_words, tab_scales, offs, w1, wg_words, wg_scales, w3_words, w3_scales, w4, wgo, offs2, out
+):
+    nc = tc.nc
+    with ExitStack() as ctx:
+        keep = ctx.enter_context(tc.tile_pool(name="keep", bufs=1))
+        ring = ctx.enter_context(tc.tile_pool(name="ring", bufs=3))
+        psum = ctx.enter_context(tc.psum_pool(name="psum", bufs=1))
+
+        idx = keep.tile([P, S // LIST_ROWS], U16, name="idx")
+        idx2 = keep.tile([P, S // LIST_ROWS], U16, name="idx2")
+        tab_w = [keep.tile([P, T], I32, name="tab_w%d" % a, align_bytes=64) for a in range(PASSES)]
+        tab_s = keep.tile([P, T // 4], I32, name="tab_s", align_bytes=64)
+        v_w = [keep.tile([P, S], U32, name="v_w%d" % a, align_bytes=64) for a in range(PASSES)]
+        v_s = keep.tile([P, S], U8, name="v_s", align_bytes=64)
+        wg_w = keep.tile([P, PASSES, N], I32, name="wg_w", align_bytes=64)
+        w_s = keep.tile([P, 2, N // 4], I32, name="w_s", align_bytes=64)
+        w3_w = keep.tile([P, 2 * N // 4], I32, name="w3_w", align_bytes=64)
+        gain = keep.tile([P, S], F32, name="gain", align_bytes=64)
+        pieces = [(e, a) for e in range(2) for a in range(PASSES)]
+        w1_raw = {ea: keep.tile([P, PACK, R], F32, name="w1_raw%d%d" % ea, align_bytes=64) for ea in pieces}
+        w1_bf = {ea: keep.tile([P, PACK, P, PACK], BF16, name="w1_bf%d%d" % ea, align_bytes=64) for ea in pieces}
+        w1_c = {ea: keep.tile([P, R], U32, name="w1_c%d%d" % ea, align_bytes=64) for ea in pieces}
+        w1_s = {ea: keep.tile([P, R], U8, name="w1_s%d%d" % ea, align_bytes=64) for ea in pieces}
+        w4_raw = [keep.tile([P, PACK, N // 2], F32, name="w4_raw%d" % u, align_bytes=64) for u in range(2)]
+        w4_bf = [keep.tile([P, N // 2, PACK], BF16, name="w4_bf%d" % u, align_bytes=64) for u in range(2)]
+        w4_c = keep.tile([P, N], U32, name="w4_c", align_bytes=64)
+        w4_s = keep.tile([P, N], U8, name="w4_s", align_bytes=64)
+        spans = [(0, 256), (256, 512), (512, S)]
+        h_bf = {sp: keep.tile([P, 2, sp[1] - sp[0], PACK], BF16, name="h_bf%d" % sp[0], align_bytes=64) for sp in spans}
+        h_c = {sp: keep.tile([P, 2, sp[1] - sp[0]], U32, name="h_c%d" % sp[0], align_bytes=64) for sp in spans}
+        h_s = {sp: keep.tile([P, 2, sp[1] - sp[0]], U8, name="h_s%d" % sp[0], align_bytes=64) for sp in spans}
+        banks = [psum.tile([P, 512], F32, name="bank%d" % b) for b in range(8)]
+        cache = [keep.tile([P, T2], F32, name="cache%d" % nt, align_bytes=64) for nt in range(N // P)]
+        warm = keep.tile([P, 2], F32, name="warm", align_bytes=64)
+
+        nc.gpsimd.memset(tab_s[:], 0)
+        nc.gpsimd.memset(w_s[:], 0)
+        for nt in range(N // P):
+            nc.gpsimd.memset(cache[nt][:], 0.0)
+        nc.vector.memset(warm[:, 0:1], 0.0)
+        nc.scalar.activation(warm[:, 1:2], warm[:, 0:1], ACT.Sigmoid)
+
+        def load_words(dst, src):
+            nc.sync.dma_start(out=dst, in_=src.rearrange("p t i -> p (t i)").bitcast(I32))
+
+        def load_w1(e, a, c0=0, c1=R):
+            rows = w1[a * K_PASS : (a + 1) * K_PASS, e * R + c0 : e * R + c1]
+            nc.sync.dma_start(out=w1_raw[e, a][:, :, c0:c1], in_=rows.rearrange("(p j) c -> p j c", j=PACK))
+
+        def load_wg(u):
+            cols = slice(u * (N // 2), (u + 1) * (N // 2))
+            nc.sync.dma_start(out=wg_w[:, :, cols], in_=wg_words[:, :, cols, :].rearrange("a p e i -> p a (e i)").bitcast(I32))
+
+        def load_w4(u):
+            cols = w4[:, u * (N // 2) : (u + 1) * (N // 2)]
+            nc.sync.dma_start(out=w4_raw[u][:], in_=cols.rearrange("(p j) c -> p j c", j=PACK))
+
+        load_words(tab_w[0][:], tab_words[0])
+        nc.sync.dma_start(idx[:], offs)
+        for q in range(QUADS):
+            nc.sync.dma_start(out=tab_s[32 * q : 32 * q + 8, :], in_=tab_scales[:, 4 * q : 4 * q + 4, :].bitcast(I32))
+        load_w1(0, 0)
+        load_words(tab_w[1][:], tab_words[1])
+        load_w1(0, 1)
+        load_w1(1, 0)
+        for q in range(QUADS):
+            nc.sync.dma_start(out=w_s[32 * q : 32 * q + 8, 0, :], in_=wg_scales[:, 4 * q : 4 * q + 4, :].bitcast(I32))
+        load_w1(1, 1, 0, R // 2)
+        load_w1(1, 1, R // 2, R)
+        load_wg(0)
+        load_w4(0)
+        nc.sync.dma_start(out=w3_w[:], in_=w3_words[0].bitcast(I32))
+        for q in range(QUADS):
+            nc.sync.dma_start(out=w_s[32 * q : 32 * q + 4, 1, :], in_=w3_scales[0, 4 * q : 4 * q + 4, :].bitcast(I32))
+        nc.sync.dma_start(out=gain[:, :256], in_=wgo[:, :256])
+        nc.sync.dma_start(idx2[:], offs2)
+        load_wg(1)
+        load_w4(1)
+        nc.sync.dma_start(out=gain[:, 256:], in_=wgo[:, 256:])
+
+        def entries(lst, j0, j1):
+            return lst[:, j0 // LIST_ROWS : j1 // LIST_ROWS]
+
+        def gather_words(a, j0, j1):
+            nc.vector.tensor_copy(out=v_w[a][:, j0:j1], in_=tab_w[a][:].bitcast(U32).indirect(entries(idx, j0, j1)))
+
+        def gather_scales(j0, j1):
+            nc.vector.tensor_copy(out=v_s[:, j0:j1], in_=tab_s[:].bitcast(U8).indirect(entries(idx, j0, j1)))
+
+        def cast_w1(e, a, m0, m1, copy):
+            src = w1_raw[e, a][:].rearrange("p j (m t) -> p m j t", t=PACK)
+            dst = w1_bf[e, a][:].rearrange("p t m j -> p m j t")
+            copy(dst[:, m0:m1], src[:, m0:m1])
+
+        def quant_w1(e, a, t0=0, t1=PACK):
+            nc.vector.quantize_mx(
+                out=w1_c[e, a][:, t0 * P : t1 * P].bitcast(FP8X4),
+                scales=w1_s[e, a][:, t0 * P : t1 * P],
+                in_=w1_bf[e, a][:, t0:t1].rearrange("p t m j -> p (t m j)"),
+            )
+
+        def quant_w4(u):
+            nc.vector.tensor_scalar_mul(
+                w4_bf[u][:].rearrange("p (c i) j -> p c j i", i=4), w4_raw[u][:].rearrange("p j (c i) -> p c j i", i=4), -1.0
+            )
+            cols = slice(u * (N // 2), (u + 1) * (N // 2))
+            nc.vector.quantize_mx(
+                out=w4_c[:, cols].bitcast(FP8X4), scales=w4_s[:, cols], in_=w4_bf[u][:].rearrange("p c j -> p (c j)")
+            )
+
+        def hidden(e, chunk, b):
+            j0 = chunk * H_CHUNK
+            sp = [x for x in spans if x[0] <= j0 < x[1]][0]
+            cols = slice(j0, j0 + H_CHUNK)
+            bank = banks[b][:].rearrange("p (t n) -> p t n", t=PACK)
+            for t in range(PACK):
+                for a in range(PASSES):
+                    nc.tensor.matmul_mx(
+                        out=bank[:, t, :],
+                        lhsT=w1_c[e, a][:, t * P : (t + 1) * P].bitcast(FP8X4),
+                        lhsT_scale=w1_s[e, a][:, t * P : (t + 1) * P],
+                        rhs=v_w[a][:, cols].bitcast(FP8X4),
+                        rhs_scale=v_s[4 * a : P, cols],
+                        start=(a == 0),
+                        stop=(a == PASSES - 1),
+                    )
+            dst = h_bf[sp][:, e, j0 - sp[0] : j0 - sp[0] + H_CHUNK, :]
+            nc.scalar.activation(dst, bank.rearrange("p t n -> p n t"), ACT.Relu)
+
+        def quant_h(sp, e0, e1):
+            nc.vector.quantize_mx(
+                out=h_c[sp][:, e0:e1, :].rearrange("p e n -> p (e n)").bitcast(FP8X4),
+                scales=h_s[sp][:, e0:e1, :].rearrange("p e n -> p (e n)"),
+                in_=h_bf[sp][:, e0:e1].rearrange("p e n t -> p (e n t)"),
+            )
+
+        def expert1(dst, nt, sp, c0, c1, stop):
+            nc.tensor.matmul_mx(
+                out=dst,
+                lhsT=w3_w[:].bitcast(U8)[:, 2 * nt * P : 2 * (nt + 1) * P].bitcast(FP4X4),
+                lhsT_scale=w_s[:, 1, :].bitcast(U8)[:, nt * P : (nt + 1) * P],
+                rhs=h_c[sp][:, 0, c0:c1].bitcast(FP8X4),
+                rhs_scale=h_s[sp][:, 0, c0:c1],
+                start=True,
+                stop=stop,
+            )
+
+        def expert2_negated(dst, nt, sp, c0, c1, start):
+            nc.tensor.matmul_mx(
+                out=dst,
+                lhsT=w4_c[:, nt * P : (nt + 1) * P].bitcast(FP8X4),
+                lhsT_scale=w4_s[:, nt * P : (nt + 1) * P],
+                rhs=h_c[sp][:, 1, c0:c1].bitcast(FP8X4),
+                rhs_scale=h_s[sp][:, 1, c0:c1],
+                start=start,
+                stop=True,
+            )
+
+        def gate_logits(z, nt, sp):
+            rows = slice(nt * P, (nt + 1) * P)
+            for a in range(PASSES):
+                nc.tensor.matmul_mx(
+                    out=z,
+                    lhsT=wg_w[:, a, rows].bitcast(FP8X4),
+                    lhsT_scale=w_s[4 * a : P, 0, :].bitcast(U8)[:, rows],
+                    rhs=v_w[a][:, sp[0] : sp[1]].bitcast(FP8X4),
+                    rhs_scale=v_s[4 * a : P, sp[0] : sp[1]],
+                    start=(a == 0),
+                    stop=(a == PASSES - 1),
+                )
+
+        def finish(plus, minus, sp):
+            width = sp[1] - sp[0]
+            y = ring.tile([P, width], F32, name="y", bufs=2)
+            nc.gpsimd.tensor_tensor(y[:], plus[:], minus[:], ALU.subtract)
+            weighted = ring.tile([P, width], F32, name="weighted", bufs=4)
+            nc.gpsimd.tensor_tensor(weighted[:], y[:], gain[:, sp[0] : sp[1]], ALU.mult)
+            return weighted
+
+        def first_gates(pair, z):
+            sp = spans[0]
+            width = sp[1] - sp[0]
+            tiles = [(2 * pair + i, slice(i * width, (i + 1) * width)) for i in range(2)]
+            for nt, cols in tiles:
+                gate_logits(z[:, cols], nt, sp)
+            gate = ring.tile([P, 2 * width], F32, name="gate")
+            nc.scalar.activation(gate[:], z[:], ACT.Sigmoid)
+            rest = ring.tile([P, 2 * width], F32, name="rest", bufs=2)
+            nc.scalar.activation(rest[:], z[:], ACT.Sigmoid, scale=-1.0)
+            return gate, rest
+
+        def first_pair(pair, gate, rest, a_bank, b_bank):
+            sp = spans[0]
+            width = sp[1] - sp[0]
+            tiles = [(2 * pair + i, slice(i * width, (i + 1) * width)) for i in range(2)]
+            for nt, cols in tiles:
+                expert1(a_bank[:, cols], nt, sp, 0, width, True)
+            for nt, cols in tiles:
+                expert2_negated(b_bank[:, cols], nt, sp, 0, width, True)
+            done = []
+            for nt, cols in tiles:
+                plus = ring.tile([P, width], F32, name="plus", bufs=4)
+                minus = ring.tile([P, width], F32, name="minus", bufs=4)
+                nc.vector.tensor_tensor(plus[:], a_bank[:, cols], gate[:, cols], ALU.mult)
+                nc.vector.tensor_tensor(minus[:], b_bank[:, cols], rest[:, cols], ALU.mult)
+                done.append((nt, sp[0], sp[1], finish(plus, minus, sp)))
+            return done
+
+        def joint_unit(u, nt, sp):
+            width = sp[1] - sp[0]
+            z = banks[2 + u % 2][:, :width]
+            gate_logits(z, nt, sp)
+            gate = ring.tile([P, width], F32, name="gate")
+            nc.scalar.activation(gate[:], z, ACT.Sigmoid)
+            a_bank, b_bank = banks[6 + u % 2], banks[4 + u % 2]
+            plus = ring.tile([P, width], F32, name="plus", bufs=4)
+            minus = ring.tile([P, width], F32, name="minus", bufs=4)
+            expert2_negated(b_bank[:, :width], nt, sp, 0, width, True)
+            nc.scalar.copy(minus[:], b_bank[:, :width])
+            step = width if width == 512 else 128
+            for c0 in range(0, width, step):
+                expert1(a_bank[:, c0 : c0 + step], nt, sp, c0, c0 + step, False)
+                expert2_negated(a_bank[:, c0 : c0 + step], nt, sp, c0, c0 + step, False)
+            nc.vector.tensor_tensor(plus[:], a_bank[:, :width], gate[:], ALU.mult)
+            return (nt, sp[0], sp[1], finish(plus, minus, sp))
+
+        def scatter(nt, j0, j1, weighted):
+            nc.vector.tensor_copy(out=cache[nt][:].indirect(entries(idx2, j0, j1)), in_=weighted[:])
+
+        half = S // 2
+        split = 84
+        gather_words(0, 0, half)
+        gather_scales(0, half)
+        cast_w1(0, 0, 0, P, nc.scalar.copy)
+        quant_w1(0, 0)
+        gather_words(1, 0, half)
+        gather_words(0, half, S)
+        gather_scales(half, S)
+        gather_words(1, half, S)
+        cast_w1(0, 1, 0, split, nc.vector.tensor_copy)
+        cast_w1(0, 1, split, P, nc.scalar.copy)
+        quant_w1(0, 1)
+        cast_w1(1, 0, 0, P, nc.vector.tensor_copy)
+        quant_w1(1, 0)
+        cast_w1(1, 1, 0, P // 2, nc.vector.tensor_copy)
+        cast_w1(1, 1, P // 2, P, nc.vector.tensor_copy)
+        for t in range(PACK):
+            quant_w1(1, 1, t, t + 1)
+        for chunk in range(3):
+            hidden(0, chunk, chunk)
+        gate, rest = first_gates(0, banks[3])
+        hidden(1, 0, 4)
+        hidden(1, 1, 5)
+        quant_h(spans[0], 1, 2)
+        quant_h(spans[0], 0, 1)
+        quant_w4(0)
+        first = first_pair(0, gate, rest, banks[4], banks[5])
+        gate, rest = first_gates(1, banks[0])
+        quant_w4(1)
+        first += first_pair(1, gate, rest, banks[1], banks[2])
+        hidden(0, 3, 3)
+        hidden(1, 2, 4)
+        hidden(1, 3, 5)
+        scatter(*first[0])
+        quant_h(spans[1], 0, 2)
+        for e, chunk, b in ((1, 4, 0), (0, 4, 1), (0, 5, 2), (1, 5, 3), (0, 6, 4), (1, 6, 5), (0, 7, 0), (1, 7, 1)):
+            hidden(e, chunk, b)
+        scatter(*first[1])
+        scatter(*first[2])
+        pending = first[3]
+        units = [(nt, sp) for sp in spans[1:] for nt in range(N // P)]
+        for u, (nt, sp) in enumerate(units):
+            ready = joint_unit(u, nt, sp)
+            scatter(*pending)
+            if pending[2] == S:
+                nc.sync.dma_start(out=out[pending[0] * P : (pending[0] + 1) * P, :], in_=cache[pending[0]][:])
+            pending = ready
+            if u == 1:
+                quant_h(spans[2], 0, 2)
+        scatter(*pending)
+        nc.sync.dma_start(out=out[pending[0] * P : (pending[0] + 1) * P, :], in_=cache[pending[0]][:])

@@ -22,6 +22,8 @@ PASSES = K // K_PASS
 QUADS = 4
 LIST_ROWS = 16
 H_CHUNK = 128
+BANK = 512
+SPANS = ((0, 256), (256, 512), (512, S))
 
 
 def tile_list_candidate_expert_blend_kernel(
@@ -42,7 +44,7 @@ def tile_list_candidate_expert_blend_kernel(
         wg_w = keep.tile([P, PASSES, N], I32, name="wg_w", align_bytes=64)
         w_s = keep.tile([P, 2, N // 4], I32, name="w_s", align_bytes=64)
         w3_w = keep.tile([P, 2 * N // 4], I32, name="w3_w", align_bytes=64)
-        gain = keep.tile([P, S], F32, name="gain", align_bytes=64)
+        gain = keep.tile([P, len(SPANS), BANK], F32, name="gain", align_bytes=64)
         pieces = [(e, a) for e in range(2) for a in range(PASSES)]
         w1_raw = {ea: keep.tile([P, PACK, R], F32, name="w1_raw%d%d" % ea, align_bytes=64) for ea in pieces}
         w1_bf = {ea: keep.tile([P, PACK, P, PACK], BF16, name="w1_bf%d%d" % ea, align_bytes=64) for ea in pieces}
@@ -52,7 +54,7 @@ def tile_list_candidate_expert_blend_kernel(
         w4_bf = [keep.tile([P, N // 2, PACK], BF16, name="w4_bf%d" % u, align_bytes=64) for u in range(2)]
         w4_c = keep.tile([P, N], U32, name="w4_c", align_bytes=64)
         w4_s = keep.tile([P, N], U8, name="w4_s", align_bytes=64)
-        spans = [(0, 256), (256, 512), (512, S)]
+        spans = SPANS
         h_bf = {sp: keep.tile([P, 2, sp[1] - sp[0], PACK], BF16, name="h_bf%d" % sp[0], align_bytes=64) for sp in spans}
         h_c = {sp: keep.tile([P, 2, sp[1] - sp[0]], U32, name="h_c%d" % sp[0], align_bytes=64) for sp in spans}
         h_s = {sp: keep.tile([P, 2, sp[1] - sp[0]], U8, name="h_s%d" % sp[0], align_bytes=64) for sp in spans}
@@ -82,6 +84,12 @@ def tile_list_candidate_expert_blend_kernel(
             cols = w4[:, u * (N // 2) : (u + 1) * (N // 2)]
             nc.sync.dma_start(out=w4_raw[u][:], in_=cols.rearrange("(p j) c -> p j c", j=PACK))
 
+        def load_gain(i):
+            j0, j1 = spans[i]
+            copies = [P, BANK // (j1 - j0), j1 - j0]
+            dst = gain[:, i, :].rearrange("p (r j) -> p r j", j=j1 - j0)
+            nc.sync.dma_start(out=dst, in_=wgo[:, j0:j1].unsqueeze(1).to_broadcast(copies))
+
         load_words(tab_w[0][:], tab_words[0])
         nc.sync.dma_start(idx[:], offs)
         for q in range(QUADS):
@@ -89,21 +97,22 @@ def tile_list_candidate_expert_blend_kernel(
         load_w1(0, 0)
         load_words(tab_w[1][:], tab_words[1])
         load_w1(0, 1)
-        load_w1(1, 0)
         for q in range(QUADS):
             nc.sync.dma_start(out=w_s[32 * q : 32 * q + 8, 0, :], in_=wg_scales[:, 4 * q : 4 * q + 4, :].bitcast(I32))
+        load_wg(0)
+        load_w1(1, 0)
         load_w1(1, 1, 0, R // 2)
         load_w1(1, 1, R // 2, R)
-        load_wg(0)
         load_w4(0)
+        load_w4(1)
+        load_wg(1)
         nc.sync.dma_start(out=w3_w[:], in_=w3_words[0].bitcast(I32))
         for q in range(QUADS):
             nc.sync.dma_start(out=w_s[32 * q : 32 * q + 4, 1, :], in_=w3_scales[0, 4 * q : 4 * q + 4, :].bitcast(I32))
-        nc.sync.dma_start(out=gain[:, :256], in_=wgo[:, :256])
+        load_gain(0)
         nc.sync.dma_start(idx2[:], offs2)
-        load_wg(1)
-        load_w4(1)
-        nc.sync.dma_start(out=gain[:, 256:], in_=wgo[:, 256:])
+        load_gain(1)
+        load_gain(2)
 
         def entries(lst, j0, j1):
             return lst[:, j0 // LIST_ROWS : j1 // LIST_ROWS]
@@ -196,63 +205,66 @@ def tile_list_candidate_expert_blend_kernel(
                     stop=(a == PASSES - 1),
                 )
 
-        def finish(plus, minus, sp):
+        def parts(unit):
+            nts, sp = unit
             width = sp[1] - sp[0]
-            y = ring.tile([P, width], F32, name="y", bufs=2)
-            nc.gpsimd.tensor_tensor(y[:], plus[:], minus[:], ALU.subtract)
-            weighted = ring.tile([P, width], F32, name="weighted", bufs=4)
-            nc.gpsimd.tensor_tensor(weighted[:], y[:], gain[:, sp[0] : sp[1]], ALU.mult)
+            return [(nt, i * width, (i + 1) * width) for i, nt in enumerate(nts)]
+
+        def sigmoid(b, sign):
+            gate = ring.tile([P, BANK], F32, name="gate", bufs=5)
+            nc.scalar.activation(gate[:], banks[b][:], ACT.Sigmoid, scale=sign)
+            return gate
+
+        def gate_of(unit, b):
+            for nt, c0, c1 in parts(unit):
+                gate_logits(banks[b][:, c0:c1], nt, unit[1])
+            return sigmoid(b, 1.0)
+
+        def difference(unit, b):
+            sp = unit[1]
+            step = BANK if sp[1] - sp[0] == BANK else 128
+            for nt, c0, c1 in parts(unit):
+                for d in range(0, c1 - c0, step):
+                    expert1(banks[b][:, c0 + d : c0 + d + step], nt, sp, d, d + step, False)
+                    expert2_negated(banks[b][:, c0 + d : c0 + d + step], nt, sp, d, d + step, False)
+
+        def gated(b, gate, name, c0=0, c1=BANK):
+            product = ring.tile([P, c1 - c0], F32, name=name, bufs=5)
+            nc.vector.tensor_tensor(product[:], banks[b][:, c0:c1], gate[:, c0:c1], ALU.mult)
+            return product
+
+        def first_expert(unit, b):
+            for nt, c0, c1 in parts(unit):
+                expert1(banks[b][:, c0:c1], nt, unit[1], 0, c1 - c0, True)
+
+        def second_expert(unit, b):
+            for nt, c0, c1 in parts(unit):
+                expert2_negated(banks[b][:, c0:c1], nt, unit[1], 0, c1 - c0, True)
+
+        def minus_e2(unit, b):
+            second_expert(unit, b)
+            minus = ring.tile([P, BANK], F32, name="minus", bufs=5)
+            nc.scalar.copy(minus[:], banks[b][:])
+            return minus
+
+        def weigh(plus, minus, factors, engine):
+            width = factors.shape[1]
+            y = ring.tile([P, width], F32, name="y", bufs=3)
+            engine.tensor_tensor(y[:], plus[:], minus[:], ALU.subtract)
+            weighted = ring.tile([P, width], F32, name="weighted", bufs=5)
+            engine.tensor_tensor(weighted[:], y[:], factors, ALU.mult)
             return weighted
 
-        def first_gates(pair, z):
-            sp = spans[0]
-            width = sp[1] - sp[0]
-            tiles = [(2 * pair + i, slice(i * width, (i + 1) * width)) for i in range(2)]
-            for nt, cols in tiles:
-                gate_logits(z[:, cols], nt, sp)
-            gate = ring.tile([P, 2 * width], F32, name="gate")
-            nc.scalar.activation(gate[:], z[:], ACT.Sigmoid)
-            rest = ring.tile([P, 2 * width], F32, name="rest", bufs=2)
-            nc.scalar.activation(rest[:], z[:], ACT.Sigmoid, scale=-1.0)
-            return gate, rest
-
-        def first_pair(pair, gate, rest, a_bank, b_bank):
-            sp = spans[0]
-            width = sp[1] - sp[0]
-            tiles = [(2 * pair + i, slice(i * width, (i + 1) * width)) for i in range(2)]
-            for nt, cols in tiles:
-                expert1(a_bank[:, cols], nt, sp, 0, width, True)
-            for nt, cols in tiles:
-                expert2_negated(b_bank[:, cols], nt, sp, 0, width, True)
-            done = []
-            for nt, cols in tiles:
-                plus = ring.tile([P, width], F32, name="plus", bufs=4)
-                minus = ring.tile([P, width], F32, name="minus", bufs=4)
-                nc.vector.tensor_tensor(plus[:], a_bank[:, cols], gate[:, cols], ALU.mult)
-                nc.vector.tensor_tensor(minus[:], b_bank[:, cols], rest[:, cols], ALU.mult)
-                done.append((nt, sp[0], sp[1], finish(plus, minus, sp)))
-            return done
-
-        def joint_unit(u, nt, sp):
-            width = sp[1] - sp[0]
-            z = banks[2 + u % 2][:, :width]
-            gate_logits(z, nt, sp)
-            gate = ring.tile([P, width], F32, name="gate")
-            nc.scalar.activation(gate[:], z, ACT.Sigmoid)
-            a_bank, b_bank = banks[6 + u % 2], banks[4 + u % 2]
-            plus = ring.tile([P, width], F32, name="plus", bufs=4)
-            minus = ring.tile([P, width], F32, name="minus", bufs=4)
-            expert2_negated(b_bank[:, :width], nt, sp, 0, width, True)
-            nc.scalar.copy(minus[:], b_bank[:, :width])
-            step = width if width == 512 else 128
-            for c0 in range(0, width, step):
-                expert1(a_bank[:, c0 : c0 + step], nt, sp, c0, c0 + step, False)
-                expert2_negated(a_bank[:, c0 : c0 + step], nt, sp, c0, c0 + step, False)
-            nc.vector.tensor_tensor(plus[:], a_bank[:, :width], gate[:], ALU.mult)
-            return (nt, sp[0], sp[1], finish(plus, minus, sp))
+        def place(unit, plus, minus):
+            sp = unit[1]
+            weighted = weigh(plus, minus, gain[:, spans.index(sp), :], nc.gpsimd)
+            for nt, c0, c1 in parts(unit):
+                scatter(nt, sp[0], sp[1], weighted[:, c0:c1])
+                if sp[1] == S:
+                    nc.sync.dma_start(out=out[nt * P : (nt + 1) * P, :], in_=cache[nt][:])
 
         def scatter(nt, j0, j1, weighted):
-            nc.vector.tensor_copy(out=cache[nt][:].indirect(entries(idx2, j0, j1)), in_=weighted[:])
+            nc.vector.tensor_copy(out=cache[nt][:].indirect(entries(idx2, j0, j1)), in_=weighted)
 
         half = S // 2
         split = 84
@@ -271,38 +283,55 @@ def tile_list_candidate_expert_blend_kernel(
         quant_w1(1, 0)
         cast_w1(1, 1, 0, P // 2, nc.vector.tensor_copy)
         cast_w1(1, 1, P // 2, P, nc.vector.tensor_copy)
-        for t in range(PACK):
-            quant_w1(1, 1, t, t + 1)
-        for chunk in range(3):
+        quant_w1(1, 1)
+        units = [(nts, sp) for sp in spans[:2] for nts in ((0, 1), (2, 3))] + [((nt,), spans[2]) for nt in range(N // P)]
+        for chunk in range(4):
             hidden(0, chunk, chunk)
-        gate, rest = first_gates(0, banks[3])
+        gate = gate_of(units[0], 6)
+        rest = sigmoid(6, -1.0)
         hidden(1, 0, 4)
         hidden(1, 1, 5)
-        quant_h(spans[0], 1, 2)
-        quant_h(spans[0], 0, 1)
+        quant_h(spans[0], 0, 2)
         quant_w4(0)
-        first = first_pair(0, gate, rest, banks[4], banks[5])
-        gate, rest = first_gates(1, banks[0])
         quant_w4(1)
-        first += first_pair(1, gate, rest, banks[1], banks[2])
-        hidden(0, 3, 3)
-        hidden(1, 2, 4)
-        hidden(1, 3, 5)
-        scatter(*first[0])
+        first_expert(units[0], 4)
+        second_expert(units[0], 5)
+        opening = []
+        for (nt, c0, c1), engine in zip(parts(units[0]), (nc.gpsimd, nc.vector)):
+            opening.append((nt, gated(4, gate, "plus", c0, c1), gated(5, rest, "minus", c0, c1), gain[:, 0, c0:c1], engine))
+        opening = [(nt, weigh(plus, minus, factors, engine)) for nt, plus, minus, factors, engine in opening]
+        hidden(1, 2, 0)
+        hidden(1, 3, 1)
         quant_h(spans[1], 0, 2)
-        for e, chunk, b in ((1, 4, 0), (0, 4, 1), (0, 5, 2), (1, 5, 3), (0, 6, 4), (1, 6, 5), (0, 7, 0), (1, 7, 1)):
-            hidden(e, chunk, b)
-        scatter(*first[1])
-        scatter(*first[2])
-        pending = first[3]
-        units = [(nt, sp) for sp in spans[1:] for nt in range(N // P)]
-        for u, (nt, sp) in enumerate(units):
-            ready = joint_unit(u, nt, sp)
-            scatter(*pending)
-            if pending[2] == S:
-                nc.sync.dma_start(out=out[pending[0] * P : (pending[0] + 1) * P, :], in_=cache[pending[0]][:])
-            pending = ready
+        s_banks = (6, 4, 5, 0, 1)
+        a_banks = (7, 2, 3)
+        chunks = [(e, c) for c in range(4, 8) for e in (1, 0)]
+        chunks_before = {2: 2, 3: 4, 4: 2}
+        turn = 0
+        last = len(units) - 1
+        plus = {}
+        for u in range(1, len(units)):
+            for i in range(chunks_before.get(u, 0)):
+                hidden(*chunks.pop(0), s_banks[turn % len(s_banks)])
+                turn += 1
+                if not chunks:
+                    quant_h(spans[2], 0, 2)
+            z_bank, b_bank = s_banks[turn % len(s_banks)], s_banks[(turn + 0) % len(s_banks)]
+            turn += 1
+            gate = gate_of(units[u], z_bank)
+            a_bank = a_banks[u % len(a_banks)]
+            if u < last:
+                difference(units[u], a_bank)
+                plus[u] = gated(a_bank, gate, "plus")
+            else:
+                rest = sigmoid(z_bank, -1.0)
+                spare = a_banks[(u + 1) % len(a_banks)]
+                first_expert(units[u], a_bank)
+                second_expert(units[u], spare)
+                plus[u], minus = gated(a_bank, gate, "plus"), gated(spare, rest, "minus")
             if u == 1:
-                quant_h(spans[2], 0, 2)
-        scatter(*pending)
-        nc.sync.dma_start(out=out[pending[0] * P : (pending[0] + 1) * P, :], in_=cache[pending[0]][:])
+                for nt, weighted in opening:
+                    scatter(nt, spans[0][0], spans[0][1], weighted[:])
+            else:
+                place(units[u - 1], plus[u - 1], minus_e2(units[u - 1], b_bank))
+        place(units[last], plus[last], minus)

@@ -23,7 +23,17 @@ QUADS = 4
 LIST_ROWS = 16
 H_CHUNK = 128
 BANK = 512
-SPANS = ((0, 256), (256, 512), (512, S))
+SPAN = 256
+SPANS = S // SPAN
+GATES = 4
+HELD = 3
+WEIGHTED = 3
+SPLIT01 = 36
+SPLIT10 = 70
+AHEAD = {1: 1, 4: 2, 5: 3}
+BEFORE = 2
+RING = (7, 5, 2, 3, 6, 0, 1, 4)
+W4_ON_SCALAR = True
 
 
 def tile_list_candidate_expert_blend_kernel(
@@ -41,32 +51,32 @@ def tile_list_candidate_expert_blend_kernel(
         tab_s = keep.tile([P, T // 4], I32, name="tab_s", align_bytes=64)
         v_w = [keep.tile([P, S], U32, name="v_w%d" % a, align_bytes=64) for a in range(PASSES)]
         v_s = keep.tile([P, S], U8, name="v_s", align_bytes=64)
-        wg_w = keep.tile([P, PASSES, N], I32, name="wg_w", align_bytes=64)
+        wg_w = [keep.tile([P, PASSES, N // 2], I32, name="wg_w%d" % u, align_bytes=64) for u in range(2)]
         w_s = keep.tile([P, 2, N // 4], I32, name="w_s", align_bytes=64)
         w3_w = keep.tile([P, 2 * N // 4], I32, name="w3_w", align_bytes=64)
-        gain = keep.tile([P, len(SPANS), BANK], F32, name="gain", align_bytes=64)
+        gain = keep.tile([P, S], F32, name="gain", align_bytes=64)
         pieces = [(e, a) for e in range(2) for a in range(PASSES)]
         w1_raw = {ea: keep.tile([P, PACK, R], F32, name="w1_raw%d%d" % ea, align_bytes=64) for ea in pieces}
         w1_bf = {ea: keep.tile([P, PACK, P, PACK], BF16, name="w1_bf%d%d" % ea, align_bytes=64) for ea in pieces}
         w1_c = {ea: keep.tile([P, R], U32, name="w1_c%d%d" % ea, align_bytes=64) for ea in pieces}
         w1_s = {ea: keep.tile([P, R], U8, name="w1_s%d%d" % ea, align_bytes=64) for ea in pieces}
         w4_raw = [keep.tile([P, PACK, N // 2], F32, name="w4_raw%d" % u, align_bytes=64) for u in range(2)]
-        w4_bf = [keep.tile([P, N // 2, PACK], BF16, name="w4_bf%d" % u, align_bytes=64) for u in range(2)]
+        w4_bf = keep.tile([P, N, PACK], BF16, name="w4_bf", align_bytes=64)
         w4_c = keep.tile([P, N], U32, name="w4_c", align_bytes=64)
         w4_s = keep.tile([P, N], U8, name="w4_s", align_bytes=64)
-        spans = SPANS
-        h_bf = {sp: keep.tile([P, 2, sp[1] - sp[0], PACK], BF16, name="h_bf%d" % sp[0], align_bytes=64) for sp in spans}
-        h_c = {sp: keep.tile([P, 2, sp[1] - sp[0]], U32, name="h_c%d" % sp[0], align_bytes=64) for sp in spans}
-        h_s = {sp: keep.tile([P, 2, sp[1] - sp[0]], U8, name="h_s%d" % sp[0], align_bytes=64) for sp in spans}
+        h_bf = {s: keep.tile([P, 2, SPAN, PACK], BF16, name="h_bf%d" % s, align_bytes=64) for s in range(2, SPANS)}
+        h_late = [keep.tile([P, SPAN, PACK], BF16, name="h_late%d" % s, align_bytes=64) for s in range(2)]
+        h_c = {s: keep.tile([P, 2, SPAN], U32, name="h_c%d" % s, align_bytes=64) for s in range(1, SPANS)}
+        h_s = [keep.tile([P, 2, SPAN], U8, name="h_s%d" % s, align_bytes=64) for s in range(SPANS)]
         banks = [psum.tile([P, 512], F32, name="bank%d" % b) for b in range(8)]
-        cache = [keep.tile([P, T2], F32, name="cache%d" % nt, align_bytes=64) for nt in range(N // P)]
+        cache = [keep.tile([P, T2], F32, name="cache%d" % nt, align_bytes=64) for nt in range(N // P - 1)]
         warm = keep.tile([P, 2], F32, name="warm", align_bytes=64)
 
-        nc.gpsimd.memset(tab_s[:], 0)
-        nc.gpsimd.memset(w_s[:], 0)
-        for nt in range(N // P):
-            nc.gpsimd.memset(cache[nt][:], 0.0)
+        nc.vector.memset(tab_s[:], 0)
         nc.vector.memset(warm[:, 0:1], 0.0)
+        nc.vector.memset(w_s[:], 0)
+        for nt in range(N // P - 1):
+            nc.vector.memset(cache[nt][:], 0.0)
         nc.scalar.activation(warm[:, 1:2], warm[:, 0:1], ACT.Sigmoid)
 
         def load_words(dst, src):
@@ -78,17 +88,14 @@ def tile_list_candidate_expert_blend_kernel(
 
         def load_wg(u):
             cols = slice(u * (N // 2), (u + 1) * (N // 2))
-            nc.sync.dma_start(out=wg_w[:, :, cols], in_=wg_words[:, :, cols, :].rearrange("a p e i -> p a (e i)").bitcast(I32))
+            nc.sync.dma_start(out=wg_w[u][:], in_=wg_words[:, :, cols, :].rearrange("a p e i -> p a (e i)").bitcast(I32))
 
         def load_w4(u):
             cols = w4[:, u * (N // 2) : (u + 1) * (N // 2)]
             nc.sync.dma_start(out=w4_raw[u][:], in_=cols.rearrange("(p j) c -> p j c", j=PACK))
 
-        def load_gain(i):
-            j0, j1 = spans[i]
-            copies = [P, BANK // (j1 - j0), j1 - j0]
-            dst = gain[:, i, :].rearrange("p (r j) -> p r j", j=j1 - j0)
-            nc.sync.dma_start(out=dst, in_=wgo[:, j0:j1].unsqueeze(1).to_broadcast(copies))
+        def load_gain(j0, j1):
+            nc.sync.dma_start(out=gain[:, j0:j1], in_=wgo[:, j0:j1])
 
         load_words(tab_w[0][:], tab_words[0])
         nc.sync.dma_start(idx[:], offs)
@@ -97,22 +104,21 @@ def tile_list_candidate_expert_blend_kernel(
         load_w1(0, 0)
         load_words(tab_w[1][:], tab_words[1])
         load_w1(0, 1)
+        nc.sync.dma_start(idx2[:], offs2)
         for q in range(QUADS):
-            nc.sync.dma_start(out=w_s[32 * q : 32 * q + 8, 0, :], in_=wg_scales[:, 4 * q : 4 * q + 4, :].bitcast(I32))
-        load_wg(0)
+            nc.gpsimd.dma_start(out=w_s[32 * q : 32 * q + 8, 0, :], in_=wg_scales[:, 4 * q : 4 * q + 4, :].bitcast(I32))
         load_w1(1, 0)
+        for q in range(QUADS):
+            nc.gpsimd.dma_start(out=w_s[32 * q : 32 * q + 4, 1, :], in_=w3_scales[0, 4 * q : 4 * q + 4, :].bitcast(I32))
         load_w1(1, 1, 0, R // 2)
         load_w1(1, 1, R // 2, R)
+        load_wg(0)
         load_w4(0)
         load_w4(1)
-        load_wg(1)
         nc.sync.dma_start(out=w3_w[:], in_=w3_words[0].bitcast(I32))
-        for q in range(QUADS):
-            nc.sync.dma_start(out=w_s[32 * q : 32 * q + 4, 1, :], in_=w3_scales[0, 4 * q : 4 * q + 4, :].bitcast(I32))
-        load_gain(0)
-        nc.sync.dma_start(idx2[:], offs2)
-        load_gain(1)
-        load_gain(2)
+        load_gain(0, SPAN)
+        load_wg(1)
+        load_gain(SPAN, S)
 
         def entries(lst, j0, j1):
             return lst[:, j0 // LIST_ROWS : j1 // LIST_ROWS]
@@ -135,53 +141,73 @@ def tile_list_candidate_expert_blend_kernel(
                 in_=w1_bf[e, a][:, t0:t1].rearrange("p t m j -> p (t m j)"),
             )
 
+        def cast_w4(u, on_scalar):
+            dst = w4_bf[:, u * (N // 2) : (u + 1) * (N // 2), :].rearrange("p (c i) j -> p c j i", i=4)
+            src = w4_raw[u][:].rearrange("p j (c i) -> p c j i", i=4)
+            if on_scalar:
+                nc.scalar.activation(dst, src, ACT.Copy, scale=-1.0)
+            else:
+                nc.vector.tensor_scalar_mul(dst, src, -1.0)
+
         def quant_w4(u):
-            nc.vector.tensor_scalar_mul(
-                w4_bf[u][:].rearrange("p (c i) j -> p c j i", i=4), w4_raw[u][:].rearrange("p j (c i) -> p c j i", i=4), -1.0
-            )
             cols = slice(u * (N // 2), (u + 1) * (N // 2))
             nc.vector.quantize_mx(
-                out=w4_c[:, cols].bitcast(FP8X4), scales=w4_s[:, cols], in_=w4_bf[u][:].rearrange("p c j -> p (c j)")
+                out=w4_c[:, cols].bitcast(FP8X4), scales=w4_s[:, cols], in_=w4_bf[:, cols, :].rearrange("p c j -> p (c j)")
             )
 
-        def hidden(e, chunk, b):
-            j0 = chunk * H_CHUNK
-            sp = [x for x in spans if x[0] <= j0 < x[1]][0]
-            cols = slice(j0, j0 + H_CHUNK)
+        def hidden_pass(e, chunk, b, a):
+            cols = slice(chunk * H_CHUNK, (chunk + 1) * H_CHUNK)
             bank = banks[b][:].rearrange("p (t n) -> p t n", t=PACK)
             for t in range(PACK):
-                for a in range(PASSES):
-                    nc.tensor.matmul_mx(
-                        out=bank[:, t, :],
-                        lhsT=w1_c[e, a][:, t * P : (t + 1) * P].bitcast(FP8X4),
-                        lhsT_scale=w1_s[e, a][:, t * P : (t + 1) * P],
-                        rhs=v_w[a][:, cols].bitcast(FP8X4),
-                        rhs_scale=v_s[4 * a : P, cols],
-                        start=(a == 0),
-                        stop=(a == PASSES - 1),
-                    )
-            dst = h_bf[sp][:, e, j0 - sp[0] : j0 - sp[0] + H_CHUNK, :]
-            nc.scalar.activation(dst, bank.rearrange("p t n -> p n t"), ACT.Relu)
+                nc.tensor.matmul_mx(
+                    out=bank[:, t, :],
+                    lhsT=w1_c[e, a][:, t * P : (t + 1) * P].bitcast(FP8X4),
+                    lhsT_scale=w1_s[e, a][:, t * P : (t + 1) * P],
+                    rhs=v_w[a][:, cols].bitcast(FP8X4),
+                    rhs_scale=v_s[4 * a : P, cols],
+                    start=(a == 0 and t == 0),
+                    stop=(a == PASSES - 1 and t == PACK - 1),
+                )
 
-        def quant_h(sp, e0, e1):
+        def rounded(e, s):
+            if s >= 2:
+                return h_bf[s][:, e]
+            return h_late[s][:] if e else h_early[:, s]
+
+        def relu(e, chunk, b):
+            s, i = divmod(chunk, SPAN // H_CHUNK)
+            dst = rounded(e, s)[:, i * H_CHUNK : (i + 1) * H_CHUNK, :]
+            nc.scalar.activation(dst, banks[b][:].rearrange("p (t n) -> p n t", t=PACK), ACT.Relu)
+
+        def hidden(e, chunk, b):
+            for a in range(PASSES):
+                hidden_pass(e, chunk, b, a)
+            relu(e, chunk, b)
+
+        def quant_h(s):
             nc.vector.quantize_mx(
-                out=h_c[sp][:, e0:e1, :].rearrange("p e n -> p (e n)").bitcast(FP8X4),
-                scales=h_s[sp][:, e0:e1, :].rearrange("p e n -> p (e n)"),
-                in_=h_bf[sp][:, e0:e1].rearrange("p e n t -> p (e n t)"),
+                out=h_c[s][:].rearrange("p e n -> p (e n)").bitcast(FP8X4),
+                scales=h_s[s][:].rearrange("p e n -> p (e n)"),
+                in_=h_bf[s][:].rearrange("p e n t -> p (e n t)"),
             )
 
-        def expert1(dst, nt, sp, c0, c1, stop):
+        def quant_expert(e, s):
+            nc.vector.quantize_mx(
+                out=h_c[s][:, e, :].bitcast(FP8X4), scales=h_s[s][:, e, :], in_=rounded(e, s).rearrange("p n t -> p (n t)")
+            )
+
+        def expert1(dst, nt, sp, c0, c1, start, stop):
             nc.tensor.matmul_mx(
                 out=dst,
                 lhsT=w3_w[:].bitcast(U8)[:, 2 * nt * P : 2 * (nt + 1) * P].bitcast(FP4X4),
                 lhsT_scale=w_s[:, 1, :].bitcast(U8)[:, nt * P : (nt + 1) * P],
                 rhs=h_c[sp][:, 0, c0:c1].bitcast(FP8X4),
                 rhs_scale=h_s[sp][:, 0, c0:c1],
-                start=True,
+                start=start,
                 stop=stop,
             )
 
-        def expert2_negated(dst, nt, sp, c0, c1, start):
+        def expert2_negated(dst, nt, sp, c0, c1, start, stop):
             nc.tensor.matmul_mx(
                 out=dst,
                 lhsT=w4_c[:, nt * P : (nt + 1) * P].bitcast(FP8X4),
@@ -189,149 +215,185 @@ def tile_list_candidate_expert_blend_kernel(
                 rhs=h_c[sp][:, 1, c0:c1].bitcast(FP8X4),
                 rhs_scale=h_s[sp][:, 1, c0:c1],
                 start=start,
-                stop=True,
+                stop=stop,
             )
 
         def gate_logits(z, nt, sp):
             rows = slice(nt * P, (nt + 1) * P)
+            own = slice(nt % 2 * P, (nt % 2 + 1) * P)
             for a in range(PASSES):
                 nc.tensor.matmul_mx(
                     out=z,
-                    lhsT=wg_w[:, a, rows].bitcast(FP8X4),
+                    lhsT=wg_w[nt // 2][:, a, own].bitcast(FP8X4),
                     lhsT_scale=w_s[4 * a : P, 0, :].bitcast(U8)[:, rows],
-                    rhs=v_w[a][:, sp[0] : sp[1]].bitcast(FP8X4),
-                    rhs_scale=v_s[4 * a : P, sp[0] : sp[1]],
+                    rhs=v_w[a][:, sp * SPAN : (sp + 1) * SPAN].bitcast(FP8X4),
+                    rhs_scale=v_s[4 * a : P, sp * SPAN : (sp + 1) * SPAN],
                     start=(a == 0),
                     stop=(a == PASSES - 1),
                 )
 
         def parts(unit):
-            nts, sp = unit
-            width = sp[1] - sp[0]
-            return [(nt, i * width, (i + 1) * width) for i, nt in enumerate(nts)]
+            return [(nt, s, i * SPAN, (i + 1) * SPAN) for i, (nt, s) in enumerate(unit)]
 
         def sigmoid(b, sign):
-            gate = ring.tile([P, BANK], F32, name="gate", bufs=5)
+            gate = ring.tile([P, BANK], F32, name="gate", bufs=GATES)
             nc.scalar.activation(gate[:], banks[b][:], ACT.Sigmoid, scale=sign)
             return gate
 
         def gate_of(unit, b):
-            for nt, c0, c1 in parts(unit):
-                gate_logits(banks[b][:, c0:c1], nt, unit[1])
+            for nt, s, c0, c1 in parts(unit):
+                gate_logits(banks[b][:, c0:c1], nt, s)
             return sigmoid(b, 1.0)
 
         def difference(unit, b):
-            sp = unit[1]
-            step = BANK if sp[1] - sp[0] == BANK else 128
-            for nt, c0, c1 in parts(unit):
-                for d in range(0, c1 - c0, step):
-                    expert1(banks[b][:, c0 + d : c0 + d + step], nt, sp, d, d + step, False)
-                    expert2_negated(banks[b][:, c0 + d : c0 + d + step], nt, sp, d, d + step, False)
-
-        def gated(b, gate, name, c0=0, c1=BANK):
-            product = ring.tile([P, c1 - c0], F32, name=name, bufs=5)
-            nc.vector.tensor_tensor(product[:], banks[b][:, c0:c1], gate[:, c0:c1], ALU.mult)
-            return product
+            for nt, s, c0, c1 in parts(unit):
+                for d in range(0, SPAN, H_CHUNK):
+                    expert1(banks[b][:, c0 + d : c0 + d + H_CHUNK], nt, s, d, d + H_CHUNK, c0 + d == 0, False)
+            for nt, s, c0, c1 in parts(unit):
+                expert2_negated(banks[b][:, c0:c1], nt, s, 0, SPAN, False, c1 == BANK)
 
         def first_expert(unit, b):
-            for nt, c0, c1 in parts(unit):
-                expert1(banks[b][:, c0:c1], nt, unit[1], 0, c1 - c0, True)
+            for nt, s, c0, c1 in parts(unit):
+                expert1(banks[b][:, c0:c1], nt, s, 0, SPAN, True, True)
 
         def second_expert(unit, b):
-            for nt, c0, c1 in parts(unit):
-                expert2_negated(banks[b][:, c0:c1], nt, unit[1], 0, c1 - c0, True)
+            for nt, s, c0, c1 in parts(unit):
+                expert2_negated(banks[b][:, c0:c1], nt, s, 0, SPAN, True, True)
 
-        def minus_e2(unit, b):
-            second_expert(unit, b)
-            minus = ring.tile([P, BANK], F32, name="minus", bufs=5)
-            nc.scalar.copy(minus[:], banks[b][:])
-            return minus
+        def copy_out(b, name):
+            held = ring.tile([P, BANK], F32, name=name, bufs=HELD)
+            nc.scalar.copy(held[:], banks[b][:])
+            return held
 
-        def weigh(plus, minus, factors, engine):
-            width = factors.shape[1]
-            y = ring.tile([P, width], F32, name="y", bufs=3)
-            engine.tensor_tensor(y[:], plus[:], minus[:], ALU.subtract)
-            weighted = ring.tile([P, width], F32, name="weighted", bufs=5)
-            engine.tensor_tensor(weighted[:], y[:], factors, ALU.mult)
+        def combine(engine, name, x, y, op):
+            result = ring.tile([P, BANK], F32, name=name, bufs=1 if name == "y" else HELD)
+            engine.tensor_tensor(result[:], x, y, op)
+            return result
+
+        def weigh(engine, unit, y, weighted):
+            s0, s1 = unit[0][1], unit[1][1]
+            if s0 == s1:
+                factors = gain[:, s0 * SPAN : (s0 + 1) * SPAN].unsqueeze(1).to_broadcast([P, 2, SPAN])
+            else:
+                factors = gain[:, s0 * SPAN : (s1 + 1) * SPAN].rearrange("p (r j) -> p r j", r=2)
+            engine.tensor_tensor(
+                weighted[:].rearrange("p (r j) -> p r j", r=2), y[:].rearrange("p (r j) -> p r j", r=2), factors, ALU.mult
+            )
             return weighted
 
-        def place(unit, plus, minus):
-            sp = unit[1]
-            weighted = weigh(plus, minus, gain[:, spans.index(sp), :], nc.gpsimd)
-            for nt, c0, c1 in parts(unit):
-                scatter(nt, sp[0], sp[1], weighted[:, c0:c1])
-                if sp[1] == S:
-                    nc.sync.dma_start(out=out[nt * P : (nt + 1) * P, :], in_=cache[nt][:])
+        def store(nt):
+            nc.sync.dma_start(out=out[nt * P : (nt + 1) * P, :], in_=cache[nt][:])
 
-        def scatter(nt, j0, j1, weighted):
-            nc.vector.tensor_copy(out=cache[nt][:].indirect(entries(idx2, j0, j1)), in_=weighted)
+        def place(unit, weighted):
+            if unit[0][0] == unit[1][0]:
+                nt, s = unit[0]
+                nc.vector.tensor_copy(out=cache[nt][:].indirect(entries(idx2, s * SPAN, (s + 2) * SPAN)), in_=weighted[:])
+                store(nt)
+                return
+            for nt, s, c0, c1 in parts(unit):
+                nc.vector.tensor_copy(out=cache[nt][:].indirect(entries(idx2, s * SPAN, (s + 1) * SPAN)), in_=weighted[:, c0:c1])
+                if s == SPANS - 1:
+                    store(nt)
 
         half = S // 2
-        split = 84
         gather_words(0, 0, half)
-        gather_scales(0, half)
-        cast_w1(0, 0, 0, P, nc.scalar.copy)
-        quant_w1(0, 0)
-        gather_words(1, 0, half)
         gather_words(0, half, S)
+        cache.append(keep.tile([P, T2], F32, name="cache3", tag="tab_w0", align_bytes=64))
+        nc.gpsimd.memset(cache[3][:], 0.0)
+        gather_scales(0, half)
         gather_scales(half, S)
+        cast_w1(0, 0, 0, P, nc.scalar.copy)
+        gather_words(1, 0, half)
+        quant_w1(0, 0)
         gather_words(1, half, S)
-        cast_w1(0, 1, 0, split, nc.vector.tensor_copy)
-        cast_w1(0, 1, split, P, nc.scalar.copy)
+        cast_w1(0, 1, 0, SPLIT01, nc.vector.tensor_copy)
+        cast_w1(0, 1, SPLIT01, P, nc.scalar.copy)
         quant_w1(0, 1)
-        cast_w1(1, 0, 0, P, nc.vector.tensor_copy)
-        quant_w1(1, 0)
+        cast_w1(1, 0, 0, SPLIT10, nc.vector.tensor_copy)
+        cast_w1(1, 0, SPLIT10, P, nc.scalar.copy)
         cast_w1(1, 1, 0, P // 2, nc.vector.tensor_copy)
+        quant_w1(1, 0)
         cast_w1(1, 1, P // 2, P, nc.vector.tensor_copy)
-        quant_w1(1, 1)
-        units = [(nts, sp) for sp in spans[:2] for nts in ((0, 1), (2, 3))] + [((nt,), spans[2]) for nt in range(N // P)]
-        for chunk in range(4):
+        quant_w1(1, 1, 0, 2)
+        quant_w1(1, 1, 2, 4)
+        units = [((nt, s), (nt + 1, s)) for s in range(2) for nt in (0, 2)]
+        units = units + [((0, s), (1, s)) for s in (2, 3)] + [((nt, 2), (nt, 3)) for nt in (2, 3)]
+        h_early = keep.tile([P, 2, SPAN, PACK], BF16, name="h_early", tag="w1_raw10", align_bytes=64)
+        h_c[0] = keep.tile([P, 2, SPAN], U32, name="h_c0", tag="w1_raw11", align_bytes=64)
+        for chunk in range(2):
             hidden(0, chunk, chunk)
-        gate = gate_of(units[0], 6)
-        rest = sigmoid(6, -1.0)
-        hidden(1, 0, 4)
-        hidden(1, 1, 5)
-        quant_h(spans[0], 0, 2)
+        for chunk in range(2):
+            hidden_pass(1, chunk, 2 + chunk, 0)
+        hidden(0, 2, 5)
+        hidden(0, 3, 6)
+        quant_expert(0, 0)
+        cast_w4(0, False)
+        gate = gate_of(units[0], 4)
+        rest = sigmoid(4, -1.0)
+        for chunk in range(2):
+            hidden_pass(1, chunk, 2 + chunk, 1)
+            relu(1, chunk, 2 + chunk)
         quant_w4(0)
+        quant_expert(0, 1)
+        quant_expert(1, 0)
+        first_expert(units[0], 0)
+        second_expert(units[0], 1)
+        plus = combine(nc.vector, "gated", banks[0][:], gate[:], ALU.mult)
+        cast_w4(1, W4_ON_SCALAR)
         quant_w4(1)
-        first_expert(units[0], 4)
-        second_expert(units[0], 5)
-        opening = []
-        for (nt, c0, c1), engine in zip(parts(units[0]), (nc.gpsimd, nc.vector)):
-            opening.append((nt, gated(4, gate, "plus", c0, c1), gated(5, rest, "minus", c0, c1), gain[:, 0, c0:c1], engine))
-        opening = [(nt, weigh(plus, minus, factors, engine)) for nt, plus, minus, factors, engine in opening]
-        hidden(1, 2, 0)
-        hidden(1, 3, 1)
-        quant_h(spans[1], 0, 2)
-        s_banks = (6, 4, 5, 0, 1)
-        a_banks = (7, 2, 3)
-        chunks = [(e, c) for c in range(4, 8) for e in (1, 0)]
-        chunks_before = {2: 2, 3: 4, 4: 2}
-        turn = 0
+        minus = combine(nc.vector, "minus", banks[1][:], rest[:], ALU.mult)
+        for chunk in range(2, 4):
+            hidden(1, chunk, chunk)
+        quant_expert(1, 1)
+        y = combine(nc.vector, "y", plus[:], minus[:], ALU.subtract)
+        turn = [0]
+
+        def take():
+            turn[0] += 1
+            return RING[(turn[0] - 1) % len(RING)]
+
+        def gated_on_vector(u):
+            gate = gate_of(units[u], take())
+            b = take()
+            difference(units[u], b)
+            gated[u] = combine(nc.vector, "gated", banks[b][:], gate[:], ALU.mult)
+
         last = len(units) - 1
-        plus = {}
+        gated = {}
         for u in range(1, len(units)):
-            for i in range(chunks_before.get(u, 0)):
-                hidden(*chunks.pop(0), s_banks[turn % len(s_banks)])
-                turn += 1
-                if not chunks:
-                    quant_h(spans[2], 0, 2)
-            z_bank, b_bank = s_banks[turn % len(s_banks)], s_banks[(turn + 0) % len(s_banks)]
-            turn += 1
-            gate = gate_of(units[u], z_bank)
-            a_bank = a_banks[u % len(a_banks)]
-            if u < last:
-                difference(units[u], a_bank)
-                plus[u] = gated(a_bank, gate, "plus")
-            else:
-                rest = sigmoid(z_bank, -1.0)
-                spare = a_banks[(u + 1) % len(a_banks)]
-                first_expert(units[u], a_bank)
-                second_expert(units[u], spare)
-                plus[u], minus = gated(a_bank, gate, "plus"), gated(spare, rest, "minus")
+            if AHEAD.get(u) == u:
+                gated_on_vector(u)
+            elif u not in AHEAD:
+                gate = gate_of(units[u], take())
+                b = take()
+                if u == last:
+                    first_expert(units[u], b)
+                else:
+                    difference(units[u], b)
+                diff = copy_out(b, "diff")
             if u == 1:
-                for nt, weighted in opening:
-                    scatter(nt, spans[0][0], spans[0][1], weighted[:])
-            else:
-                place(units[u - 1], plus[u - 1], minus_e2(units[u - 1], b_bank))
-        place(units[last], plus[last], minus)
+                ready = weigh(nc.vector, units[0], y, keep.tile([P, BANK], F32, name="first", tag="h_late1", align_bytes=64))
+            chunks = [(e, c) for c in (2 * u + 2, 2 * u + 3) for e in range(2)] if u + 1 < SPANS else []
+            for e, c in chunks[:BEFORE]:
+                hidden(e, c, take())
+            b = take()
+            second_expert(units[u], b)
+            minus = copy_out(b, "minus")
+            for e, c in chunks[BEFORE:]:
+                hidden(e, c, take())
+            if chunks:
+                quant_h(u + 1)
+            for later in range(u + 1, len(units)):
+                if AHEAD.get(later) == u:
+                    gated_on_vector(later)
+            place(units[u - 1], ready)
+            if u == last:
+                diff = combine(nc.gpsimd, "y", diff[:], minus[:], ALU.add)
+            if u not in AHEAD:
+                gated[u] = combine(nc.gpsimd, "plus", diff[:], gate[:], ALU.mult)
+            y = combine(nc.gpsimd, "y", gated[u][:], minus[:], ALU.subtract)
+            if u < last:
+                ready = weigh(nc.gpsimd, units[u], y, ring.tile([P, BANK], F32, name="weighted", bufs=WEIGHTED))
+        nt, s = units[last][0]
+        nc.vector.tensor_tensor(cache[nt][:].indirect(entries(idx2, s * SPAN, S)), y[:], gain[:, s * SPAN : S], ALU.mult)
+        store(nt)

@@ -66,17 +66,17 @@ def tile_list_candidate_expert_blend_kernel(
         w4_s = keep.tile([P, N], U8, name="w4_s", align_bytes=64)
         h_bf = {s: keep.tile([P, 2, SPAN, PACK], BF16, name="h_bf%d" % s, align_bytes=64) for s in range(2, SPANS)}
         h_late = [keep.tile([P, SPAN, PACK], BF16, name="h_late%d" % s, align_bytes=64) for s in range(2)]
-        h_c = {s: keep.tile([P, 2, SPAN], U32, name="h_c%d" % s, align_bytes=64) for s in range(1, SPANS)}
+        h_c = {s: keep.tile([P, 2, SPAN], U32, name="h_c%d" % s, align_bytes=64) for s in range(2, SPANS)}
         h_s = [keep.tile([P, 2, SPAN], U8, name="h_s%d" % s, align_bytes=64) for s in range(SPANS)]
         banks = [psum.tile([P, 512], F32, name="bank%d" % b) for b in range(8)]
-        cache = [keep.tile([P, T2], F32, name="cache%d" % nt, align_bytes=64) for nt in range(N // P - 1)]
+        cache = [keep.tile([P, T2], F32, name="cache%d" % nt, align_bytes=64) for nt in range(N // P)]
         warm = keep.tile([P, 2], F32, name="warm", align_bytes=64)
 
-        nc.vector.memset(tab_s[:], 0)
+        nc.gpsimd.memset(tab_s[:], 0)
+        nc.gpsimd.memset(w_s[:], 0)
+        for nt in range(N // P):
+            nc.gpsimd.memset(cache[nt][:], 0.0)
         nc.vector.memset(warm[:, 0:1], 0.0)
-        nc.vector.memset(w_s[:], 0)
-        for nt in range(N // P - 1):
-            nc.vector.memset(cache[nt][:], 0.0)
         nc.scalar.activation(warm[:, 1:2], warm[:, 0:1], ACT.Sigmoid)
 
         def load_words(dst, src):
@@ -97,6 +97,14 @@ def tile_list_candidate_expert_blend_kernel(
         def load_gain(j0, j1):
             nc.sync.dma_start(out=gain[:, j0:j1], in_=wgo[:, j0:j1])
 
+        def load_wg_scales():
+            for q in range(QUADS):
+                nc.sync.dma_start(out=w_s[32 * q : 32 * q + 8, 0, :], in_=wg_scales[:, 4 * q : 4 * q + 4, :].bitcast(I32))
+
+        def load_w3_scales():
+            for q in range(QUADS):
+                nc.sync.dma_start(out=w_s[32 * q : 32 * q + 4, 1, :], in_=w3_scales[0, 4 * q : 4 * q + 4, :].bitcast(I32))
+
         load_words(tab_w[0][:], tab_words[0])
         nc.sync.dma_start(idx[:], offs)
         for q in range(QUADS):
@@ -105,17 +113,15 @@ def tile_list_candidate_expert_blend_kernel(
         load_words(tab_w[1][:], tab_words[1])
         load_w1(0, 1)
         nc.sync.dma_start(idx2[:], offs2)
-        for q in range(QUADS):
-            nc.gpsimd.dma_start(out=w_s[32 * q : 32 * q + 8, 0, :], in_=wg_scales[:, 4 * q : 4 * q + 4, :].bitcast(I32))
+        load_wg_scales()
         load_w1(1, 0)
-        for q in range(QUADS):
-            nc.gpsimd.dma_start(out=w_s[32 * q : 32 * q + 4, 1, :], in_=w3_scales[0, 4 * q : 4 * q + 4, :].bitcast(I32))
+        load_w3_scales()
         load_w1(1, 1, 0, R // 2)
         load_w1(1, 1, R // 2, R)
         load_wg(0)
         load_w4(0)
-        load_w4(1)
         nc.sync.dma_start(out=w3_w[:], in_=w3_words[0].bitcast(I32))
+        load_w4(1)
         load_gain(0, SPAN)
         load_wg(1)
         load_gain(SPAN, S)
@@ -298,8 +304,6 @@ def tile_list_candidate_expert_blend_kernel(
         half = S // 2
         gather_words(0, 0, half)
         gather_words(0, half, S)
-        cache.append(keep.tile([P, T2], F32, name="cache3", tag="tab_w0", align_bytes=64))
-        nc.gpsimd.memset(cache[3][:], 0.0)
         gather_scales(0, half)
         gather_scales(half, S)
         cast_w1(0, 0, 0, P, nc.scalar.copy)
@@ -319,7 +323,8 @@ def tile_list_candidate_expert_blend_kernel(
         units = [((nt, s), (nt + 1, s)) for s in range(2) for nt in (0, 2)]
         units = units + [((0, s), (1, s)) for s in (2, 3)] + [((nt, 2), (nt, 3)) for nt in (2, 3)]
         h_early = keep.tile([P, 2, SPAN, PACK], BF16, name="h_early", tag="w1_raw10", align_bytes=64)
-        h_c[0] = keep.tile([P, 2, SPAN], U32, name="h_c0", tag="w1_raw11", align_bytes=64)
+        h_c_early = keep.tile([P, 2, 2, SPAN], U32, name="h_c_early", tag="w1_raw11", align_bytes=64)
+        h_c[0], h_c[1] = h_c_early[:, 0], h_c_early[:, 1]
         for chunk in range(2):
             hidden(0, chunk, chunk)
         for chunk in range(2):

@@ -30,7 +30,7 @@ HELD = 3
 WEIGHTED = 3
 SPLIT01 = 36
 SPLIT10 = 70
-AHEAD = {1: 1, 4: 2, 5: 3}
+AHEAD = {1: 1, 2: 1, 3: 2, 4: 2, 5: 3, 6: 4}
 BEFORE = 2
 RING = (7, 5, 2, 3, 6, 0, 1, 4)
 W4_ON_SCALAR = True

@@ -1,6 +1,7 @@
 from contextlib import ExitStack
 
 import concourse.mybir as mybir
+from concourse.masks import make_identity
 
 K, H, R, N, T, S, T2, P = 1024, 1024, 512, 512, 2048, 1024, 2048, 128
 FLOPS = 2 * S * (K * H + K * N + 2 * R * N)
@@ -30,10 +31,11 @@ HELD = 3
 WEIGHTED = 3
 SPLIT01 = 36
 SPLIT10 = 70
-AHEAD = {1: 1, 2: 1, 3: 2, 4: 2, 5: 3, 6: 4}
+AHEAD = {1: 1, 2: 1, 3: 1, 4: 2, 5: 4, 6: 5, 7: 6}
 BEFORE = 2
 RING = (7, 5, 2, 3, 6, 0, 1, 4)
 W4_ON_SCALAR = True
+TURNED = 4
 
 
 def tile_list_candidate_expert_blend_kernel(
@@ -74,6 +76,8 @@ def tile_list_candidate_expert_blend_kernel(
 
         nc.gpsimd.memset(tab_s[:], 0)
         nc.gpsimd.memset(w_s[:], 0)
+        identity = keep.tile([P, P], F32, name="identity", align_bytes=64)
+        make_identity(nc, identity[:])
         for nt in range(N // P):
             nc.gpsimd.memset(cache[nt][:], 0.0)
         nc.vector.memset(warm[:, 0:1], 0.0)
@@ -266,13 +270,84 @@ def tile_list_candidate_expert_blend_kernel(
             for nt, s, c0, c1 in parts(unit):
                 expert2_negated(banks[b][:, c0:c1], nt, s, 0, SPAN, True, True)
 
+        def blocks(unit):
+            return [(nt, s, i * P, c0 + i * P) for nt, s, c0, c1 in parts(unit) for i in range(SPAN // P)]
+
+        def turned_gate(unit, b):
+            for nt, s, j, c in blocks(unit):
+                cols = slice(s * SPAN + j, s * SPAN + j + P)
+                for a in range(PASSES):
+                    nc.tensor.matmul_mx(
+                        out=banks[b][:, c : c + P],
+                        lhsT=v_w[a][:, cols].bitcast(FP8X4),
+                        lhsT_scale=v_s[4 * a : P, cols],
+                        rhs=wg_w[nt // 2][:, a, nt % 2 * P : (nt % 2 + 1) * P].bitcast(FP8X4),
+                        rhs_scale=w_s[4 * a : P, 0, :].bitcast(U8)[:, nt * P : (nt + 1) * P],
+                        start=(a == 0),
+                        stop=(a == PASSES - 1),
+                    )
+
+        def turned_expert1(dst, nt, s, j, stop):
+            nc.tensor.matmul_mx(
+                out=dst,
+                lhsT=h_c[s][:, 0, j : j + P].bitcast(FP8X4),
+                lhsT_scale=h_s[s][:, 0, j : j + P],
+                rhs=w3_w[:].bitcast(U8)[:, 2 * nt * P : 2 * (nt + 1) * P].bitcast(FP4X4),
+                rhs_scale=w_s[:, 1, :].bitcast(U8)[:, nt * P : (nt + 1) * P],
+                start=True,
+                stop=stop,
+            )
+
+        def turned_expert2(dst, nt, s, j, start):
+            nc.tensor.matmul_mx(
+                out=dst,
+                lhsT=h_c[s][:, 1, j : j + P].bitcast(FP8X4),
+                lhsT_scale=h_s[s][:, 1, j : j + P],
+                rhs=w4_c[:, nt * P : (nt + 1) * P].bitcast(FP8X4),
+                rhs_scale=w4_s[:, nt * P : (nt + 1) * P],
+                start=start,
+                stop=True,
+            )
+
+        def turned_terms(u):
+            unit, apart = units[u], u == len(units) - 1
+            b = take()
+            turned_gate(unit, b)
+            gate = sigmoid(b, 1.0)
+            if apart:
+                rest = sigmoid(b, -1.0)
+            b = take()
+            for nt, s, j, c in blocks(unit):
+                turned_expert1(banks[b][:, c : c + P], nt, s, j, apart)
+                if not apart:
+                    turned_expert2(banks[b][:, c : c + P], nt, s, j, False)
+            first = copy_out(b, "diff")
+            b = take()
+            for nt, s, j, c in blocks(unit):
+                turned_expert2(banks[b][:, c : c + P], nt, s, j, True)
+            second = ring.tile([P, BANK], F32, name="second", bufs=HELD)
+            nc.scalar.activation(second[:], banks[b][:], ACT.Copy, scale=-1.0)
+            terms[u] = [second, combine(nc.gpsimd, "plus", first[:], gate[:], ALU.mult)]
+            if apart:
+                rests[u] = rest
+
+        def turned_sum(u):
+            if u in rests:
+                terms[u] = [terms[u][1], combine(nc.gpsimd, "summed", terms[u][0][:], rests[u][:], ALU.mult)]
+            b = take()
+            for i, term in enumerate(terms[u]):
+                for c in range(0, BANK, P):
+                    opens, closes = i == 0 and c == 0, i == 1 and c == BANK - P
+                    nc.tensor.matmul(banks[b][:, c : c + P], term[:, c : c + P], identity[:], start=opens, stop=closes, is_transpose=True)
+            return copy_out(b, "summed" if u < len(units) - 1 else "diff")
+
         def copy_out(b, name):
-            held = ring.tile([P, BANK], F32, name=name, bufs=HELD)
+            held = ring.tile([P, BANK], F32, name=name, bufs=1 if name == "summed" else HELD)
             nc.scalar.copy(held[:], banks[b][:])
             return held
 
         def combine(engine, name, x, y, op):
-            result = ring.tile([P, BANK], F32, name=name, bufs=1 if name == "y" else HELD)
+            result = ring.tile([P, BANK], F32, name=name, bufs=1 if name in ("y", "summed") else HELD)
             engine.tensor_tensor(result[:], x, y, op)
             return result
 
@@ -364,39 +439,34 @@ def tile_list_candidate_expert_blend_kernel(
             gated[u] = combine(nc.vector, "gated", banks[b][:], gate[:], ALU.mult)
 
         last = len(units) - 1
-        gated = {}
+        gated, terms, rests = {}, {}, {}
         for u in range(1, len(units)):
             if AHEAD.get(u) == u:
                 gated_on_vector(u)
-            elif u not in AHEAD:
-                gate = gate_of(units[u], take())
-                b = take()
-                if u == last:
-                    first_expert(units[u], b)
-                else:
-                    difference(units[u], b)
-                diff = copy_out(b, "diff")
             if u == 1:
                 ready = weigh(nc.vector, units[0], y, keep.tile([P, BANK], F32, name="first", tag="h_late1", align_bytes=64))
             chunks = [(e, c) for c in (2 * u + 2, 2 * u + 3) for e in range(2)] if u + 1 < SPANS else []
             for e, c in chunks[:BEFORE]:
                 hidden(e, c, take())
-            b = take()
-            second_expert(units[u], b)
-            minus = copy_out(b, "minus")
+            if u < TURNED:
+                b = take()
+                second_expert(units[u], b)
+                minus = copy_out(b, "minus")
             for e, c in chunks[BEFORE:]:
                 hidden(e, c, take())
             if chunks:
                 quant_h(u + 1)
             for later in range(u + 1, len(units)):
                 if AHEAD.get(later) == u:
-                    gated_on_vector(later)
+                    if later < TURNED:
+                        gated_on_vector(later)
+                    else:
+                        turned_terms(later)
             place(units[u - 1], ready)
-            if u == last:
-                diff = combine(nc.gpsimd, "y", diff[:], minus[:], ALU.add)
-            if u not in AHEAD:
-                gated[u] = combine(nc.gpsimd, "plus", diff[:], gate[:], ALU.mult)
-            y = combine(nc.gpsimd, "y", gated[u][:], minus[:], ALU.subtract)
+            if u < TURNED:
+                y = combine(nc.gpsimd, "y", gated[u][:], minus[:], ALU.subtract)
+            else:
+                y = turned_sum(u)
             if u < last:
                 ready = weigh(nc.gpsimd, units[u], y, ring.tile([P, BANK], F32, name="weighted", bufs=WEIGHTED))
         nt, s = units[last][0]

@@ -31,11 +31,13 @@ HELD = 3
 WEIGHTED = 3
 SPLIT01 = 36
 SPLIT10 = 70
-AHEAD = {1: 1, 2: 1, 3: 1, 4: 2, 5: 4, 6: 5, 7: 6}
 BEFORE = 2
-RING = (7, 5, 2, 3, 6, 0, 1, 4)
+RING = (7, 2, 3, 4, 0, 1)
 W4_ON_SCALAR = True
-TURNED = 4
+TURNED = 3
+VB = (6, 5)
+EARLY = {2: (3,), 3: (4,), 4: (5,), 5: (6,), 6: (7,)}
+LATE = {1: (2,)}
 
 
 def tile_list_candidate_expert_blend_kernel(
@@ -434,17 +436,25 @@ def tile_list_candidate_expert_blend_kernel(
 
         def gated_on_vector(u):
             gate = gate_of(units[u], take())
-            b = take()
+            b = VB[u % len(VB)] if VB else take()
             difference(units[u], b)
             gated[u] = combine(nc.vector, "gated", banks[b][:], gate[:], ALU.mult)
+
+        def prepare(u):
+            if u < TURNED:
+                gated_on_vector(u)
+            else:
+                turned_terms(u)
 
         last = len(units) - 1
         gated, terms, rests = {}, {}, {}
         for u in range(1, len(units)):
-            if AHEAD.get(u) == u:
+            if u == 1:
                 gated_on_vector(u)
             if u == 1:
                 ready = weigh(nc.vector, units[0], y, keep.tile([P, BANK], F32, name="first", tag="h_late1", align_bytes=64))
+            for later in EARLY.get(u, ()):
+                prepare(later)
             chunks = [(e, c) for c in (2 * u + 2, 2 * u + 3) for e in range(2)] if u + 1 < SPANS else []
             for e, c in chunks[:BEFORE]:
                 hidden(e, c, take())
@@ -456,12 +466,8 @@ def tile_list_candidate_expert_blend_kernel(
                 hidden(e, c, take())
             if chunks:
                 quant_h(u + 1)
-            for later in range(u + 1, len(units)):
-                if AHEAD.get(later) == u:
-                    if later < TURNED:
-                        gated_on_vector(later)
-                    else:
-                        turned_terms(later)
+            for later in LATE.get(u, ()):
+                prepare(later)
             place(units[u - 1], ready)
             if u < TURNED:
                 y = combine(nc.gpsimd, "y", gated[u][:], minus[:], ALU.subtract)

@@ -26,18 +26,21 @@ H_CHUNK = 128
 BANK = 512
 SPAN = 256
 SPANS = S // SPAN
-GATES = 4
+SPLIT10 = 128
+SPLIT4 = 112
+HTAG = {(0, 0): "w1_bf10"}
+VRELU = 9
+SPLIT01 = 96
+GATES = 5
 HELD = 3
-WEIGHTED = 3
-SPLIT01 = 36
-SPLIT10 = 70
-BEFORE = 2
-RING = (7, 2, 3, 4, 0, 1)
-W4_ON_SCALAR = True
-TURNED = 3
-VB = (6, 5)
-EARLY = {2: (3,), 3: (4,), 4: (5,), 5: (6,), 6: (7,)}
-LATE = {1: (2,)}
+WEIGHTED = 6
+W4B_ON_SCALAR = True
+MODES = ("V", "A", "T", "T", "T", "T", "T", "X")
+ON_VECTOR = (1,)
+SLOTS = ("h_bf13", "h_bf11")
+STEPS = "b1 g1 p0 b2 g2 f1 b3 g3 f2 b4 g4 f3 b5 g5 f4 b6 g6 f5 b7 g7 f6 f7"
+TENANTS = (0, 1, 2, 3)
+RING = (0, 1, 2, 6, 3, 4, 5, 7)
 
 
 def tile_list_candidate_expert_blend_kernel(
@@ -68,10 +71,9 @@ def tile_list_candidate_expert_blend_kernel(
         w4_bf = keep.tile([P, N, PACK], BF16, name="w4_bf", align_bytes=64)
         w4_c = keep.tile([P, N], U32, name="w4_c", align_bytes=64)
         w4_s = keep.tile([P, N], U8, name="w4_s", align_bytes=64)
-        h_bf = {s: keep.tile([P, 2, SPAN, PACK], BF16, name="h_bf%d" % s, align_bytes=64) for s in range(2, SPANS)}
-        h_late = [keep.tile([P, SPAN, PACK], BF16, name="h_late%d" % s, align_bytes=64) for s in range(2)]
-        h_c = {s: keep.tile([P, 2, SPAN], U32, name="h_c%d" % s, align_bytes=64) for s in range(2, SPANS)}
-        h_s = [keep.tile([P, 2, SPAN], U8, name="h_s%d" % s, align_bytes=64) for s in range(SPANS)]
+        h_bf = {(e, s): keep.tile([P, SPAN, PACK], BF16, name="h_bf%d%d" % (e, s), align_bytes=64) for e in range(2) for s in range(SPANS)}
+        h_c = {(e, s): keep.tile([P, SPAN], U32, name="h_c%d%d" % (e, s), tag=HTAG.get((e, s), "h_c%d%d" % (e, s)), align_bytes=64) for e in range(2) for s in range(SPANS)}
+        h_s = {(e, s): keep.tile([P, SPAN], U8, name="h_s%d%d" % (e, s), align_bytes=64) for e in range(2) for s in range(SPANS)}
         banks = [psum.tile([P, 512], F32, name="bank%d" % b) for b in range(8)]
         cache = [keep.tile([P, T2], F32, name="cache%d" % nt, align_bytes=64) for nt in range(N // P)]
         warm = keep.tile([P, 2], F32, name="warm", align_bytes=64)
@@ -115,22 +117,22 @@ def tile_list_candidate_expert_blend_kernel(
         nc.sync.dma_start(idx[:], offs)
         for q in range(QUADS):
             nc.sync.dma_start(out=tab_s[32 * q : 32 * q + 8, :], in_=tab_scales[:, 4 * q : 4 * q + 4, :].bitcast(I32))
-        load_w1(0, 0)
         load_words(tab_w[1][:], tab_words[1])
-        load_w1(0, 1)
-        nc.sync.dma_start(idx2[:], offs2)
         load_wg_scales()
+        load_wg(0)
+        load_w1(0, 0)
+        load_w1(0, 1)
         load_w1(1, 0)
-        load_w3_scales()
         load_w1(1, 1, 0, R // 2)
         load_w1(1, 1, R // 2, R)
-        load_wg(0)
         load_w4(0)
         nc.sync.dma_start(out=w3_w[:], in_=w3_words[0].bitcast(I32))
+        load_w3_scales()
         load_w4(1)
-        load_gain(0, SPAN)
+        nc.sync.dma_start(idx2[:], offs2)
+        load_gain(0, 2 * SPAN)
+        load_gain(2 * SPAN, S)
         load_wg(1)
-        load_gain(SPAN, S)
 
         def entries(lst, j0, j1):
             return lst[:, j0 // LIST_ROWS : j1 // LIST_ROWS]
@@ -153,9 +155,9 @@ def tile_list_candidate_expert_blend_kernel(
                 in_=w1_bf[e, a][:, t0:t1].rearrange("p t m j -> p (t m j)"),
             )
 
-        def cast_w4(u, on_scalar):
-            dst = w4_bf[:, u * (N // 2) : (u + 1) * (N // 2), :].rearrange("p (c i) j -> p c j i", i=4)
-            src = w4_raw[u][:].rearrange("p j (c i) -> p c j i", i=4)
+        def cast_w4(on_scalar, c0, c1):
+            dst = w4_bf[:].rearrange("p (c i) j -> p c j i", i=4)[:, c0:c1]
+            src = w4_raw[c0 // 64][:].rearrange("p j (c i) -> p c j i", i=4)[:, c0 % 64 : (c1 - 1) % 64 + 1]
             if on_scalar:
                 nc.scalar.activation(dst, src, ACT.Copy, scale=-1.0)
             else:
@@ -181,300 +183,231 @@ def tile_list_candidate_expert_blend_kernel(
                     stop=(a == PASSES - 1 and t == PACK - 1),
                 )
 
-        def rounded(e, s):
-            if s >= 2:
-                return h_bf[s][:, e]
-            return h_late[s][:] if e else h_early[:, s]
-
-        def relu(e, chunk, b):
+        def relu(e, chunk, b, on_vector=False):
             s, i = divmod(chunk, SPAN // H_CHUNK)
-            dst = rounded(e, s)[:, i * H_CHUNK : (i + 1) * H_CHUNK, :]
-            nc.scalar.activation(dst, banks[b][:].rearrange("p (t n) -> p n t", t=PACK), ACT.Relu)
+            dst = h_bf[e, s][:, i * H_CHUNK : (i + 1) * H_CHUNK, :]
+            src = banks[b][:].rearrange("p (t n) -> p n t", t=PACK)
+            if on_vector:
+                nc.vector.tensor_scalar_max(dst, src, 0.0)
+            else:
+                nc.scalar.activation(dst, src, ACT.Relu)
 
         def hidden(e, chunk, b):
             for a in range(PASSES):
                 hidden_pass(e, chunk, b, a)
             relu(e, chunk, b)
 
-        def quant_h(s):
-            nc.vector.quantize_mx(
-                out=h_c[s][:].rearrange("p e n -> p (e n)").bitcast(FP8X4),
-                scales=h_s[s][:].rearrange("p e n -> p (e n)"),
-                in_=h_bf[s][:].rearrange("p e n t -> p (e n t)"),
-            )
+        def quant_h(e, s):
+            nc.vector.quantize_mx(out=h_c[e, s][:].bitcast(FP8X4), scales=h_s[e, s][:], in_=h_bf[e, s][:].rearrange("p n t -> p (n t)"))
 
-        def quant_expert(e, s):
-            nc.vector.quantize_mx(
-                out=h_c[s][:, e, :].bitcast(FP8X4), scales=h_s[s][:, e, :], in_=rounded(e, s).rearrange("p n t -> p (n t)")
-            )
+        def w3_cols(nt):
+            return w3_w[:].bitcast(U8)[:, 2 * nt * P : 2 * (nt + 1) * P].bitcast(FP4X4), w_s[:, 1, :].bitcast(U8)[:, nt * P : (nt + 1) * P]
 
-        def expert1(dst, nt, sp, c0, c1, start, stop):
-            nc.tensor.matmul_mx(
-                out=dst,
-                lhsT=w3_w[:].bitcast(U8)[:, 2 * nt * P : 2 * (nt + 1) * P].bitcast(FP4X4),
-                lhsT_scale=w_s[:, 1, :].bitcast(U8)[:, nt * P : (nt + 1) * P],
-                rhs=h_c[sp][:, 0, c0:c1].bitcast(FP8X4),
-                rhs_scale=h_s[sp][:, 0, c0:c1],
-                start=start,
-                stop=stop,
-            )
+        def w4_cols(nt):
+            return w4_c[:, nt * P : (nt + 1) * P].bitcast(FP8X4), w4_s[:, nt * P : (nt + 1) * P]
 
-        def expert2_negated(dst, nt, sp, c0, c1, start, stop):
-            nc.tensor.matmul_mx(
-                out=dst,
-                lhsT=w4_c[:, nt * P : (nt + 1) * P].bitcast(FP8X4),
-                lhsT_scale=w4_s[:, nt * P : (nt + 1) * P],
-                rhs=h_c[sp][:, 1, c0:c1].bitcast(FP8X4),
-                rhs_scale=h_s[sp][:, 1, c0:c1],
-                start=start,
-                stop=stop,
-            )
-
-        def gate_logits(z, nt, sp):
-            rows = slice(nt * P, (nt + 1) * P)
+        def wg_cols(nt, a):
             own = slice(nt % 2 * P, (nt % 2 + 1) * P)
-            for a in range(PASSES):
-                nc.tensor.matmul_mx(
-                    out=z,
-                    lhsT=wg_w[nt // 2][:, a, own].bitcast(FP8X4),
-                    lhsT_scale=w_s[4 * a : P, 0, :].bitcast(U8)[:, rows],
-                    rhs=v_w[a][:, sp * SPAN : (sp + 1) * SPAN].bitcast(FP8X4),
-                    rhs_scale=v_s[4 * a : P, sp * SPAN : (sp + 1) * SPAN],
-                    start=(a == 0),
-                    stop=(a == PASSES - 1),
-                )
+            return wg_w[nt // 2][:, a, own].bitcast(FP8X4), w_s[4 * a : P, 0, :].bitcast(U8)[:, nt * P : (nt + 1) * P]
 
-        def parts(unit):
-            return [(nt, s, i * SPAN, (i + 1) * SPAN) for i, (nt, s) in enumerate(unit)]
+        def h_cols(e, s, j0, j1):
+            return h_c[e, s][:, j0:j1].bitcast(FP8X4), h_s[e, s][:, j0:j1]
 
-        def sigmoid(b, sign):
-            gate = ring.tile([P, BANK], F32, name="gate", bufs=GATES)
-            nc.scalar.activation(gate[:], banks[b][:], ACT.Sigmoid, scale=sign)
+        def v_cols(a, j0, j1):
+            return v_w[a][:, j0:j1].bitcast(FP8X4), v_s[4 * a : P, j0:j1]
+
+        def mx(dst, stationary, moving, start, stop):
+            nc.tensor.matmul_mx(
+                out=dst, lhsT=stationary[0], lhsT_scale=stationary[1], rhs=moving[0], rhs_scale=moving[1], start=start, stop=stop
+            )
+
+        turn = [0]
+
+        def take():
+            turn[0] += 1
+            return banks[TENANTS[turn[0] - 1] if turn[0] <= len(TENANTS) else RING[(turn[0] - 1 - len(TENANTS)) % len(RING)]]
+
+        def held(name, bufs=HELD):
+            return ring.tile([P, BANK], F32, name=name, bufs=bufs)
+
+        def sigmoid(bank, sign=1.0):
+            gate = held("gate", GATES)
+            nc.scalar.activation(gate[:], bank[:], ACT.Sigmoid, scale=sign)
             return gate
 
-        def gate_of(unit, b):
-            for nt, s, c0, c1 in parts(unit):
-                gate_logits(banks[b][:, c0:c1], nt, s)
-            return sigmoid(b, 1.0)
+        def blocks(atoms):
+            return [(nt, s, j, i * SPAN + j) for i, (nt, s) in enumerate(atoms) for j in range(0, SPAN, P)]
 
-        def difference(unit, b):
-            for nt, s, c0, c1 in parts(unit):
-                for d in range(0, SPAN, H_CHUNK):
-                    expert1(banks[b][:, c0 + d : c0 + d + H_CHUNK], nt, s, d, d + H_CHUNK, c0 + d == 0, False)
-            for nt, s, c0, c1 in parts(unit):
-                expert2_negated(banks[b][:, c0:c1], nt, s, 0, SPAN, False, c1 == BANK)
-
-        def first_expert(unit, b):
-            for nt, s, c0, c1 in parts(unit):
-                expert1(banks[b][:, c0:c1], nt, s, 0, SPAN, True, True)
-
-        def second_expert(unit, b):
-            for nt, s, c0, c1 in parts(unit):
-                expert2_negated(banks[b][:, c0:c1], nt, s, 0, SPAN, True, True)
-
-        def blocks(unit):
-            return [(nt, s, i * P, c0 + i * P) for nt, s, c0, c1 in parts(unit) for i in range(SPAN // P)]
-
-        def turned_gate(unit, b):
-            for nt, s, j, c in blocks(unit):
-                cols = slice(s * SPAN + j, s * SPAN + j + P)
+        def plain_gate(unit):
+            bank = take()
+            for i, (nt, s) in enumerate(unit):
                 for a in range(PASSES):
-                    nc.tensor.matmul_mx(
-                        out=banks[b][:, c : c + P],
-                        lhsT=v_w[a][:, cols].bitcast(FP8X4),
-                        lhsT_scale=v_s[4 * a : P, cols],
-                        rhs=wg_w[nt // 2][:, a, nt % 2 * P : (nt % 2 + 1) * P].bitcast(FP8X4),
-                        rhs_scale=w_s[4 * a : P, 0, :].bitcast(U8)[:, nt * P : (nt + 1) * P],
-                        start=(a == 0),
-                        stop=(a == PASSES - 1),
-                    )
+                    mx(bank[:, i * SPAN : (i + 1) * SPAN], wg_cols(nt, a), v_cols(a, s * SPAN, (s + 1) * SPAN), a == 0, a == PASSES - 1)
+            return sigmoid(bank), sigmoid(bank, -1.0)
 
-        def turned_expert1(dst, nt, s, j, stop):
-            nc.tensor.matmul_mx(
-                out=dst,
-                lhsT=h_c[s][:, 0, j : j + P].bitcast(FP8X4),
-                lhsT_scale=h_s[s][:, 0, j : j + P],
-                rhs=w3_w[:].bitcast(U8)[:, 2 * nt * P : 2 * (nt + 1) * P].bitcast(FP4X4),
-                rhs_scale=w_s[:, 1, :].bitcast(U8)[:, nt * P : (nt + 1) * P],
-                start=True,
-                stop=stop,
-            )
-
-        def turned_expert2(dst, nt, s, j, start):
-            nc.tensor.matmul_mx(
-                out=dst,
-                lhsT=h_c[s][:, 1, j : j + P].bitcast(FP8X4),
-                lhsT_scale=h_s[s][:, 1, j : j + P],
-                rhs=w4_c[:, nt * P : (nt + 1) * P].bitcast(FP8X4),
-                rhs_scale=w4_s[:, nt * P : (nt + 1) * P],
-                start=start,
-                stop=True,
-            )
-
-        def turned_terms(u):
-            unit, apart = units[u], u == len(units) - 1
-            b = take()
-            turned_gate(unit, b)
-            gate = sigmoid(b, 1.0)
-            if apart:
-                rest = sigmoid(b, -1.0)
-            b = take()
+        def turned_gate(unit):
+            bank = take()
             for nt, s, j, c in blocks(unit):
-                turned_expert1(banks[b][:, c : c + P], nt, s, j, apart)
-                if not apart:
-                    turned_expert2(banks[b][:, c : c + P], nt, s, j, False)
-            first = copy_out(b, "diff")
-            b = take()
-            for nt, s, j, c in blocks(unit):
-                turned_expert2(banks[b][:, c : c + P], nt, s, j, True)
-            second = ring.tile([P, BANK], F32, name="second", bufs=HELD)
-            nc.scalar.activation(second[:], banks[b][:], ACT.Copy, scale=-1.0)
-            terms[u] = [second, combine(nc.gpsimd, "plus", first[:], gate[:], ALU.mult)]
-            if apart:
-                rests[u] = rest
+                for a in range(PASSES):
+                    mx(bank[:, c : c + P], v_cols(a, s * SPAN + j, s * SPAN + j + P), wg_cols(nt, a), a == 0, a == PASSES - 1)
+            return sigmoid(bank)
 
-        def turned_sum(u):
-            if u in rests:
-                terms[u] = [terms[u][1], combine(nc.gpsimd, "summed", terms[u][0][:], rests[u][:], ALU.mult)]
-            b = take()
-            for i, term in enumerate(terms[u]):
-                for c in range(0, BANK, P):
-                    opens, closes = i == 0 and c == 0, i == 1 and c == BANK - P
-                    nc.tensor.matmul(banks[b][:, c : c + P], term[:, c : c + P], identity[:], start=opens, stop=closes, is_transpose=True)
-            return copy_out(b, "summed" if u < len(units) - 1 else "diff")
+        def factors(atoms):
+            s0, s1 = atoms[0][1], atoms[-1][1]
+            if len(atoms) == 2 and s0 == s1:
+                return gain[:, s0 * SPAN : (s0 + 1) * SPAN].unsqueeze(1).to_broadcast([P, 2, SPAN])
+            return gain[:, s0 * SPAN : (s1 + 1) * SPAN].rearrange("p (r j) -> p r j", j=SPAN)
 
-        def copy_out(b, name):
-            held = ring.tile([P, BANK], F32, name=name, bufs=1 if name == "summed" else HELD)
-            nc.scalar.copy(held[:], banks[b][:])
-            return held
-
-        def combine(engine, name, x, y, op):
-            result = ring.tile([P, BANK], F32, name=name, bufs=1 if name in ("y", "summed") else HELD)
-            engine.tensor_tensor(result[:], x, y, op)
-            return result
-
-        def weigh(engine, unit, y, weighted):
-            s0, s1 = unit[0][1], unit[1][1]
-            if s0 == s1:
-                factors = gain[:, s0 * SPAN : (s0 + 1) * SPAN].unsqueeze(1).to_broadcast([P, 2, SPAN])
-            else:
-                factors = gain[:, s0 * SPAN : (s1 + 1) * SPAN].rearrange("p (r j) -> p r j", r=2)
+        def weigh(engine, atoms, y):
+            w = len(atoms) * SPAN
+            weighted = held("weighted", WEIGHTED)
             engine.tensor_tensor(
-                weighted[:].rearrange("p (r j) -> p r j", r=2), y[:].rearrange("p (r j) -> p r j", r=2), factors, ALU.mult
+                weighted[:, :w].rearrange("p (r j) -> p r j", j=SPAN), y[:, :w].rearrange("p (r j) -> p r j", j=SPAN), factors(atoms), ALU.mult
             )
             return weighted
 
-        def store(nt):
-            nc.sync.dma_start(out=out[nt * P : (nt + 1) * P, :], in_=cache[nt][:])
+        def turned_terms(atoms, joint, on_vector=False):
+            w = len(atoms) * SPAN
+            bank = take()
+            for nt, s, j, c in blocks(atoms):
+                mx(bank[:, c : c + P], h_cols(0, s, j, j + P), w3_cols(nt), True, not joint)
+                if joint:
+                    mx(bank[:, c : c + P], h_cols(1, s, j, j + P), w4_cols(nt), False, True)
+            c1 = w % BANK
+            other = bank if c1 else take()
+            for nt, s, j, c in blocks(atoms):
+                mx(other[:, c1 + c : c1 + c + P], h_cols(1, s, j, j + P), w4_cols(nt), True, True)
+            diff = bank if on_vector else held("diff")
+            if not on_vector:
+                nc.scalar.copy(diff[:, :w], bank[:, :w])
+            second = held("second")
+            nc.scalar.activation(second[:, :w], other[:, c1 : c1 + w], ACT.Copy, scale=-1.0)
+            return diff, second
 
-        def place(unit, weighted):
-            if unit[0][0] == unit[1][0]:
-                nt, s = unit[0]
-                nc.vector.tensor_copy(out=cache[nt][:].indirect(entries(idx2, s * SPAN, (s + 2) * SPAN)), in_=weighted[:])
-                store(nt)
-                return
-            for nt, s, c0, c1 in parts(unit):
-                nc.vector.tensor_copy(out=cache[nt][:].indirect(entries(idx2, s * SPAN, (s + 1) * SPAN)), in_=weighted[:, c0:c1])
-                if s == SPANS - 1:
-                    store(nt)
+        def gated_terms(atoms, gate, joint, slot, copies, engine):
+            w = len(atoms) * SPAN
+            diff, second = copies
+            if not joint:
+                first, diff = diff, held("apart", 1)
+                nc.gpsimd.tensor_tensor(diff[:, :w], first[:, :w], second[:, :w], ALU.subtract)
+            gated = keep.tile([P, BANK], F32, name="gated", tag=slot, align_bytes=64)
+            engine.tensor_tensor(gated[:, :w], diff[:, :w], gate, ALU.mult)
+            return second, gated
+
+        def turned_sum(atoms, terms, slot):
+            w = len(atoms) * SPAN
+            bank = take()
+            for i, term in enumerate(terms):
+                for c in range(0, w, P):
+                    nc.tensor.matmul(
+                        bank[:, c : c + P], term[:, c : c + P], identity[:], start=(i == 0 and c == 0), stop=(i == 1 and c == w - P), is_transpose=True
+                    )
+            summed = keep.tile([P, BANK], F32, name="summed", tag=slot, align_bytes=64)
+            nc.scalar.copy(summed[:, :w], bank[:, :w])
+            return summed
+
+        done = {nt: 0 for nt in range(N // P)}
+
+        def place(atoms, weighted, fused=False):
+            runs = [atoms] if atoms[0][0] == atoms[-1][0] else [[atom] for atom in atoms]
+            c = 0
+            for run in runs:
+                nt, s = run[0]
+                w = len(run) * SPAN
+                window = cache[nt][:].indirect(entries(idx2, s * SPAN, s * SPAN + w))
+                if fused:
+                    nc.vector.tensor_tensor(window, weighted[:, c : c + w], gain[:, s * SPAN : s * SPAN + w], ALU.mult)
+                else:
+                    nc.vector.tensor_copy(out=window, in_=weighted[:, c : c + w])
+                c = c + w
+                done[nt] = done[nt] + w
+                if done[nt] == S:
+                    nc.sync.dma_start(out=out[nt * P : (nt + 1) * P, :], in_=cache[nt][:])
 
         half = S // 2
         gather_words(0, 0, half)
         gather_words(0, half, S)
         gather_scales(0, half)
         gather_scales(half, S)
-        cast_w1(0, 0, 0, P, nc.scalar.copy)
         gather_words(1, 0, half)
-        quant_w1(0, 0)
         gather_words(1, half, S)
+        units = [((0, s), (1, s)) for s in range(SPANS)] + [((nt, s), (nt, s + 1)) for s in (0, 2) for nt in (2, 3)]
+        gate, rest = plain_gate(units[0])
+        gates = {u: turned_gate(units[u]) for u in (1, 2, 3)}
+        cast_w1(0, 0, 0, P, nc.vector.tensor_copy)
+        quant_w1(0, 0)
         cast_w1(0, 1, 0, SPLIT01, nc.vector.tensor_copy)
         cast_w1(0, 1, SPLIT01, P, nc.scalar.copy)
         quant_w1(0, 1)
         cast_w1(1, 0, 0, SPLIT10, nc.vector.tensor_copy)
-        cast_w1(1, 0, SPLIT10, P, nc.scalar.copy)
-        cast_w1(1, 1, 0, P // 2, nc.vector.tensor_copy)
+        if SPLIT10 < P:
+            cast_w1(1, 0, SPLIT10, P, nc.scalar.copy)
         quant_w1(1, 0)
+        cast_w1(1, 1, 0, P // 2, nc.vector.tensor_copy)
         cast_w1(1, 1, P // 2, P, nc.vector.tensor_copy)
         quant_w1(1, 1, 0, 2)
         quant_w1(1, 1, 2, 4)
-        units = [((nt, s), (nt + 1, s)) for s in range(2) for nt in (0, 2)]
-        units = units + [((0, s), (1, s)) for s in (2, 3)] + [((nt, 2), (nt, 3)) for nt in (2, 3)]
-        h_early = keep.tile([P, 2, SPAN, PACK], BF16, name="h_early", tag="w1_raw10", align_bytes=64)
-        h_c_early = keep.tile([P, 2, 2, SPAN], U32, name="h_c_early", tag="w1_raw11", align_bytes=64)
-        h_c[0], h_c[1] = h_c_early[:, 0], h_c_early[:, 1]
+        for chunk in range(8):
+            hidden(0, chunk, (chunk + 4) % 8)
         for chunk in range(2):
-            hidden(0, chunk, chunk)
+            hidden_pass(1, chunk, 4 + chunk, 0)
         for chunk in range(2):
-            hidden_pass(1, chunk, 2 + chunk, 0)
-        hidden(0, 2, 5)
-        hidden(0, 3, 6)
-        quant_expert(0, 0)
-        cast_w4(0, False)
-        gate = gate_of(units[0], 4)
-        rest = sigmoid(4, -1.0)
-        for chunk in range(2):
-            hidden_pass(1, chunk, 2 + chunk, 1)
-            relu(1, chunk, 2 + chunk)
+            hidden_pass(1, chunk, 4 + chunk, 1)
+            relu(1, chunk, 4 + chunk, chunk == VRELU)
+        cast_w4(False, 0, 64)
+        cast_w4(True, SPLIT4, P)
+        quant_h(1, 0)
         quant_w4(0)
-        quant_expert(0, 1)
-        quant_expert(1, 0)
-        first_expert(units[0], 0)
-        second_expert(units[0], 1)
-        plus = combine(nc.vector, "gated", banks[0][:], gate[:], ALU.mult)
-        cast_w4(1, W4_ON_SCALAR)
+        for s in range(SPANS):
+            quant_h(0, s)
+        ebank, mbank = banks[3], banks[7]
+        halves = [slice(i * SPAN, (i + 1) * SPAN) for i in range(2)]
+        for i, (nt, s) in enumerate(units[0]):
+            mx(mbank[:, halves[i]], w4_cols(nt), h_cols(1, s, 0, SPAN), True, True)
+        for i, (nt, s) in enumerate(units[0]):
+            mx(ebank[:, halves[i]], w3_cols(nt), h_cols(0, s, 0, SPAN), True, True)
+        hidden(1, 2, 0)
+        hidden(1, 3, 1)
+        for chunk, b in zip(range(4, 8), (2, 6, 4, 5)):
+            hidden(1, chunk, b)
+        plus = held("vp", 1)
+        minus = held("vg", 1)
+        y = held("vy", 1)
+        for cols in halves:
+            nc.vector.tensor_tensor(minus[:, cols], mbank[:, cols], rest[:, cols], ALU.mult)
+        nc.vector.tensor_tensor(plus[:], ebank[:], gate[:], ALU.mult)
+        if SPLIT4 > 64:
+            cast_w4(False, 64, SPLIT4)
+        quant_h(1, 1)
+        for cols in halves:
+            nc.vector.tensor_tensor(y[:, cols], plus[:, cols], minus[:, cols], ALU.subtract)
+        quant_h(1, 2)
+        first = [weigh(nc.vector, units[0][i : i + 1], y[:, halves[i]]) for i in range(2)]
         quant_w4(1)
-        minus = combine(nc.vector, "minus", banks[1][:], rest[:], ALU.mult)
-        for chunk in range(2, 4):
-            hidden(1, chunk, chunk)
-        quant_expert(1, 1)
-        y = combine(nc.vector, "y", plus[:], minus[:], ALU.subtract)
-        turn = [0]
 
-        def take():
-            turn[0] += 1
-            return RING[(turn[0] - 1) % len(RING)]
-
-        def gated_on_vector(u):
-            gate = gate_of(units[u], take())
-            b = VB[u % len(VB)] if VB else take()
-            difference(units[u], b)
-            gated[u] = combine(nc.vector, "gated", banks[b][:], gate[:], ALU.mult)
-
-        def prepare(u):
-            if u < TURNED:
-                gated_on_vector(u)
-            else:
-                turned_terms(u)
+        def atom(u, i):
+            return units[u][i : i + 1]
 
         last = len(units) - 1
-        gated, terms, rests = {}, {}, {}
-        for u in range(1, len(units)):
-            if u == 1:
-                gated_on_vector(u)
-            if u == 1:
-                ready = weigh(nc.vector, units[0], y, keep.tile([P, BANK], F32, name="first", tag="h_late1", align_bytes=64))
-            for later in EARLY.get(u, ()):
-                prepare(later)
-            chunks = [(e, c) for c in (2 * u + 2, 2 * u + 3) for e in range(2)] if u + 1 < SPANS else []
-            for e, c in chunks[:BEFORE]:
-                hidden(e, c, take())
-            if u < TURNED:
-                b = take()
-                second_expert(units[u], b)
-                minus = copy_out(b, "minus")
-            for e, c in chunks[BEFORE:]:
-                hidden(e, c, take())
-            if chunks:
-                quant_h(u + 1)
-            for later in LATE.get(u, ()):
-                prepare(later)
-            place(units[u - 1], ready)
-            if u < TURNED:
-                y = combine(nc.gpsimd, "y", gated[u][:], minus[:], ALU.subtract)
-            else:
-                y = turned_sum(u)
-            if u < last:
-                ready = weigh(nc.gpsimd, units[u], y, ring.tile([P, BANK], F32, name="weighted", bufs=WEIGHTED))
-        nt, s = units[last][0]
-        nc.vector.tensor_tensor(cache[nt][:].indirect(entries(idx2, s * SPAN, S)), y[:], gain[:, s * SPAN : S], ALU.mult)
-        store(nt)
+        copies, terms = {}, {}
+
+        def begin(u):
+            if u not in gates:
+                gates[u] = turned_gate(units[u])
+            copies[u] = turned_terms(units[u], u < last, u in ON_VECTOR)
+
+        def gate_unit(u):
+            engine = nc.vector if u in ON_VECTOR else nc.gpsimd
+            terms[u] = gated_terms(units[u], gates[u][:], u < last, SLOTS[u % len(SLOTS)], copies[u], engine)
+
+        def finish(u):
+            summed = turned_sum(units[u], terms[u], SLOTS[u % len(SLOTS)])
+            place(units[u], summed if u == last else weigh(nc.gpsimd, units[u], summed), u == last)
+
+        def first_places(u):
+            quant_h(1, 3)
+            for i in range(2):
+                place(atom(0, i), first[i])
+
+        for step in STEPS.split():
+            {"b": begin, "g": gate_unit, "f": finish, "p": first_places}[step[0]](int(step[1]))

@@ -27,20 +27,36 @@ BANK = 512
 SPAN = 256
 SPANS = S // SPAN
 SPLIT10 = 128
-SPLIT4 = 112
-HTAG = {(0, 0): "w1_bf10"}
-VRELU = 9
+SPLIT4 = 96
+JOINT = 6
+JOINT0 = 1
+PE_DIFF = 1
+PIN0 = "pin0"
+HTAG = {(0, 0): "w1_bf11"}
+EARLY1 = 0
+LASTSLOT = 0
+PAIRS = 1
+WIDE = 0
+EARLY11 = 0
+SPLIT40 = 64
+HB = (0, 1, 4, 5, 0, 1)
+VRELU = (1,)
+LOADS = 'sgabcdef3tFiwWG'
+EARLY_GATES = 1
+GATED = (1, 2, 3)
+SPLIT00 = 128
+EB = (4,5,6,7,0,1,2,3)
 SPLIT01 = 96
 GATES = 5
-HELD = 3
+HELD = 4
 WEIGHTED = 6
 W4B_ON_SCALAR = True
 MODES = ("V", "A", "T", "T", "T", "T", "T", "X")
 ON_VECTOR = (1,)
-SLOTS = ("h_bf13", "h_bf11")
-STEPS = "b1 g1 p0 b2 g2 f1 b3 g3 f2 b4 g4 f3 b5 g5 f4 b6 g6 f5 b7 g7 f6 f7"
+SLOTS = ("w4_bf", "h_bf11")
+STEPS = "b1 g1 p0 b2 g2 f1 b3 g3 f2 b4 g4 a6 f3 b5 g5 b6 f4 a7 g6 f5 b7 g7 f6 f7"
 TENANTS = (0, 1, 2, 3)
-RING = (0, 1, 2, 6, 3, 4, 5, 7)
+RING = (2, 6, 5, 3, 7, 0, 1, 4)
 
 
 def tile_list_candidate_expert_blend_kernel(
@@ -71,9 +87,17 @@ def tile_list_candidate_expert_blend_kernel(
         w4_bf = keep.tile([P, N, PACK], BF16, name="w4_bf", align_bytes=64)
         w4_c = keep.tile([P, N], U32, name="w4_c", align_bytes=64)
         w4_s = keep.tile([P, N], U8, name="w4_s", align_bytes=64)
-        h_bf = {(e, s): keep.tile([P, SPAN, PACK], BF16, name="h_bf%d%d" % (e, s), align_bytes=64) for e in range(2) for s in range(SPANS)}
-        h_c = {(e, s): keep.tile([P, SPAN], U32, name="h_c%d%d" % (e, s), tag=HTAG.get((e, s), "h_c%d%d" % (e, s)), align_bytes=64) for e in range(2) for s in range(SPANS)}
-        h_s = {(e, s): keep.tile([P, SPAN], U8, name="h_s%d%d" % (e, s), align_bytes=64) for e in range(2) for s in range(SPANS)}
+        groups = ([(0, 0, 2), (0, 2, 2)] if PAIRS else [(0, s, 1) for s in range(SPANS)]) + [(1, s, 1) for s in range(SPANS)]
+        h_bf, h_c, h_s = {}, {}, {}
+        for e, s0, n in groups:
+            h_bf[e, s0] = keep.tile([P, n * SPAN, PACK], BF16, name="h_bf%d%d" % (e, s0), align_bytes=64)
+            h_c[e, s0] = keep.tile([P, n * SPAN], U32, name="h_c%d%d" % (e, s0), tag=HTAG.get((e, s0), "h_c%d%d" % (e, s0)), align_bytes=64)
+            h_s[e, s0] = keep.tile([P, n * SPAN], U8, name="h_s%d%d" % (e, s0), align_bytes=64)
+
+        def group_of(e, j):
+            s0 = max(g[1] for g in groups if g[0] == e and g[1] * SPAN <= j)
+            return (e, s0), j - s0 * SPAN
+
         banks = [psum.tile([P, 512], F32, name="bank%d" % b) for b in range(8)]
         cache = [keep.tile([P, T2], F32, name="cache%d" % nt, align_bytes=64) for nt in range(N // P)]
         warm = keep.tile([P, 2], F32, name="warm", align_bytes=64)
@@ -118,21 +142,25 @@ def tile_list_candidate_expert_blend_kernel(
         for q in range(QUADS):
             nc.sync.dma_start(out=tab_s[32 * q : 32 * q + 8, :], in_=tab_scales[:, 4 * q : 4 * q + 4, :].bitcast(I32))
         load_words(tab_w[1][:], tab_words[1])
-        load_wg_scales()
-        load_wg(0)
-        load_w1(0, 0)
-        load_w1(0, 1)
-        load_w1(1, 0)
-        load_w1(1, 1, 0, R // 2)
-        load_w1(1, 1, R // 2, R)
-        load_w4(0)
-        nc.sync.dma_start(out=w3_w[:], in_=w3_words[0].bitcast(I32))
-        load_w3_scales()
-        load_w4(1)
-        nc.sync.dma_start(idx2[:], offs2)
-        load_gain(0, 2 * SPAN)
-        load_gain(2 * SPAN, S)
-        load_wg(1)
+        loads = {
+            "s": load_wg_scales,
+            "g": lambda: load_wg(0),
+            "G": lambda: load_wg(1),
+            "a": lambda: load_w1(0, 0),
+            "b": lambda: load_w1(0, 1),
+            "c": lambda: load_w1(1, 0),
+            "d": lambda: load_w1(1, 1, 0, R // 2),
+            "e": lambda: load_w1(1, 1, R // 2, R),
+            "f": lambda: load_w4(0),
+            "F": lambda: load_w4(1),
+            "3": lambda: nc.sync.dma_start(out=w3_w[:], in_=w3_words[0].bitcast(I32)),
+            "t": load_w3_scales,
+            "i": lambda: nc.sync.dma_start(idx2[:], offs2),
+            "w": lambda: load_gain(0, 2 * SPAN),
+            "W": lambda: load_gain(2 * SPAN, S),
+        }
+        for key in LOADS:
+            loads[key]()
 
         def entries(lst, j0, j1):
             return lst[:, j0 // LIST_ROWS : j1 // LIST_ROWS]
@@ -184,8 +212,8 @@ def tile_list_candidate_expert_blend_kernel(
                 )
 
         def relu(e, chunk, b, on_vector=False):
-            s, i = divmod(chunk, SPAN // H_CHUNK)
-            dst = h_bf[e, s][:, i * H_CHUNK : (i + 1) * H_CHUNK, :]
+            key, j = group_of(e, chunk * H_CHUNK)
+            dst = h_bf[key][:, j : j + H_CHUNK, :]
             src = banks[b][:].rearrange("p (t n) -> p n t", t=PACK)
             if on_vector:
                 nc.vector.tensor_scalar_max(dst, src, 0.0)
@@ -195,7 +223,7 @@ def tile_list_candidate_expert_blend_kernel(
         def hidden(e, chunk, b):
             for a in range(PASSES):
                 hidden_pass(e, chunk, b, a)
-            relu(e, chunk, b)
+            relu(e, chunk, b, e == 1 and chunk in VRELU)
 
         def quant_h(e, s):
             nc.vector.quantize_mx(out=h_c[e, s][:].bitcast(FP8X4), scales=h_s[e, s][:], in_=h_bf[e, s][:].rearrange("p n t -> p (n t)"))
@@ -211,7 +239,8 @@ def tile_list_candidate_expert_blend_kernel(
             return wg_w[nt // 2][:, a, own].bitcast(FP8X4), w_s[4 * a : P, 0, :].bitcast(U8)[:, nt * P : (nt + 1) * P]
 
         def h_cols(e, s, j0, j1):
-            return h_c[e, s][:, j0:j1].bitcast(FP8X4), h_s[e, s][:, j0:j1]
+            key, j = group_of(e, s * SPAN + j0)
+            return h_c[key][:, j : j + j1 - j0].bitcast(FP8X4), h_s[key][:, j : j + j1 - j0]
 
         def v_cols(a, j0, j1):
             return v_w[a][:, j0:j1].bitcast(FP8X4), v_s[4 * a : P, j0:j1]
@@ -243,7 +272,7 @@ def tile_list_candidate_expert_blend_kernel(
             for i, (nt, s) in enumerate(unit):
                 for a in range(PASSES):
                     mx(bank[:, i * SPAN : (i + 1) * SPAN], wg_cols(nt, a), v_cols(a, s * SPAN, (s + 1) * SPAN), a == 0, a == PASSES - 1)
-            return sigmoid(bank), sigmoid(bank, -1.0)
+            return sigmoid(bank), (None if JOINT0 else sigmoid(bank, -1.0))
 
         def turned_gate(unit):
             bank = take()
@@ -258,16 +287,46 @@ def tile_list_candidate_expert_blend_kernel(
                 return gain[:, s0 * SPAN : (s0 + 1) * SPAN].unsqueeze(1).to_broadcast([P, 2, SPAN])
             return gain[:, s0 * SPAN : (s1 + 1) * SPAN].rearrange("p (r j) -> p r j", j=SPAN)
 
-        def weigh(engine, atoms, y):
+        def weigh(engine, atoms, y, weighted=None):
             w = len(atoms) * SPAN
-            weighted = held("weighted", WEIGHTED)
+            weighted = weighted or held("weighted", WEIGHTED)
             engine.tensor_tensor(
                 weighted[:, :w].rearrange("p (r j) -> p r j", j=SPAN), y[:, :w].rearrange("p (r j) -> p r j", j=SPAN), factors(atoms), ALU.mult
             )
             return weighted
 
+        def turn_over(tiles):
+            bank = take()
+            for i, term in enumerate(tiles):
+                for c in range(0, BANK, P):
+                    opens, closes = i == 0 and c == 0, i == len(tiles) - 1 and c == BANK - P
+                    nc.tensor.matmul(bank[:, c : c + P], term[:, c : c + P], identity[:], start=opens, stop=closes, is_transpose=True)
+            return bank
+
+        def plain_terms(atoms):
+            plain = []
+            for e, cols in enumerate((w3_cols, w4_cols)):
+                bank = take()
+                for i, (nt, s) in enumerate(atoms):
+                    mx(bank[:, i * SPAN : (i + 1) * SPAN], cols(nt), h_cols(e, s, 0, SPAN), True, True)
+                plain.append(held("plain", 4))
+                nc.scalar.copy(plain[e][:], bank[:])
+            return plain
+
+        early = {}
+
+        def terms_by_transposes(atoms):
+            plain = early.get(atoms) or plain_terms(atoms)
+            diff = held("diff")
+            nc.scalar.copy(diff[:], turn_over(plain)[:])
+            second = held("second")
+            nc.scalar.activation(second[:], turn_over(plain[1:])[:], ACT.Copy, scale=-1.0)
+            return diff, second
+
         def turned_terms(atoms, joint, on_vector=False):
             w = len(atoms) * SPAN
+            if not joint and PE_DIFF:
+                return terms_by_transposes(atoms)
             bank = take()
             for nt, s, j, c in blocks(atoms):
                 mx(bank[:, c : c + P], h_cols(0, s, j, j + P), w3_cols(nt), True, not joint)
@@ -287,7 +346,7 @@ def tile_list_candidate_expert_blend_kernel(
         def gated_terms(atoms, gate, joint, slot, copies, engine):
             w = len(atoms) * SPAN
             diff, second = copies
-            if not joint:
+            if not joint and not PE_DIFF:
                 first, diff = diff, held("apart", 1)
                 nc.gpsimd.tensor_tensor(diff[:, :w], first[:, :w], second[:, :w], ALU.subtract)
             gated = keep.tile([P, BANK], F32, name="gated", tag=slot, align_bytes=64)
@@ -331,10 +390,14 @@ def tile_list_candidate_expert_blend_kernel(
         gather_scales(half, S)
         gather_words(1, 0, half)
         gather_words(1, half, S)
-        units = [((0, s), (1, s)) for s in range(SPANS)] + [((nt, s), (nt, s + 1)) for s in (0, 2) for nt in (2, 3)]
-        gate, rest = plain_gate(units[0])
-        gates = {u: turned_gate(units[u]) for u in (1, 2, 3)}
-        cast_w1(0, 0, 0, P, nc.vector.tensor_copy)
+        units = [((0, s), (1, s)) for s in range(2)] + ([((nt, 2), (nt, 3)) for nt in (0, 1)] if WIDE else [((0, s), (1, s)) for s in (2, 3)])
+        units = units + [((nt, s), (nt, s + 1)) for s in (0, 2) for nt in (2, 3)]
+        if EARLY_GATES:
+            gate, rest = plain_gate(units[0])
+            gates = {u: turned_gate(units[u]) for u in GATED}
+        cast_w1(0, 0, 0, SPLIT00, nc.vector.tensor_copy)
+        if SPLIT00 < P:
+            cast_w1(0, 0, SPLIT00, P, nc.scalar.copy)
         quant_w1(0, 0)
         cast_w1(0, 1, 0, SPLIT01, nc.vector.tensor_copy)
         cast_w1(0, 1, SPLIT01, P, nc.scalar.copy)
@@ -348,43 +411,23 @@ def tile_list_candidate_expert_blend_kernel(
         quant_w1(1, 1, 0, 2)
         quant_w1(1, 1, 2, 4)
         for chunk in range(8):
-            hidden(0, chunk, (chunk + 4) % 8)
+            hidden(0, chunk, EB[chunk])
         for chunk in range(2):
             hidden_pass(1, chunk, 4 + chunk, 0)
+        if not EARLY_GATES:
+            gate, rest = plain_gate(units[0])
+            gates = {u: turned_gate(units[u]) for u in GATED}
         for chunk in range(2):
             hidden_pass(1, chunk, 4 + chunk, 1)
-            relu(1, chunk, 4 + chunk, chunk == VRELU)
-        cast_w4(False, 0, 64)
-        cast_w4(True, SPLIT4, P)
+            relu(1, chunk, 4 + chunk, chunk in VRELU)
+        cast_w4(False, 0, SPLIT40)
+        if SPLIT40 < 64:
+            cast_w4(True, SPLIT40, 64)
         quant_h(1, 0)
         quant_w4(0)
-        for s in range(SPANS):
-            quant_h(0, s)
-        ebank, mbank = banks[3], banks[7]
-        halves = [slice(i * SPAN, (i + 1) * SPAN) for i in range(2)]
-        for i, (nt, s) in enumerate(units[0]):
-            mx(mbank[:, halves[i]], w4_cols(nt), h_cols(1, s, 0, SPAN), True, True)
-        for i, (nt, s) in enumerate(units[0]):
-            mx(ebank[:, halves[i]], w3_cols(nt), h_cols(0, s, 0, SPAN), True, True)
-        hidden(1, 2, 0)
-        hidden(1, 3, 1)
-        for chunk, b in zip(range(4, 8), (2, 6, 4, 5)):
-            hidden(1, chunk, b)
-        plus = held("vp", 1)
-        minus = held("vg", 1)
-        y = held("vy", 1)
-        for cols in halves:
-            nc.vector.tensor_tensor(minus[:, cols], mbank[:, cols], rest[:, cols], ALU.mult)
-        nc.vector.tensor_tensor(plus[:], ebank[:], gate[:], ALU.mult)
-        if SPLIT4 > 64:
-            cast_w4(False, 64, SPLIT4)
-        quant_h(1, 1)
-        for cols in halves:
-            nc.vector.tensor_tensor(y[:, cols], plus[:, cols], minus[:, cols], ALU.subtract)
-        quant_h(1, 2)
-        first = [weigh(nc.vector, units[0][i : i + 1], y[:, halves[i]]) for i in range(2)]
-        quant_w4(1)
-
+        for e, s0, n in groups:
+            if e == 0:
+                quant_h(0, s0)
         def atom(u, i):
             return units[u][i : i + 1]
 
@@ -394,20 +437,77 @@ def tile_list_candidate_expert_blend_kernel(
         def begin(u):
             if u not in gates:
                 gates[u] = turned_gate(units[u])
-            copies[u] = turned_terms(units[u], u < last, u in ON_VECTOR)
+            copies[u] = turned_terms(units[u], u < JOINT, u in ON_VECTOR)
 
         def gate_unit(u):
             engine = nc.vector if u in ON_VECTOR else nc.gpsimd
-            terms[u] = gated_terms(units[u], gates[u][:], u < last, SLOTS[u % len(SLOTS)], copies[u], engine)
+            terms[u] = gated_terms(units[u], gates[u][:], u < JOINT, SLOTS[u % len(SLOTS)], copies[u], engine)
 
         def finish(u):
             summed = turned_sum(units[u], terms[u], SLOTS[u % len(SLOTS)])
             place(units[u], summed if u == last else weigh(nc.gpsimd, units[u], summed), u == last)
 
+        dbank, mbank = banks[3], banks[7]
+        halves = [slice(i * SPAN, (i + 1) * SPAN) for i in range(2)]
+        if JOINT0:
+            for nt, s, j, c in blocks(units[0]):
+                mx(dbank[:, c : c + P], w3_cols(nt), h_cols(0, s, j, j + P), c == 0, False)
+            for i, (nt, s) in enumerate(units[0]):
+                mx(dbank[:, halves[i]], w4_cols(nt), h_cols(1, s, 0, SPAN), False, i == 1)
+        for i, (nt, s) in enumerate(units[0]):
+            mx(mbank[:, halves[i]], w4_cols(nt), h_cols(1, s, 0, SPAN), True, True)
+        if not JOINT0:
+            for i, (nt, s) in enumerate(units[0]):
+                mx(dbank[:, halves[i]], w3_cols(nt), h_cols(0, s, 0, SPAN), True, True)
+        for chunk, b in zip(range(2, 8), HB):
+            hidden(1, chunk, b)
+            if chunk == 3 and EARLY1:
+                quant_h(1, 1)
+            if chunk == EARLY1:
+                begin(1)
+        gated = held("vg", 1)
+        y = held("vy", 1)
+        if EARLY11 and not EARLY1:
+            quant_h(1, 1)
+        if JOINT0:
+            for cols in halves:
+                nc.vector.tensor_tensor(gated[:, cols], dbank[:, cols], gate[:, cols], ALU.mult)
+            other = mbank
+        else:
+            other = held("vp", 1)
+            for cols in halves:
+                nc.vector.tensor_tensor(other[:, cols], mbank[:, cols], rest[:, cols], ALU.mult)
+            nc.vector.tensor_tensor(gated[:], dbank[:], gate[:], ALU.mult)
+        if not EARLY11 and not EARLY1:
+            quant_h(1, 1)
+        for cols in halves:
+            nc.vector.tensor_tensor(y[:, cols], gated[:, cols], other[:, cols], ALU.subtract)
+        if SPLIT4 < P:
+            cast_w4(True, SPLIT4, P)
+        if SPLIT4 > 64:
+            cast_w4(False, 64, SPLIT4)
+        first = []
+
         def first_places(u):
+            quant_h(1, 2)
+            quant_w4(1)
             quant_h(1, 3)
+            first.append(weigh(nc.vector, atom(0, 0), y[:, halves[0]], keep.tile([P, SPAN], F32, name="pinned0", tag=PIN0, align_bytes=64)))
+            pinned = keep.tile([P, SPAN], F32, name="pinned", tag="h_bf13", align_bytes=64)
+            first.append(weigh(nc.vector, atom(0, 1), y[:, halves[1]], pinned))
             for i in range(2):
                 place(atom(0, i), first[i])
 
+        def by_halves(u):
+            slot = keep.tile([P, BANK], F32, name="summed", tag="halves", align_bytes=64)
+            for i in range(2):
+                bank = take()
+                for n, term in enumerate(terms[u]):
+                    for c in range(0, SPAN, P):
+                        src = term[:, i * SPAN + c : i * SPAN + c + P]
+                        nc.tensor.matmul(bank[:, c : c + P], src, identity[:], start=(n == 0 and c == 0), stop=(n == 1 and c == P), is_transpose=True)
+                nc.scalar.copy(slot[:, halves[i]], bank[:, :SPAN])
+                place(atom(u, i), weigh(nc.gpsimd, atom(u, i), slot[:, halves[i]]))
+
         for step in STEPS.split():
-            {"b": begin, "g": gate_unit, "f": finish, "p": first_places}[step[0]](int(step[1]))
+            {"b": begin, "g": gate_unit, "f": finish, "p": first_places, "h": by_halves, "a": lambda u: early.setdefault(units[u], plain_terms(units[u]))}[step[0]](int(step[1]))

@@ -31,6 +31,8 @@ SPLIT4 = 96
 JOINT = 6
 JOINT0 = 1
 PE_DIFF = 1
+MERGE = 1
+SPLIT11 = 128
 PIN0 = "pin0"
 HTAG = {(0, 0): "w1_bf11"}
 EARLY1 = 0
@@ -79,7 +81,8 @@ def tile_list_candidate_expert_blend_kernel(
         w3_w = keep.tile([P, 2 * N // 4], I32, name="w3_w", align_bytes=64)
         gain = keep.tile([P, S], F32, name="gain", align_bytes=64)
         pieces = [(e, a) for e in range(2) for a in range(PASSES)]
-        w1_raw = {ea: keep.tile([P, PACK, R], F32, name="w1_raw%d%d" % ea, align_bytes=64) for ea in pieces}
+        parts = [(0, 0, 0, R), (0, 1, 0, R), (1, 0, 0, R)] + ([(1, 1, 0, R // 2), (1, 1, R // 2, R)] if "d" in LOADS else [(1, 1, 0, R)])
+        w1_raw = {part[:3]: keep.tile([P, PACK, part[3] - part[2]], F32, name="w1_raw%d%d_%d" % part[:3], align_bytes=64) for part in parts}
         w1_bf = {ea: keep.tile([P, PACK, P, PACK], BF16, name="w1_bf%d%d" % ea, align_bytes=64) for ea in pieces}
         w1_c = {ea: keep.tile([P, R], U32, name="w1_c%d%d" % ea, align_bytes=64) for ea in pieces}
         w1_s = {ea: keep.tile([P, R], U8, name="w1_s%d%d" % ea, align_bytes=64) for ea in pieces}
@@ -116,7 +119,7 @@ def tile_list_candidate_expert_blend_kernel(
 
         def load_w1(e, a, c0=0, c1=R):
             rows = w1[a * K_PASS : (a + 1) * K_PASS, e * R + c0 : e * R + c1]
-            nc.sync.dma_start(out=w1_raw[e, a][:, :, c0:c1], in_=rows.rearrange("(p j) c -> p j c", j=PACK))
+            nc.sync.dma_start(out=w1_raw[e, a, c0][:], in_=rows.rearrange("(p j) c -> p j c", j=PACK))
 
         def load_wg(u):
             cols = slice(u * (N // 2), (u + 1) * (N // 2))
@@ -144,6 +147,7 @@ def tile_list_candidate_expert_blend_kernel(
         load_words(tab_w[1][:], tab_words[1])
         loads = {
             "s": load_wg_scales,
+            "D": lambda: load_w1(1, 1),
             "g": lambda: load_wg(0),
             "G": lambda: load_wg(1),
             "a": lambda: load_w1(0, 0),
@@ -172,9 +176,10 @@ def tile_list_candidate_expert_blend_kernel(
             nc.vector.tensor_copy(out=v_s[:, j0:j1], in_=tab_s[:].bitcast(U8).indirect(entries(idx, j0, j1)))
 
         def cast_w1(e, a, m0, m1, copy):
-            src = w1_raw[e, a][:].rearrange("p j (m t) -> p m j t", t=PACK)
+            c0 = max(part[2] for part in parts if part[:2] == (e, a) and part[2] <= m0 * PACK)
+            src = w1_raw[e, a, c0][:].rearrange("p j (m t) -> p m j t", t=PACK)
             dst = w1_bf[e, a][:].rearrange("p t m j -> p m j t")
-            copy(dst[:, m0:m1], src[:, m0:m1])
+            copy(dst[:, m0:m1], src[:, m0 - c0 // PACK : m1 - c0 // PACK])
 
         def quant_w1(e, a, t0=0, t1=PACK):
             nc.vector.quantize_mx(
@@ -406,8 +411,13 @@ def tile_list_candidate_expert_blend_kernel(
         if SPLIT10 < P:
             cast_w1(1, 0, SPLIT10, P, nc.scalar.copy)
         quant_w1(1, 0)
-        cast_w1(1, 1, 0, P // 2, nc.vector.tensor_copy)
-        cast_w1(1, 1, P // 2, P, nc.vector.tensor_copy)
+        if "d" in LOADS:
+            cast_w1(1, 1, 0, P // 2, nc.vector.tensor_copy)
+            cast_w1(1, 1, P // 2, P, nc.vector.tensor_copy)
+        else:
+            cast_w1(1, 1, 0, SPLIT11, nc.vector.tensor_copy)
+            if SPLIT11 < P:
+                cast_w1(1, 1, SPLIT11, P, nc.scalar.copy)
         quant_w1(1, 1, 0, 2)
         quant_w1(1, 1, 2, 4)
         for chunk in range(8):
@@ -465,12 +475,13 @@ def tile_list_candidate_expert_blend_kernel(
                 quant_h(1, 1)
             if chunk == EARLY1:
                 begin(1)
+        pieces0 = [slice(0, BANK)] if MERGE else halves
         gated = held("vg", 1)
         y = held("vy", 1)
         if EARLY11 and not EARLY1:
             quant_h(1, 1)
         if JOINT0:
-            for cols in halves:
+            for cols in pieces0:
                 nc.vector.tensor_tensor(gated[:, cols], dbank[:, cols], gate[:, cols], ALU.mult)
             other = mbank
         else:
@@ -480,7 +491,7 @@ def tile_list_candidate_expert_blend_kernel(
             nc.vector.tensor_tensor(gated[:], dbank[:], gate[:], ALU.mult)
         if not EARLY11 and not EARLY1:
             quant_h(1, 1)
-        for cols in halves:
+        for cols in pieces0:
             nc.vector.tensor_tensor(y[:, cols], gated[:, cols], other[:, cols], ALU.subtract)
         if SPLIT4 < P:
             cast_w4(True, SPLIT4, P)

@@ -27,10 +27,15 @@ BANK = 512
 SPAN = 256
 SPANS = S // SPAN
 SPLIT10 = 128
-SPLIT4 = 96
+SPLIT4 = 128
 JOINT = 6
 JOINT0 = 1
 PE_DIFF = 1
+VRELU0 = (1,)
+H01 = (4, 5)
+DM = (3, 7)
+W0EARLY = 0
+PIN1 = "h_bf13"
 MERGE = 1
 SPLIT11 = 128
 PIN0 = "pin0"
@@ -228,7 +233,7 @@ def tile_list_candidate_expert_blend_kernel(
         def hidden(e, chunk, b):
             for a in range(PASSES):
                 hidden_pass(e, chunk, b, a)
-            relu(e, chunk, b, e == 1 and chunk in VRELU)
+            relu(e, chunk, b, chunk in (VRELU if e else VRELU0))
 
         def quant_h(e, s):
             nc.vector.quantize_mx(out=h_c[e, s][:].bitcast(FP8X4), scales=h_s[e, s][:], in_=h_bf[e, s][:].rearrange("p n t -> p (n t)"))
@@ -274,16 +279,17 @@ def tile_list_candidate_expert_blend_kernel(
 
         def plain_gate(unit):
             bank = take()
-            for i, (nt, s) in enumerate(unit):
-                for a in range(PASSES):
-                    mx(bank[:, i * SPAN : (i + 1) * SPAN], wg_cols(nt, a), v_cols(a, s * SPAN, (s + 1) * SPAN), a == 0, a == PASSES - 1)
+            for a in range(PASSES):
+                for i, (nt, s) in enumerate(unit):
+                    mx(bank[:, i * SPAN : (i + 1) * SPAN], wg_cols(nt, a), v_cols(a, s * SPAN, (s + 1) * SPAN), a + i == 0, a + i == PASSES)
             return sigmoid(bank), (None if JOINT0 else sigmoid(bank, -1.0))
 
         def turned_gate(unit):
             bank = take()
-            for nt, s, j, c in blocks(unit):
-                for a in range(PASSES):
-                    mx(bank[:, c : c + P], v_cols(a, s * SPAN + j, s * SPAN + j + P), wg_cols(nt, a), a == 0, a == PASSES - 1)
+            for a in range(PASSES):
+                for nt, s, j, c in blocks(unit):
+                    opens, closes = a == 0 and c == 0, a == PASSES - 1 and c == BANK - P
+                    mx(bank[:, c : c + P], v_cols(a, s * SPAN + j, s * SPAN + j + P), wg_cols(nt, a), opens, closes)
             return sigmoid(bank)
 
         def factors(atoms):
@@ -423,13 +429,13 @@ def tile_list_candidate_expert_blend_kernel(
         for chunk in range(8):
             hidden(0, chunk, EB[chunk])
         for chunk in range(2):
-            hidden_pass(1, chunk, 4 + chunk, 0)
+            hidden_pass(1, chunk, H01[chunk], 0)
         if not EARLY_GATES:
             gate, rest = plain_gate(units[0])
             gates = {u: turned_gate(units[u]) for u in GATED}
         for chunk in range(2):
-            hidden_pass(1, chunk, 4 + chunk, 1)
-            relu(1, chunk, 4 + chunk, chunk in VRELU)
+            hidden_pass(1, chunk, H01[chunk], 1)
+            relu(1, chunk, H01[chunk], chunk in VRELU)
         cast_w4(False, 0, SPLIT40)
         if SPLIT40 < 64:
             cast_w4(True, SPLIT40, 64)
@@ -457,7 +463,7 @@ def tile_list_candidate_expert_blend_kernel(
             summed = turned_sum(units[u], terms[u], SLOTS[u % len(SLOTS)])
             place(units[u], summed if u == last else weigh(nc.gpsimd, units[u], summed), u == last)
 
-        dbank, mbank = banks[3], banks[7]
+        dbank, mbank = banks[DM[0]], banks[DM[1]]
         halves = [slice(i * SPAN, (i + 1) * SPAN) for i in range(2)]
         if JOINT0:
             for nt, s, j, c in blocks(units[0]):
@@ -502,9 +508,12 @@ def tile_list_candidate_expert_blend_kernel(
         def first_places(u):
             quant_h(1, 2)
             quant_w4(1)
-            quant_h(1, 3)
+            if not W0EARLY:
+                quant_h(1, 3)
             first.append(weigh(nc.vector, atom(0, 0), y[:, halves[0]], keep.tile([P, SPAN], F32, name="pinned0", tag=PIN0, align_bytes=64)))
-            pinned = keep.tile([P, SPAN], F32, name="pinned", tag="h_bf13", align_bytes=64)
+            if W0EARLY:
+                quant_h(1, 3)
+            pinned = keep.tile([P, SPAN], F32, name="pinned", tag=PIN1, align_bytes=64)
             first.append(weigh(nc.vector, atom(0, 1), y[:, halves[1]], pinned))
             for i in range(2):
                 place(atom(0, i), first[i])

@@ -60,7 +60,7 @@ WEIGHTED = 6
 W4B_ON_SCALAR = True
 MODES = ("V", "A", "T", "T", "T", "T", "T", "X")
 ON_VECTOR = (1,)
-SLOTS = ("w4_bf", "h_bf11")
+SLOTS = ("w4_raw0", "h_bf11")
 STEPS = "b1 g1 p0 b2 g2 f1 b3 g3 f2 b4 g4 a6 f3 b5 g5 b6 f4 a7 g6 f5 b7 g7 f6 f7"
 TENANTS = (0, 1, 2, 3)
 RING = (2, 6, 5, 3, 7, 0, 1, 4)
@@ -483,7 +483,7 @@ def tile_list_candidate_expert_blend_kernel(
                 begin(1)
         pieces0 = [slice(0, BANK)] if MERGE else halves
         gated = held("vg", 1)
-        y = held("vy", 1)
+        y = keep.tile([P, BANK], F32, name="vy", tag=SLOTS[0], align_bytes=64)
         if EARLY11 and not EARLY1:
             quant_h(1, 1)
         if JOINT0:

@@ -18,52 +18,20 @@ ACT = mybir.ActivationFunctionType
 ALU = mybir.AluOpType
 
 PACK = 4
-K_PASS = P * PACK
-PASSES = K // K_PASS
+PASSES = K // (P * PACK)
 QUADS = 4
 LIST_ROWS = 16
-H_CHUNK = 128
 BANK = 512
-SPAN = 256
+BANKS = 8
+CHUNK = BANK // PACK
+SPAN = BANK // 2
 SPANS = S // SPAN
-SPLIT10 = 128
-SPLIT4 = 128
-JOINT = 6
-JOINT0 = 1
-PE_DIFF = 1
-VRELU0 = (1,)
-H01 = (4, 5)
-DM = (3, 7)
-W0EARLY = 0
-PIN1 = "h_bf13"
-MERGE = 1
-SPLIT11 = 128
-PIN0 = "pin0"
-HTAG = {(0, 0): "w1_bf11"}
-EARLY1 = 0
-LASTSLOT = 0
-PAIRS = 1
-WIDE = 0
-EARLY11 = 0
-SPLIT40 = 64
-HB = (0, 1, 4, 5, 0, 1)
-VRELU = (1,)
-LOADS = 'sgabcdef3tFiwWG'
-EARLY_GATES = 1
-GATED = (1, 2, 3)
-SPLIT00 = 128
-EB = (4,5,6,7,0,1,2,3)
-SPLIT01 = 96
-GATES = 5
-HELD = 4
-WEIGHTED = 6
-W4B_ON_SCALAR = True
-MODES = ("V", "A", "T", "T", "T", "T", "T", "X")
-ON_VECTOR = (1,)
-SLOTS = ("w4_raw0", "h_bf11")
-STEPS = "b1 g1 p0 b2 g2 f1 b3 g3 f2 b4 g4 a6 f3 b5 g5 b6 f4 a7 g6 f5 b7 g7 f6 f7"
-TENANTS = (0, 1, 2, 3)
-RING = (2, 6, 5, 3, 7, 0, 1, 4)
+ROW_TILES = N // P
+SUMMED_UNITS = 6
+EARLY_GATES = 4
+VECTOR_SHARE = 96
+TERM_BUFS = 4
+WEIGHTED_BUFS = 6
 
 
 def tile_list_candidate_expert_blend_kernel(
@@ -72,59 +40,59 @@ def tile_list_candidate_expert_blend_kernel(
     nc = tc.nc
     with ExitStack() as ctx:
         keep = ctx.enter_context(tc.tile_pool(name="keep", bufs=1))
-        ring = ctx.enter_context(tc.tile_pool(name="ring", bufs=3))
+        ring = ctx.enter_context(tc.tile_pool(name="ring", bufs=1))
         psum = ctx.enter_context(tc.psum_pool(name="psum", bufs=1))
+
+        def kept(shape, dtype, name, tag=None):
+            return keep.tile(shape, dtype, name=name, tag=tag or name, align_bytes=64)
+
+        def held(name, bufs):
+            return ring.tile([P, BANK], F32, name=name, bufs=bufs)
 
         idx = keep.tile([P, S // LIST_ROWS], U16, name="idx")
         idx2 = keep.tile([P, S // LIST_ROWS], U16, name="idx2")
-        tab_w = [keep.tile([P, T], I32, name="tab_w%d" % a, align_bytes=64) for a in range(PASSES)]
-        tab_s = keep.tile([P, T // 4], I32, name="tab_s", align_bytes=64)
-        v_w = [keep.tile([P, S], U32, name="v_w%d" % a, align_bytes=64) for a in range(PASSES)]
-        v_s = keep.tile([P, S], U8, name="v_s", align_bytes=64)
-        wg_w = [keep.tile([P, PASSES, N // 2], I32, name="wg_w%d" % u, align_bytes=64) for u in range(2)]
-        w_s = keep.tile([P, 2, N // 4], I32, name="w_s", align_bytes=64)
-        w3_w = keep.tile([P, 2 * N // 4], I32, name="w3_w", align_bytes=64)
-        gain = keep.tile([P, S], F32, name="gain", align_bytes=64)
+        tab_w = [kept([P, T], I32, "tab_w%d" % a) for a in range(PASSES)]
+        tab_s = kept([P, T // 4], I32, "tab_s")
+        v_w = [kept([P, S], U32, "v_w%d" % a) for a in range(PASSES)]
+        v_s = kept([P, S], U8, "v_s")
+        wg_w = [kept([P, PASSES, N // 2], I32, "wg_w%d" % u) for u in range(2)]
+        w_s = kept([P, 2, N // 4], I32, "w_s")
+        w3_w = kept([P, 2 * N // 4], I32, "w3_w")
+        gain = kept([P, S], F32, "gain")
+        w1_parts = {(0, 0, 0): R, (0, 1, 0): R, (1, 0, 0): R, (1, 1, 0): R // 2, (1, 1, R // 2): R // 2}
+        w1_raw = {part: kept([P, PACK, cols], F32, "w1_raw%d%d_%d" % part) for part, cols in w1_parts.items()}
         pieces = [(e, a) for e in range(2) for a in range(PASSES)]
-        parts = [(0, 0, 0, R), (0, 1, 0, R), (1, 0, 0, R)] + ([(1, 1, 0, R // 2), (1, 1, R // 2, R)] if "d" in LOADS else [(1, 1, 0, R)])
-        w1_raw = {part[:3]: keep.tile([P, PACK, part[3] - part[2]], F32, name="w1_raw%d%d_%d" % part[:3], align_bytes=64) for part in parts}
-        w1_bf = {ea: keep.tile([P, PACK, P, PACK], BF16, name="w1_bf%d%d" % ea, align_bytes=64) for ea in pieces}
-        w1_c = {ea: keep.tile([P, R], U32, name="w1_c%d%d" % ea, align_bytes=64) for ea in pieces}
-        w1_s = {ea: keep.tile([P, R], U8, name="w1_s%d%d" % ea, align_bytes=64) for ea in pieces}
-        w4_raw = [keep.tile([P, PACK, N // 2], F32, name="w4_raw%d" % u, align_bytes=64) for u in range(2)]
-        w4_bf = keep.tile([P, N, PACK], BF16, name="w4_bf", align_bytes=64)
-        w4_c = keep.tile([P, N], U32, name="w4_c", align_bytes=64)
-        w4_s = keep.tile([P, N], U8, name="w4_s", align_bytes=64)
-        groups = ([(0, 0, 2), (0, 2, 2)] if PAIRS else [(0, s, 1) for s in range(SPANS)]) + [(1, s, 1) for s in range(SPANS)]
-        h_bf, h_c, h_s = {}, {}, {}
-        for e, s0, n in groups:
-            h_bf[e, s0] = keep.tile([P, n * SPAN, PACK], BF16, name="h_bf%d%d" % (e, s0), align_bytes=64)
-            h_c[e, s0] = keep.tile([P, n * SPAN], U32, name="h_c%d%d" % (e, s0), tag=HTAG.get((e, s0), "h_c%d%d" % (e, s0)), align_bytes=64)
-            h_s[e, s0] = keep.tile([P, n * SPAN], U8, name="h_s%d%d" % (e, s0), align_bytes=64)
-
-        def group_of(e, j):
-            s0 = max(g[1] for g in groups if g[0] == e and g[1] * SPAN <= j)
-            return (e, s0), j - s0 * SPAN
-
-        banks = [psum.tile([P, 512], F32, name="bank%d" % b) for b in range(8)]
-        cache = [keep.tile([P, T2], F32, name="cache%d" % nt, align_bytes=64) for nt in range(N // P)]
-        warm = keep.tile([P, 2], F32, name="warm", align_bytes=64)
+        w1_bf = {ea: kept([P, PACK, P, PACK], BF16, "w1_bf%d%d" % ea) for ea in pieces}
+        w1_c = {ea: kept([P, R], U32, "w1_c%d%d" % ea) for ea in pieces}
+        w1_s = {ea: kept([P, R], U8, "w1_s%d%d" % ea) for ea in pieces}
+        w4_raw = [kept([P, PACK, N // 2], F32, "w4_raw%d" % u) for u in range(2)]
+        w4_bf = kept([P, N, PACK], BF16, "w4_bf")
+        w4_c = kept([P, N], U32, "w4_c")
+        w4_s = kept([P, N], U8, "w4_s")
+        h_spans = {(0, 0): 2, (0, 2): 2, (1, 0): 1, (1, 1): 1, (1, 2): 1, (1, 3): 1}
+        h_bf = {key: kept([P, n * SPAN, PACK], BF16, "h_bf%d%d" % key) for key, n in h_spans.items()}
+        h_c = {key: kept([P, n * SPAN], U32, "h_c%d%d" % key, "w1_bf11" if key == (0, 0) else None) for key, n in h_spans.items()}
+        h_s = {key: kept([P, n * SPAN], U8, "h_s%d%d" % key) for key, n in h_spans.items()}
+        banks = [psum.tile([P, BANK], F32, name="bank%d" % b) for b in range(BANKS)]
+        cache = [kept([P, T2], F32, "cache%d" % nt) for nt in range(ROW_TILES)]
+        identity = kept([P, P], F32, "identity")
+        warm = kept([P, 2], F32, "warm")
 
         nc.gpsimd.memset(tab_s[:], 0)
         nc.gpsimd.memset(w_s[:], 0)
-        identity = keep.tile([P, P], F32, name="identity", align_bytes=64)
         make_identity(nc, identity[:])
-        for nt in range(N // P):
+        for nt in range(ROW_TILES):
             nc.gpsimd.memset(cache[nt][:], 0.0)
         nc.vector.memset(warm[:, 0:1], 0.0)
         nc.scalar.activation(warm[:, 1:2], warm[:, 0:1], ACT.Sigmoid)
 
-        def load_words(dst, src):
-            nc.sync.dma_start(out=dst, in_=src.rearrange("p t i -> p (t i)").bitcast(I32))
+        def load_table(a):
+            nc.sync.dma_start(out=tab_w[a][:], in_=tab_words[a].rearrange("p t i -> p (t i)").bitcast(I32))
 
-        def load_w1(e, a, c0=0, c1=R):
-            rows = w1[a * K_PASS : (a + 1) * K_PASS, e * R + c0 : e * R + c1]
-            nc.sync.dma_start(out=w1_raw[e, a, c0][:], in_=rows.rearrange("(p j) c -> p j c", j=PACK))
+        def load_planes(dst, scales):
+            rows = 4 * scales.shape[0]
+            for q in range(QUADS):
+                nc.sync.dma_start(out=dst[32 * q : 32 * q + rows], in_=scales[:, 4 * q : 4 * q + 4, :].bitcast(I32))
 
         def load_wg(u):
             cols = slice(u * (N // 2), (u + 1) * (N // 2))
@@ -134,57 +102,43 @@ def tile_list_candidate_expert_blend_kernel(
             cols = w4[:, u * (N // 2) : (u + 1) * (N // 2)]
             nc.sync.dma_start(out=w4_raw[u][:], in_=cols.rearrange("(p j) c -> p j c", j=PACK))
 
-        def load_gain(j0, j1):
-            nc.sync.dma_start(out=gain[:, j0:j1], in_=wgo[:, j0:j1])
-
-        def load_wg_scales():
-            for q in range(QUADS):
-                nc.sync.dma_start(out=w_s[32 * q : 32 * q + 8, 0, :], in_=wg_scales[:, 4 * q : 4 * q + 4, :].bitcast(I32))
-
-        def load_w3_scales():
-            for q in range(QUADS):
-                nc.sync.dma_start(out=w_s[32 * q : 32 * q + 4, 1, :], in_=w3_scales[0, 4 * q : 4 * q + 4, :].bitcast(I32))
-
-        load_words(tab_w[0][:], tab_words[0])
+        load_table(0)
         nc.sync.dma_start(idx[:], offs)
-        for q in range(QUADS):
-            nc.sync.dma_start(out=tab_s[32 * q : 32 * q + 8, :], in_=tab_scales[:, 4 * q : 4 * q + 4, :].bitcast(I32))
-        load_words(tab_w[1][:], tab_words[1])
-        loads = {
-            "s": load_wg_scales,
-            "D": lambda: load_w1(1, 1),
-            "g": lambda: load_wg(0),
-            "G": lambda: load_wg(1),
-            "a": lambda: load_w1(0, 0),
-            "b": lambda: load_w1(0, 1),
-            "c": lambda: load_w1(1, 0),
-            "d": lambda: load_w1(1, 1, 0, R // 2),
-            "e": lambda: load_w1(1, 1, R // 2, R),
-            "f": lambda: load_w4(0),
-            "F": lambda: load_w4(1),
-            "3": lambda: nc.sync.dma_start(out=w3_w[:], in_=w3_words[0].bitcast(I32)),
-            "t": load_w3_scales,
-            "i": lambda: nc.sync.dma_start(idx2[:], offs2),
-            "w": lambda: load_gain(0, 2 * SPAN),
-            "W": lambda: load_gain(2 * SPAN, S),
-        }
-        for key in LOADS:
-            loads[key]()
+        load_planes(tab_s[:], tab_scales)
+        load_table(1)
+        load_planes(w_s[:, 0, :], wg_scales)
+        load_wg(0)
+        for (e, a, c0), cols in w1_parts.items():
+            rows = w1[a * P * PACK : (a + 1) * P * PACK, e * R + c0 : e * R + c0 + cols]
+            nc.sync.dma_start(out=w1_raw[e, a, c0][:], in_=rows.rearrange("(p j) c -> p j c", j=PACK))
+        load_w4(0)
+        nc.sync.dma_start(out=w3_w[:], in_=w3_words[0].bitcast(I32))
+        load_planes(w_s[:, 1, :], w3_scales)
+        load_w4(1)
+        nc.sync.dma_start(idx2[:], offs2)
+        for half in range(2):
+            cols = slice(half * (S // 2), (half + 1) * (S // 2))
+            nc.sync.dma_start(out=gain[:, cols], in_=wgo[:, cols])
+        load_wg(1)
+
+        taken = []
+
+        def take():
+            taken.append(banks[len(taken) % BANKS])
+            return taken[-1]
 
         def entries(lst, j0, j1):
             return lst[:, j0 // LIST_ROWS : j1 // LIST_ROWS]
 
-        def gather_words(a, j0, j1):
-            nc.vector.tensor_copy(out=v_w[a][:, j0:j1], in_=tab_w[a][:].bitcast(U32).indirect(entries(idx, j0, j1)))
+        def gather(dst, window):
+            for j0 in range(0, S, S // 2):
+                j1 = j0 + S // 2
+                nc.vector.tensor_copy(out=dst[:, j0:j1], in_=window.indirect(entries(idx, j0, j1)))
 
-        def gather_scales(j0, j1):
-            nc.vector.tensor_copy(out=v_s[:, j0:j1], in_=tab_s[:].bitcast(U8).indirect(entries(idx, j0, j1)))
-
-        def cast_w1(e, a, m0, m1, copy):
-            c0 = max(part[2] for part in parts if part[:2] == (e, a) and part[2] <= m0 * PACK)
-            src = w1_raw[e, a, c0][:].rearrange("p j (m t) -> p m j t", t=PACK)
-            dst = w1_bf[e, a][:].rearrange("p t m j -> p m j t")
-            copy(dst[:, m0:m1], src[:, m0 - c0 // PACK : m1 - c0 // PACK])
+        def cast_w1(e, a, c0, copy, m0=0, m1=None):
+            src = w1_raw[e, a, c0][:].rearrange("p j (m t) -> p m j t", t=PACK)[:, m0:m1]
+            dst = w1_bf[e, a][:].rearrange("p t m j -> p m j t")[:, c0 // PACK + m0 : c0 // PACK + m0 + src.shape[1]]
+            copy(dst, src)
 
         def quant_w1(e, a, t0=0, t1=PACK):
             nc.vector.quantize_mx(
@@ -193,13 +147,9 @@ def tile_list_candidate_expert_blend_kernel(
                 in_=w1_bf[e, a][:, t0:t1].rearrange("p t m j -> p (t m j)"),
             )
 
-        def cast_w4(on_scalar, c0, c1):
-            dst = w4_bf[:].rearrange("p (c i) j -> p c j i", i=4)[:, c0:c1]
-            src = w4_raw[c0 // 64][:].rearrange("p j (c i) -> p c j i", i=4)[:, c0 % 64 : (c1 - 1) % 64 + 1]
-            if on_scalar:
-                nc.scalar.activation(dst, src, ACT.Copy, scale=-1.0)
-            else:
-                nc.vector.tensor_scalar_mul(dst, src, -1.0)
+        def cast_w4(u):
+            dst = w4_bf[:, u * (N // 2) : (u + 1) * (N // 2), :].rearrange("p (c i) j -> p c j i", i=4)
+            nc.vector.tensor_scalar_mul(dst, w4_raw[u][:].rearrange("p j (c i) -> p c j i", i=4), -1.0)
 
         def quant_w4(u):
             cols = slice(u * (N // 2), (u + 1) * (N // 2))
@@ -207,327 +157,223 @@ def tile_list_candidate_expert_blend_kernel(
                 out=w4_c[:, cols].bitcast(FP8X4), scales=w4_s[:, cols], in_=w4_bf[:, cols, :].rearrange("p c j -> p (c j)")
             )
 
-        def hidden_pass(e, chunk, b, a):
-            cols = slice(chunk * H_CHUNK, (chunk + 1) * H_CHUNK)
-            bank = banks[b][:].rearrange("p (t n) -> p t n", t=PACK)
-            for t in range(PACK):
-                nc.tensor.matmul_mx(
-                    out=bank[:, t, :],
-                    lhsT=w1_c[e, a][:, t * P : (t + 1) * P].bitcast(FP8X4),
-                    lhsT_scale=w1_s[e, a][:, t * P : (t + 1) * P],
-                    rhs=v_w[a][:, cols].bitcast(FP8X4),
-                    rhs_scale=v_s[4 * a : P, cols],
-                    start=(a == 0 and t == 0),
-                    stop=(a == PASSES - 1 and t == PACK - 1),
-                )
-
-        def relu(e, chunk, b, on_vector=False):
-            key, j = group_of(e, chunk * H_CHUNK)
-            dst = h_bf[key][:, j : j + H_CHUNK, :]
-            src = banks[b][:].rearrange("p (t n) -> p n t", t=PACK)
-            if on_vector:
-                nc.vector.tensor_scalar_max(dst, src, 0.0)
-            else:
-                nc.scalar.activation(dst, src, ACT.Relu)
-
-        def hidden(e, chunk, b):
-            for a in range(PASSES):
-                hidden_pass(e, chunk, b, a)
-            relu(e, chunk, b, chunk in (VRELU if e else VRELU0))
-
         def quant_h(e, s):
-            nc.vector.quantize_mx(out=h_c[e, s][:].bitcast(FP8X4), scales=h_s[e, s][:], in_=h_bf[e, s][:].rearrange("p n t -> p (n t)"))
+            nc.vector.quantize_mx(
+                out=h_c[e, s][:].bitcast(FP8X4), scales=h_s[e, s][:], in_=h_bf[e, s][:].rearrange("p n t -> p (n t)")
+            )
+
+        def h_place(e, j):
+            s0 = max(s for expert, s in h_spans if expert == e and s * SPAN <= j)
+            return (e, s0), j - s0 * SPAN
+
+        def w1_cols(e, a, t):
+            return w1_c[e, a][:, t * P : (t + 1) * P].bitcast(FP8X4), w1_s[e, a][:, t * P : (t + 1) * P]
 
         def w3_cols(nt):
-            return w3_w[:].bitcast(U8)[:, 2 * nt * P : 2 * (nt + 1) * P].bitcast(FP4X4), w_s[:, 1, :].bitcast(U8)[:, nt * P : (nt + 1) * P]
+            codes = w3_w[:].bitcast(U8)[:, 2 * nt * P : 2 * (nt + 1) * P].bitcast(FP4X4)
+            return codes, w_s[:, 1, :].bitcast(U8)[:, nt * P : (nt + 1) * P]
 
         def w4_cols(nt):
             return w4_c[:, nt * P : (nt + 1) * P].bitcast(FP8X4), w4_s[:, nt * P : (nt + 1) * P]
 
         def wg_cols(nt, a):
-            own = slice(nt % 2 * P, (nt % 2 + 1) * P)
-            return wg_w[nt // 2][:, a, own].bitcast(FP8X4), w_s[4 * a : P, 0, :].bitcast(U8)[:, nt * P : (nt + 1) * P]
+            codes = wg_w[nt // 2][:, a, nt % 2 * P : (nt % 2 + 1) * P].bitcast(FP8X4)
+            return codes, w_s[4 * a : P, 0, :].bitcast(U8)[:, nt * P : (nt + 1) * P]
 
-        def h_cols(e, s, j0, j1):
-            key, j = group_of(e, s * SPAN + j0)
-            return h_c[key][:, j : j + j1 - j0].bitcast(FP8X4), h_s[key][:, j : j + j1 - j0]
+        def h_cols(e, j0, width):
+            key, j = h_place(e, j0)
+            return h_c[key][:, j : j + width].bitcast(FP8X4), h_s[key][:, j : j + width]
 
-        def v_cols(a, j0, j1):
-            return v_w[a][:, j0:j1].bitcast(FP8X4), v_s[4 * a : P, j0:j1]
+        def v_cols(a, j0, width):
+            return v_w[a][:, j0 : j0 + width].bitcast(FP8X4), v_s[4 * a : P, j0 : j0 + width]
 
         def mx(dst, stationary, moving, start, stop):
             nc.tensor.matmul_mx(
                 out=dst, lhsT=stationary[0], lhsT_scale=stationary[1], rhs=moving[0], rhs_scale=moving[1], start=start, stop=stop
             )
 
-        turn = [0]
+        def hidden_pass(e, chunk, bank, a):
+            for t in range(PACK):
+                opens, closes = a == 0 and t == 0, a == PASSES - 1 and t == PACK - 1
+                mx(bank[:, t * CHUNK : (t + 1) * CHUNK], w1_cols(e, a, t), v_cols(a, chunk * CHUNK, CHUNK), opens, closes)
 
-        def take():
-            turn[0] += 1
-            return banks[TENANTS[turn[0] - 1] if turn[0] <= len(TENANTS) else RING[(turn[0] - 1 - len(TENANTS)) % len(RING)]]
+        def relu_views(e, chunk, bank):
+            key, j = h_place(e, chunk * CHUNK)
+            return h_bf[key][:, j : j + CHUNK, :], bank[:].rearrange("p (t n) -> p n t", t=PACK)
 
-        def held(name, bufs=HELD):
-            return ring.tile([P, BANK], F32, name=name, bufs=bufs)
+        def hidden(e, chunk):
+            bank = take()
+            for a in range(PASSES):
+                hidden_pass(e, chunk, bank, a)
+            nc.scalar.activation(*relu_views(e, chunk, bank), ACT.Relu)
 
-        def sigmoid(bank, sign=1.0):
-            gate = held("gate", GATES)
-            nc.scalar.activation(gate[:], bank[:], ACT.Sigmoid, scale=sign)
+        units = [((0, s), (1, s)) for s in range(SPANS)] + [((nt, s), (nt, s + 1)) for s in (0, 2) for nt in (2, 3)]
+        last = len(units) - 1
+
+        def halves(u):
+            return [(nt, s * SPAN, slice(i * SPAN, (i + 1) * SPAN)) for i, (nt, s) in enumerate(units[u])]
+
+        def blocks(u):
+            return [(nt, j + c, slice(cols.start + c, cols.start + c + P)) for nt, j, cols in halves(u) for c in range(0, SPAN, P)]
+
+        def gate_of(u):
+            bank = take()
+            parts = blocks(u) if u else halves(u)
+            for a in range(PASSES):
+                for i, (nt, j, cols) in enumerate(parts):
+                    weights, values = wg_cols(nt, a), v_cols(a, j, BANK // len(parts))
+                    opens, closes = a == 0 and i == 0, a == PASSES - 1 and i == len(parts) - 1
+                    mx(bank[:, cols], *((values, weights) if u else (weights, values)), opens, closes)
+            gate = held("gate", EARLY_GATES + 1)
+            nc.scalar.activation(gate[:], bank[:], ACT.Sigmoid)
             return gate
-
-        def blocks(atoms):
-            return [(nt, s, j, i * SPAN + j) for i, (nt, s) in enumerate(atoms) for j in range(0, SPAN, P)]
-
-        def plain_gate(unit):
-            bank = take()
-            for a in range(PASSES):
-                for i, (nt, s) in enumerate(unit):
-                    mx(bank[:, i * SPAN : (i + 1) * SPAN], wg_cols(nt, a), v_cols(a, s * SPAN, (s + 1) * SPAN), a + i == 0, a + i == PASSES)
-            return sigmoid(bank), (None if JOINT0 else sigmoid(bank, -1.0))
-
-        def turned_gate(unit):
-            bank = take()
-            for a in range(PASSES):
-                for nt, s, j, c in blocks(unit):
-                    opens, closes = a == 0 and c == 0, a == PASSES - 1 and c == BANK - P
-                    mx(bank[:, c : c + P], v_cols(a, s * SPAN + j, s * SPAN + j + P), wg_cols(nt, a), opens, closes)
-            return sigmoid(bank)
-
-        def factors(atoms):
-            s0, s1 = atoms[0][1], atoms[-1][1]
-            if len(atoms) == 2 and s0 == s1:
-                return gain[:, s0 * SPAN : (s0 + 1) * SPAN].unsqueeze(1).to_broadcast([P, 2, SPAN])
-            return gain[:, s0 * SPAN : (s1 + 1) * SPAN].rearrange("p (r j) -> p r j", j=SPAN)
-
-        def weigh(engine, atoms, y, weighted=None):
-            w = len(atoms) * SPAN
-            weighted = weighted or held("weighted", WEIGHTED)
-            engine.tensor_tensor(
-                weighted[:, :w].rearrange("p (r j) -> p r j", j=SPAN), y[:, :w].rearrange("p (r j) -> p r j", j=SPAN), factors(atoms), ALU.mult
-            )
-            return weighted
 
         def turn_over(tiles):
             bank = take()
-            for i, term in enumerate(tiles):
+            for i, tile in enumerate(tiles):
                 for c in range(0, BANK, P):
                     opens, closes = i == 0 and c == 0, i == len(tiles) - 1 and c == BANK - P
-                    nc.tensor.matmul(bank[:, c : c + P], term[:, c : c + P], identity[:], start=opens, stop=closes, is_transpose=True)
+                    nc.tensor.matmul(bank[:, c : c + P], tile[:, c : c + P], identity[:], start=opens, stop=closes, is_transpose=True)
             return bank
 
-        def plain_terms(atoms):
-            plain = []
-            for e, cols in enumerate((w3_cols, w4_cols)):
+        def copy_out(name, bufs, bank):
+            tile = held(name, bufs)
+            nc.scalar.copy(tile[:], bank[:])
+            return tile
+
+        def second_term(bank):
+            tile = held("second", TERM_BUFS)
+            nc.scalar.activation(tile[:], bank[:], ACT.Copy, scale=-1.0)
+            return tile
+
+        def turned_banks(u):
+            diff = take()
+            for nt, j, cols in blocks(u):
+                mx(diff[:, cols], h_cols(0, j, P), w3_cols(nt), True, False)
+                mx(diff[:, cols], h_cols(1, j, P), w4_cols(nt), False, True)
+            minus = take()
+            for nt, j, cols in blocks(u):
+                mx(minus[:, cols], h_cols(1, j, P), w4_cols(nt), True, True)
+            return diff, minus
+
+        def upright_terms(u):
+            terms = []
+            for e, weights in enumerate((w3_cols, w4_cols)):
                 bank = take()
-                for i, (nt, s) in enumerate(atoms):
-                    mx(bank[:, i * SPAN : (i + 1) * SPAN], cols(nt), h_cols(e, s, 0, SPAN), True, True)
-                plain.append(held("plain", 4))
-                nc.scalar.copy(plain[e][:], bank[:])
-            return plain
+                for nt, j, cols in halves(u):
+                    mx(bank[:, cols], weights(nt), h_cols(e, j, SPAN), True, True)
+                terms.append(copy_out("upright", 2 * (len(units) - SUMMED_UNITS), bank))
+            return terms
 
-        early = {}
+        buffer_tags = ("w4_raw0", "h_bf11")
 
-        def terms_by_transposes(atoms):
-            plain = early.get(atoms) or plain_terms(atoms)
-            diff = held("diff")
-            nc.scalar.copy(diff[:], turn_over(plain)[:])
-            second = held("second")
-            nc.scalar.activation(second[:], turn_over(plain[1:])[:], ACT.Copy, scale=-1.0)
-            return diff, second
+        def unit_buffer(u, name):
+            return kept([P, BANK], F32, name, buffer_tags[u % 2])
 
-        def turned_terms(atoms, joint, on_vector=False):
-            w = len(atoms) * SPAN
-            if not joint and PE_DIFF:
-                return terms_by_transposes(atoms)
-            bank = take()
-            for nt, s, j, c in blocks(atoms):
-                mx(bank[:, c : c + P], h_cols(0, s, j, j + P), w3_cols(nt), True, not joint)
-                if joint:
-                    mx(bank[:, c : c + P], h_cols(1, s, j, j + P), w4_cols(nt), False, True)
-            c1 = w % BANK
-            other = bank if c1 else take()
-            for nt, s, j, c in blocks(atoms):
-                mx(other[:, c1 + c : c1 + c + P], h_cols(1, s, j, j + P), w4_cols(nt), True, True)
-            diff = bank if on_vector else held("diff")
-            if not on_vector:
-                nc.scalar.copy(diff[:, :w], bank[:, :w])
-            second = held("second")
-            nc.scalar.activation(second[:, :w], other[:, c1 : c1 + w], ACT.Copy, scale=-1.0)
-            return diff, second
+        def gated_term(u, engine, diff):
+            gated = unit_buffer(u, "gated")
+            engine.tensor_tensor(gated[:], diff[:], gates[u][:], ALU.mult)
+            return gated
 
-        def gated_terms(atoms, gate, joint, slot, copies, engine):
-            w = len(atoms) * SPAN
-            diff, second = copies
-            if not joint and not PE_DIFF:
-                first, diff = diff, held("apart", 1)
-                nc.gpsimd.tensor_tensor(diff[:, :w], first[:, :w], second[:, :w], ALU.subtract)
-            gated = keep.tile([P, BANK], F32, name="gated", tag=slot, align_bytes=64)
-            engine.tensor_tensor(gated[:, :w], diff[:, :w], gate, ALU.mult)
-            return second, gated
+        def scatter(nt, j, width, values, fused=False):
+            window = cache[nt][:].indirect(entries(idx2, j, j + width))
+            if fused:
+                nc.vector.tensor_tensor(window, values, gain[:, j : j + width], ALU.mult)
+            else:
+                nc.vector.tensor_copy(out=window, in_=values)
+            if j + width == S:
+                nc.sync.dma_start(out=out[nt * P : (nt + 1) * P, :], in_=cache[nt][:])
 
-        def turned_sum(atoms, terms, slot):
-            w = len(atoms) * SPAN
-            bank = take()
-            for i, term in enumerate(terms):
-                for c in range(0, w, P):
-                    nc.tensor.matmul(
-                        bank[:, c : c + P], term[:, c : c + P], identity[:], start=(i == 0 and c == 0), stop=(i == 1 and c == w - P), is_transpose=True
-                    )
-            summed = keep.tile([P, BANK], F32, name="summed", tag=slot, align_bytes=64)
-            nc.scalar.copy(summed[:, :w], bank[:, :w])
-            return summed
+        def finish(u, terms):
+            bank = turn_over(terms)
+            summed = unit_buffer(u, "summed")
+            nc.scalar.copy(summed[:], bank[:])
+            (nt0, j0, cols0), (nt1, j1, cols1) = halves(u)
+            if u == last:
+                scatter(nt0, j0, BANK, summed[:], fused=True)
+                return
+            weighted = held("weighted", WEIGHTED_BUFS)
+            if nt0 == nt1:
+                nc.gpsimd.tensor_tensor(weighted[:], summed[:], gain[:, j0 : j0 + BANK], ALU.mult)
+                scatter(nt0, j0, BANK, weighted[:])
+            else:
+                both = gain[:, j0 : j0 + SPAN].unsqueeze(1).to_broadcast([P, 2, SPAN])
+                by_half = "p (r j) -> p r j"
+                nc.gpsimd.tensor_tensor(weighted[:].rearrange(by_half, r=2), summed[:].rearrange(by_half, r=2), both, ALU.mult)
+                scatter(nt0, j0, SPAN, weighted[:, cols0])
+                scatter(nt1, j1, SPAN, weighted[:, cols1])
 
-        done = {nt: 0 for nt in range(N // P)}
-
-        def place(atoms, weighted, fused=False):
-            runs = [atoms] if atoms[0][0] == atoms[-1][0] else [[atom] for atom in atoms]
-            c = 0
-            for run in runs:
-                nt, s = run[0]
-                w = len(run) * SPAN
-                window = cache[nt][:].indirect(entries(idx2, s * SPAN, s * SPAN + w))
-                if fused:
-                    nc.vector.tensor_tensor(window, weighted[:, c : c + w], gain[:, s * SPAN : s * SPAN + w], ALU.mult)
-                else:
-                    nc.vector.tensor_copy(out=window, in_=weighted[:, c : c + w])
-                c = c + w
-                done[nt] = done[nt] + w
-                if done[nt] == S:
-                    nc.sync.dma_start(out=out[nt * P : (nt + 1) * P, :], in_=cache[nt][:])
-
-        half = S // 2
-        gather_words(0, 0, half)
-        gather_words(0, half, S)
-        gather_scales(0, half)
-        gather_scales(half, S)
-        gather_words(1, 0, half)
-        gather_words(1, half, S)
-        units = [((0, s), (1, s)) for s in range(2)] + ([((nt, 2), (nt, 3)) for nt in (0, 1)] if WIDE else [((0, s), (1, s)) for s in (2, 3)])
-        units = units + [((nt, s), (nt, s + 1)) for s in (0, 2) for nt in (2, 3)]
-        if EARLY_GATES:
-            gate, rest = plain_gate(units[0])
-            gates = {u: turned_gate(units[u]) for u in GATED}
-        cast_w1(0, 0, 0, SPLIT00, nc.vector.tensor_copy)
-        if SPLIT00 < P:
-            cast_w1(0, 0, SPLIT00, P, nc.scalar.copy)
+        gather(v_w[0], tab_w[0][:].bitcast(U32))
+        gather(v_s, tab_s[:].bitcast(U8))
+        gather(v_w[1], tab_w[1][:].bitcast(U32))
+        gates = {u: gate_of(u) for u in range(EARLY_GATES)}
+        cast_w1(0, 0, 0, nc.vector.tensor_copy)
         quant_w1(0, 0)
-        cast_w1(0, 1, 0, SPLIT01, nc.vector.tensor_copy)
-        cast_w1(0, 1, SPLIT01, P, nc.scalar.copy)
+        cast_w1(0, 1, 0, nc.vector.tensor_copy)
         quant_w1(0, 1)
-        cast_w1(1, 0, 0, SPLIT10, nc.vector.tensor_copy)
-        if SPLIT10 < P:
-            cast_w1(1, 0, SPLIT10, P, nc.scalar.copy)
+        cast_w1(1, 0, 0, nc.vector.tensor_copy)
         quant_w1(1, 0)
-        if "d" in LOADS:
-            cast_w1(1, 1, 0, P // 2, nc.vector.tensor_copy)
-            cast_w1(1, 1, P // 2, P, nc.vector.tensor_copy)
-        else:
-            cast_w1(1, 1, 0, SPLIT11, nc.vector.tensor_copy)
-            if SPLIT11 < P:
-                cast_w1(1, 1, SPLIT11, P, nc.scalar.copy)
-        quant_w1(1, 1, 0, 2)
-        quant_w1(1, 1, 2, 4)
-        for chunk in range(8):
-            hidden(0, chunk, EB[chunk])
-        for chunk in range(2):
-            hidden_pass(1, chunk, H01[chunk], 0)
-        if not EARLY_GATES:
-            gate, rest = plain_gate(units[0])
-            gates = {u: turned_gate(units[u]) for u in GATED}
-        for chunk in range(2):
-            hidden_pass(1, chunk, H01[chunk], 1)
-            relu(1, chunk, H01[chunk], chunk in VRELU)
-        cast_w4(False, 0, SPLIT40)
-        if SPLIT40 < 64:
-            cast_w4(True, SPLIT40, 64)
+        cast_w1(1, 1, 0, nc.vector.tensor_copy)
+        cast_w1(1, 1, R // 2, nc.vector.tensor_copy)
+        quant_w1(1, 1, 0, PACK // 2)
+        quant_w1(1, 1, PACK // 2, PACK)
+        for chunk in range(S // CHUNK):
+            hidden(0, chunk)
+
+        first_banks = [take(), take()]
+        for a in range(PASSES):
+            for chunk, bank in enumerate(first_banks):
+                hidden_pass(1, chunk, bank, a)
+        nc.scalar.activation(*relu_views(1, 0, first_banks[0]), ACT.Relu)
+        nc.vector.tensor_scalar_max(*relu_views(1, 1, first_banks[1]), 0.0)
+        cast_w4(0)
         quant_h(1, 0)
         quant_w4(0)
-        for e, s0, n in groups:
-            if e == 0:
-                quant_h(0, s0)
-        def atom(u, i):
-            return units[u][i : i + 1]
+        quant_h(0, 0)
+        quant_h(0, 2)
+        hidden(1, 2)
+        hidden(1, 3)
 
-        last = len(units) - 1
-        copies, terms = {}, {}
+        diff0, minus0 = take(), take()
+        for i, (nt, j, cols) in enumerate(blocks(0)):
+            mx(diff0[:, cols], w3_cols(nt), h_cols(0, j, P), i == 0, False)
+        for i, (nt, j, cols) in enumerate(halves(0)):
+            mx(diff0[:, cols], w4_cols(nt), h_cols(1, j, SPAN), False, i == 1)
+        for nt, j, cols in halves(0):
+            mx(minus0[:, cols], w4_cols(nt), h_cols(1, j, SPAN), True, True)
+        for chunk in range(2 * SPAN // CHUNK, S // CHUNK):
+            hidden(1, chunk)
+        gated0 = held("gated0", 1)
+        nc.vector.tensor_tensor(gated0[:], diff0[:], gates[0][:], ALU.mult)
+        quant_h(1, 1)
+        blend0 = unit_buffer(0, "blend0")
+        nc.vector.tensor_tensor(blend0[:], gated0[:], minus0[:], ALU.subtract)
+        cast_w4(1)
 
-        def begin(u):
+        diff1, minus1 = turned_banks(1)
+        second1 = second_term(minus1)
+        terms = {1: (second1, gated_term(1, nc.vector, diff1))}
+        quant_h(1, 2)
+        quant_w4(1)
+        quant_h(1, 3)
+        weighted0 = [kept([P, SPAN], F32, "weighted0a"), kept([P, SPAN], F32, "weighted0b", "h_bf13")]
+        for tile, (nt, j, cols) in zip(weighted0, halves(0)):
+            nc.vector.tensor_tensor(tile[:], blend0[:, cols], gain[:, j : j + SPAN], ALU.mult)
+        for tile, (nt, j, cols) in zip(weighted0, halves(0)):
+            scatter(nt, j, SPAN, tile[:])
+
+        upright = {}
+        for u in range(2, len(units)):
             if u not in gates:
-                gates[u] = turned_gate(units[u])
-            copies[u] = turned_terms(units[u], u < JOINT, u in ON_VECTOR)
-
-        def gate_unit(u):
-            engine = nc.vector if u in ON_VECTOR else nc.gpsimd
-            terms[u] = gated_terms(units[u], gates[u][:], u < JOINT, SLOTS[u % len(SLOTS)], copies[u], engine)
-
-        def finish(u):
-            summed = turned_sum(units[u], terms[u], SLOTS[u % len(SLOTS)])
-            place(units[u], summed if u == last else weigh(nc.gpsimd, units[u], summed), u == last)
-
-        dbank, mbank = banks[DM[0]], banks[DM[1]]
-        halves = [slice(i * SPAN, (i + 1) * SPAN) for i in range(2)]
-        if JOINT0:
-            for nt, s, j, c in blocks(units[0]):
-                mx(dbank[:, c : c + P], w3_cols(nt), h_cols(0, s, j, j + P), c == 0, False)
-            for i, (nt, s) in enumerate(units[0]):
-                mx(dbank[:, halves[i]], w4_cols(nt), h_cols(1, s, 0, SPAN), False, i == 1)
-        for i, (nt, s) in enumerate(units[0]):
-            mx(mbank[:, halves[i]], w4_cols(nt), h_cols(1, s, 0, SPAN), True, True)
-        if not JOINT0:
-            for i, (nt, s) in enumerate(units[0]):
-                mx(dbank[:, halves[i]], w3_cols(nt), h_cols(0, s, 0, SPAN), True, True)
-        for chunk, b in zip(range(2, 8), HB):
-            hidden(1, chunk, b)
-            if chunk == 3 and EARLY1:
-                quant_h(1, 1)
-            if chunk == EARLY1:
-                begin(1)
-        pieces0 = [slice(0, BANK)] if MERGE else halves
-        gated = held("vg", 1)
-        y = keep.tile([P, BANK], F32, name="vy", tag=SLOTS[0], align_bytes=64)
-        if EARLY11 and not EARLY1:
-            quant_h(1, 1)
-        if JOINT0:
-            for cols in pieces0:
-                nc.vector.tensor_tensor(gated[:, cols], dbank[:, cols], gate[:, cols], ALU.mult)
-            other = mbank
-        else:
-            other = held("vp", 1)
-            for cols in halves:
-                nc.vector.tensor_tensor(other[:, cols], mbank[:, cols], rest[:, cols], ALU.mult)
-            nc.vector.tensor_tensor(gated[:], dbank[:], gate[:], ALU.mult)
-        if not EARLY11 and not EARLY1:
-            quant_h(1, 1)
-        for cols in pieces0:
-            nc.vector.tensor_tensor(y[:, cols], gated[:, cols], other[:, cols], ALU.subtract)
-        if SPLIT4 < P:
-            cast_w4(True, SPLIT4, P)
-        if SPLIT4 > 64:
-            cast_w4(False, 64, SPLIT4)
-        first = []
-
-        def first_places(u):
-            quant_h(1, 2)
-            quant_w4(1)
-            if not W0EARLY:
-                quant_h(1, 3)
-            first.append(weigh(nc.vector, atom(0, 0), y[:, halves[0]], keep.tile([P, SPAN], F32, name="pinned0", tag=PIN0, align_bytes=64)))
-            if W0EARLY:
-                quant_h(1, 3)
-            pinned = keep.tile([P, SPAN], F32, name="pinned", tag=PIN1, align_bytes=64)
-            first.append(weigh(nc.vector, atom(0, 1), y[:, halves[1]], pinned))
-            for i in range(2):
-                place(atom(0, i), first[i])
-
-        def by_halves(u):
-            slot = keep.tile([P, BANK], F32, name="summed", tag="halves", align_bytes=64)
-            for i in range(2):
-                bank = take()
-                for n, term in enumerate(terms[u]):
-                    for c in range(0, SPAN, P):
-                        src = term[:, i * SPAN + c : i * SPAN + c + P]
-                        nc.tensor.matmul(bank[:, c : c + P], src, identity[:], start=(n == 0 and c == 0), stop=(n == 1 and c == P), is_transpose=True)
-                nc.scalar.copy(slot[:, halves[i]], bank[:, :SPAN])
-                place(atom(u, i), weigh(nc.gpsimd, atom(u, i), slot[:, halves[i]]))
-
-        for step in STEPS.split():
-            {"b": begin, "g": gate_unit, "f": finish, "p": first_places, "h": by_halves, "a": lambda u: early.setdefault(units[u], plain_terms(units[u]))}[step[0]](int(step[1]))
+                gates[u] = gate_of(u)
+            if u < SUMMED_UNITS:
+                diff_bank, minus_bank = turned_banks(u)
+                diff = copy_out("diff", TERM_BUFS, diff_bank)
+            else:
+                diff = copy_out("diff", TERM_BUFS, turn_over(upright[u]))
+                minus_bank = turn_over(upright[u][1:])
+            terms[u] = (second_term(minus_bank), gated_term(u, nc.gpsimd, diff))
+            if SUMMED_UNITS <= u + 2 <= last:
+                upright[u + 2] = upright_terms(u + 2)
+            finish(u - 1, terms[u - 1])
+        finish(last, terms[last])

@@ -201,11 +201,14 @@ def tile_list_candidate_expert_blend_kernel(
             key, j = h_place(e, chunk * CHUNK)
             return h_bf[key][:, j : j + CHUNK, :], bank[:].rearrange("p (t n) -> p n t", t=PACK)
 
-        def hidden(e, chunk):
+        def hidden(e, chunk, on_vector=False):
             bank = take()
             for a in range(PASSES):
                 hidden_pass(e, chunk, bank, a)
-            nc.scalar.activation(*relu_views(e, chunk, bank), ACT.Relu)
+            if on_vector:
+                nc.vector.tensor_scalar_max(*relu_views(e, chunk, bank), 0.0)
+            else:
+                nc.scalar.activation(*relu_views(e, chunk, bank), ACT.Relu)
 
         units = [((0, s), (1, s)) for s in range(SPANS)] + [((nt, s), (nt, s + 1)) for s in (0, 2) for nt in (2, 3)]
         last = len(units) - 1
@@ -332,7 +335,7 @@ def tile_list_candidate_expert_blend_kernel(
         quant_h(0, 0)
         quant_h(0, 2)
         hidden(1, 2)
-        hidden(1, 3)
+        hidden(1, 3, on_vector=True)
 
         diff0, minus0 = take(), take()
         for i, (nt, j, cols) in enumerate(blocks(0)):

@@ -111,9 +111,10 @@ def tile_list_candidate_expert_blend_kernel(
         for (e, a, c0), cols in w1_parts.items():
             rows = w1[a * P * PACK : (a + 1) * P * PACK, e * R + c0 : e * R + c0 + cols]
             nc.sync.dma_start(out=w1_raw[e, a, c0][:], in_=rows.rearrange("(p j) c -> p j c", j=PACK))
+            if (e, a) == (0, 0):
+                load_planes(w_s[:, 1, :], w3_scales)
         load_w4(0)
         nc.sync.dma_start(out=w3_w[:], in_=w3_words[0].bitcast(I32))
-        load_planes(w_s[:, 1, :], w3_scales)
         load_w4(1)
         nc.sync.dma_start(idx2[:], offs2)
         for half in range(2):
@@ -192,9 +193,9 @@ def tile_list_candidate_expert_blend_kernel(
                 out=dst, lhsT=stationary[0], lhsT_scale=stationary[1], rhs=moving[0], rhs_scale=moving[1], start=start, stop=stop
             )
 
-        def hidden_pass(e, chunk, bank, a):
+        def hidden_pass(e, chunk, bank, a, order=(0, 1)):
             for t in range(PACK):
-                opens, closes = a == 0 and t == 0, a == PASSES - 1 and t == PACK - 1
+                opens, closes = a == order[0] and t == 0, a == order[-1] and t == PACK - 1
                 mx(bank[:, t * CHUNK : (t + 1) * CHUNK], w1_cols(e, a, t), v_cols(a, chunk * CHUNK, CHUNK), opens, closes)
 
         def relu_views(e, chunk, bank):
@@ -203,8 +204,9 @@ def tile_list_candidate_expert_blend_kernel(
 
         def hidden(e, chunk, on_vector=False):
             bank = take()
-            for a in range(PASSES):
-                hidden_pass(e, chunk, bank, a)
+            order = (1, 0) if e else (0, 1)
+            for a in order:
+                hidden_pass(e, chunk, bank, a, order)
             if on_vector:
                 nc.vector.tensor_scalar_max(*relu_views(e, chunk, bank), 0.0)
             else:
@@ -219,7 +221,7 @@ def tile_list_candidate_expert_blend_kernel(
         def blocks(u):
             return [(nt, j + c, slice(cols.start + c, cols.start + c + P)) for nt, j, cols in halves(u) for c in range(0, SPAN, P)]
 
-        def gate_of(u):
+        def gate_of(u, gate=None):
             bank = take()
             parts = blocks(u) if u else halves(u)
             for a in range(PASSES):
@@ -227,8 +229,8 @@ def tile_list_candidate_expert_blend_kernel(
                     weights, values = wg_cols(nt, a), v_cols(a, j, BANK // len(parts))
                     opens, closes = a == 0 and i == 0, a == PASSES - 1 and i == len(parts) - 1
                     mx(bank[:, cols], *((values, weights) if u else (weights, values)), opens, closes)
-            gate = held("gate", EARLY_GATES + 1)
-            nc.scalar.activation(gate[:], bank[:], ACT.Sigmoid)
+            gate = held("gate", 3)[:] if gate is None else gate
+            nc.scalar.activation(gate, bank[:], ACT.Sigmoid)
             return gate
 
         def turn_over(tiles):
@@ -275,7 +277,7 @@ def tile_list_candidate_expert_blend_kernel(
 
         def gated_term(u, engine, diff):
             gated = unit_buffer(u, "gated")
-            engine.tensor_tensor(gated[:], diff[:], gates[u][:], ALU.mult)
+            engine.tensor_tensor(gated[:], diff[:], gates[u], ALU.mult)
             return gated
 
         def scatter(nt, j, width, values, fused=False):
@@ -309,33 +311,45 @@ def tile_list_candidate_expert_blend_kernel(
         gather(v_w[0], tab_w[0][:].bitcast(U32))
         gather(v_s, tab_s[:].bitcast(U8))
         gather(v_w[1], tab_w[1][:].bitcast(U32))
-        gates = {u: gate_of(u) for u in range(EARLY_GATES)}
-        cast_w1(0, 0, 0, nc.vector.tensor_copy)
+        gates = {}
+        cast_w1(0, 0, 0, nc.vector.tensor_copy, 0, 80)
+        cast_w1(0, 0, 0, nc.scalar.copy, 80, 128)
         quant_w1(0, 0)
-        cast_w1(0, 1, 0, nc.vector.tensor_copy)
-        quant_w1(0, 1)
-        cast_w1(1, 0, 0, nc.vector.tensor_copy)
+        pair = kept([P, 2, BANK], F32, "gates0", "w1_raw00_0")
+        for i in range(2):
+            gates[0 + i] = gate_of(0 + i, pair[:, i, :])
+        cast_w1(0, 1, 0, nc.vector.tensor_copy, 0, 88)
+        cast_w1(0, 1, 0, nc.scalar.copy, 88, 128)
+        quant_w1(0, 1, 0, PACK // 2)
+        quant_w1(0, 1, PACK // 2, PACK)
+        pair = kept([P, 2, BANK], F32, "gates2", "w1_raw01_0")
+        for i in range(2):
+            gates[2 + i] = gate_of(2 + i, pair[:, i, :])
+        cast_w1(1, 0, 0, nc.vector.tensor_copy, 0, 128)
         quant_w1(1, 0)
-        cast_w1(1, 1, 0, nc.vector.tensor_copy)
-        cast_w1(1, 1, R // 2, nc.vector.tensor_copy)
+        cast_w1(1, 1, 0, nc.vector.tensor_copy, 0, 64)
+        for chunk in range(S // CHUNK):
+            hidden(0, chunk, on_vector=chunk in [])
+        cast_w1(1, 1, 256, nc.vector.tensor_copy, 0, 64)
         quant_w1(1, 1, 0, PACK // 2)
         quant_w1(1, 1, PACK // 2, PACK)
-        for chunk in range(S // CHUNK):
-            hidden(0, chunk)
 
-        first_banks = [take(), take()]
+        first_banks = [take() for chunk in range(6)]
         for a in range(PASSES):
             for chunk, bank in enumerate(first_banks):
                 hidden_pass(1, chunk, bank, a)
-        nc.scalar.activation(*relu_views(1, 0, first_banks[0]), ACT.Relu)
-        nc.vector.tensor_scalar_max(*relu_views(1, 1, first_banks[1]), 0.0)
+        for chunk, bank in enumerate(first_banks):
+            if chunk in [0]:
+                nc.vector.tensor_scalar_max(*relu_views(1, chunk, bank), 0.0)
+            else:
+                nc.scalar.activation(*relu_views(1, chunk, bank), ACT.Relu)
         cast_w4(0)
         quant_h(1, 0)
         quant_w4(0)
         quant_h(0, 0)
         quant_h(0, 2)
-        hidden(1, 2)
-        hidden(1, 3, on_vector=True)
+        for chunk in range(6, 4):
+            hidden(1, chunk, on_vector=chunk in [0])
 
         diff0, minus0 = take(), take()
         for i, (nt, j, cols) in enumerate(blocks(0)):
@@ -344,10 +358,10 @@ def tile_list_candidate_expert_blend_kernel(
             mx(diff0[:, cols], w4_cols(nt), h_cols(1, j, SPAN), False, i == 1)
         for nt, j, cols in halves(0):
             mx(minus0[:, cols], w4_cols(nt), h_cols(1, j, SPAN), True, True)
-        for chunk in range(2 * SPAN // CHUNK, S // CHUNK):
-            hidden(1, chunk)
+        for chunk in range(max(6, 2 * SPAN // CHUNK), S // CHUNK):
+            hidden(1, chunk, on_vector=chunk in [0])
         gated0 = held("gated0", 1)
-        nc.vector.tensor_tensor(gated0[:], diff0[:], gates[0][:], ALU.mult)
+        nc.vector.tensor_tensor(gated0[:], diff0[:], gates[0], ALU.mult)
         quant_h(1, 1)
         blend0 = unit_buffer(0, "blend0")
         nc.vector.tensor_tensor(blend0[:], gated0[:], minus0[:], ALU.subtract)

@@ -71,17 +71,18 @@ def tile_list_candidate_expert_blend_kernel(
         w4_s = kept([P, N], U8, "w4_s")
         h_spans = {(0, 0): 2, (0, 2): 2, (1, 0): 1, (1, 1): 1, (1, 2): 1, (1, 3): 1}
         h_bf = {key: kept([P, n * SPAN, PACK], BF16, "h_bf%d%d" % key) for key, n in h_spans.items()}
-        h_c = {key: kept([P, n * SPAN], U32, "h_c%d%d" % key, "w1_bf11" if key == (0, 0) else None) for key, n in h_spans.items()}
+        h_c = {key: kept([P, n * SPAN], U32, "h_c%d%d" % key, {(0, 0): "w1_raw10_0", (0, 2): "w1_bf11"}.get(key)) for key, n in h_spans.items()}
         h_s = {key: kept([P, n * SPAN], U8, "h_s%d%d" % key) for key, n in h_spans.items()}
         banks = [psum.tile([P, BANK], F32, name="bank%d" % b) for b in range(BANKS)]
         cache = [kept([P, T2], F32, "cache%d" % nt) for nt in range(ROW_TILES)]
         identity = kept([P, P], F32, "identity")
         warm = kept([P, 2], F32, "warm")
 
-        nc.gpsimd.memset(tab_s[:], 0)
+        nc.vector.memset(tab_s[:], 0)
+        nc.vector.memset(cache[ROW_TILES - 1][:], 0.0)
         nc.gpsimd.memset(w_s[:], 0)
         make_identity(nc, identity[:])
-        for nt in range(ROW_TILES):
+        for nt in range(ROW_TILES - 1):
             nc.gpsimd.memset(cache[nt][:], 0.0)
         nc.vector.memset(warm[:, 0:1], 0.0)
         nc.scalar.activation(warm[:, 1:2], warm[:, 0:1], ACT.Sigmoid)
@@ -102,24 +103,32 @@ def tile_list_candidate_expert_blend_kernel(
             cols = w4[:, u * (N // 2) : (u + 1) * (N // 2)]
             nc.sync.dma_start(out=w4_raw[u][:], in_=cols.rearrange("(p j) c -> p j c", j=PACK))
 
+        def load_w1(e, a, c0):
+            rows = w1[a * P * PACK : (a + 1) * P * PACK, e * R + c0 : e * R + c0 + w1_parts[e, a, c0]]
+            nc.sync.dma_start(out=w1_raw[e, a, c0][:], in_=rows.rearrange("(p j) c -> p j c", j=PACK))
+
+        def load_gain(half):
+            cols = slice(half * (S // 2), (half + 1) * (S // 2))
+            nc.sync.dma_start(out=gain[:, cols], in_=wgo[:, cols])
+
         load_table(0)
         nc.sync.dma_start(idx[:], offs)
         load_planes(tab_s[:], tab_scales)
-        load_table(1)
+        load_w1(0, 0, 0)
+        load_planes(w_s[:, 1, :], w3_scales)
+        load_w1(0, 1, 0)
         load_planes(w_s[:, 0, :], wg_scales)
+        load_table(1)
+        load_w1(1, 0, 0)
         load_wg(0)
-        for (e, a, c0), cols in w1_parts.items():
-            rows = w1[a * P * PACK : (a + 1) * P * PACK, e * R + c0 : e * R + c0 + cols]
-            nc.sync.dma_start(out=w1_raw[e, a, c0][:], in_=rows.rearrange("(p j) c -> p j c", j=PACK))
-            if (e, a) == (0, 0):
-                load_planes(w_s[:, 1, :], w3_scales)
+        load_w1(1, 1, 0)
+        load_w1(1, 1, R // 2)
         load_w4(0)
         nc.sync.dma_start(out=w3_w[:], in_=w3_words[0].bitcast(I32))
         load_w4(1)
         nc.sync.dma_start(idx2[:], offs2)
-        for half in range(2):
-            cols = slice(half * (S // 2), (half + 1) * (S // 2))
-            nc.sync.dma_start(out=gain[:, cols], in_=wgo[:, cols])
+        load_gain(0)
+        load_gain(1)
         load_wg(1)
 
         taken = []
@@ -131,9 +140,9 @@ def tile_list_candidate_expert_blend_kernel(
         def entries(lst, j0, j1):
             return lst[:, j0 // LIST_ROWS : j1 // LIST_ROWS]
 
-        def gather(dst, window):
-            for j0 in range(0, S, S // 2):
-                j1 = j0 + S // 2
+        def gather(dst, window, width=S // 2):
+            for j0 in range(0, S, width):
+                j1 = j0 + width
                 nc.vector.tensor_copy(out=dst[:, j0:j1], in_=window.indirect(entries(idx, j0, j1)))
 
         def cast_w1(e, a, c0, copy, m0=0, m1=None):
@@ -148,9 +157,12 @@ def tile_list_candidate_expert_blend_kernel(
                 in_=w1_bf[e, a][:, t0:t1].rearrange("p t m j -> p (t m j)"),
             )
 
-        def cast_w4(u):
+        def cast_w4(u, share):
             dst = w4_bf[:, u * (N // 2) : (u + 1) * (N // 2), :].rearrange("p (c i) j -> p c j i", i=4)
-            nc.vector.tensor_scalar_mul(dst, w4_raw[u][:].rearrange("p j (c i) -> p c j i", i=4), -1.0)
+            src = w4_raw[u][:].rearrange("p j (c i) -> p c j i", i=4)
+            nc.vector.tensor_scalar_mul(dst[:, :share], src[:, :share], -1.0)
+            if share < src.shape[1]:
+                nc.scalar.mul(dst[:, share:], src[:, share:], -1.0)
 
         def quant_w4(u):
             cols = slice(u * (N // 2), (u + 1) * (N // 2))
@@ -221,7 +233,7 @@ def tile_list_candidate_expert_blend_kernel(
         def blocks(u):
             return [(nt, j + c, slice(cols.start + c, cols.start + c + P)) for nt, j, cols in halves(u) for c in range(0, SPAN, P)]
 
-        def gate_of(u, gate=None):
+        def gate_of(u):
             bank = take()
             parts = blocks(u) if u else halves(u)
             for a in range(PASSES):
@@ -229,8 +241,8 @@ def tile_list_candidate_expert_blend_kernel(
                     weights, values = wg_cols(nt, a), v_cols(a, j, BANK // len(parts))
                     opens, closes = a == 0 and i == 0, a == PASSES - 1 and i == len(parts) - 1
                     mx(bank[:, cols], *((values, weights) if u else (weights, values)), opens, closes)
-            gate = held("gate", 3)[:] if gate is None else gate
-            nc.scalar.activation(gate, bank[:], ACT.Sigmoid)
+            gate = held("gate", EARLY_GATES + 1)
+            nc.scalar.activation(gate[:], bank[:], ACT.Sigmoid)
             return gate
 
         def turn_over(tiles):
@@ -277,7 +289,7 @@ def tile_list_candidate_expert_blend_kernel(
 
         def gated_term(u, engine, diff):
             gated = unit_buffer(u, "gated")
-            engine.tensor_tensor(gated[:], diff[:], gates[u], ALU.mult)
+            engine.tensor_tensor(gated[:], diff[:], gates[u][:], ALU.mult)
             return gated
 
         def scatter(nt, j, width, values, fused=False):
@@ -310,46 +322,42 @@ def tile_list_candidate_expert_blend_kernel(
 
         gather(v_w[0], tab_w[0][:].bitcast(U32))
         gather(v_s, tab_s[:].bitcast(U8))
-        gather(v_w[1], tab_w[1][:].bitcast(U32))
         gates = {}
-        cast_w1(0, 0, 0, nc.vector.tensor_copy, 0, 80)
-        cast_w1(0, 0, 0, nc.scalar.copy, 80, 128)
+        cast_w1(0, 0, 0, nc.vector.tensor_copy, 0, 48)
+        cast_w1(0, 0, 0, nc.scalar.copy, 48, 128)
         quant_w1(0, 0)
-        pair = kept([P, 2, BANK], F32, "gates0", "w1_raw00_0")
-        for i in range(2):
-            gates[0 + i] = gate_of(0 + i, pair[:, i, :])
         cast_w1(0, 1, 0, nc.vector.tensor_copy, 0, 88)
         cast_w1(0, 1, 0, nc.scalar.copy, 88, 128)
         quant_w1(0, 1, 0, PACK // 2)
         quant_w1(0, 1, PACK // 2, PACK)
-        pair = kept([P, 2, BANK], F32, "gates2", "w1_raw01_0")
-        for i in range(2):
-            gates[2 + i] = gate_of(2 + i, pair[:, i, :])
+        gather(v_w[1], tab_w[1][:].bitcast(U32), SPAN)
         cast_w1(1, 0, 0, nc.vector.tensor_copy, 0, 128)
         quant_w1(1, 0)
         cast_w1(1, 1, 0, nc.vector.tensor_copy, 0, 64)
         for chunk in range(S // CHUNK):
             hidden(0, chunk, on_vector=chunk in [])
+        quant_h(0, 0)
         cast_w1(1, 1, 256, nc.vector.tensor_copy, 0, 64)
         quant_w1(1, 1, 0, PACK // 2)
         quant_w1(1, 1, PACK // 2, PACK)
 
-        first_banks = [take() for chunk in range(6)]
+        for u in range(2):
+            gates[u] = gate_of(u)
+        first_banks = [take() for chunk in range(7)]
         for a in range(PASSES):
             for chunk, bank in enumerate(first_banks):
                 hidden_pass(1, chunk, bank, a)
         for chunk, bank in enumerate(first_banks):
-            if chunk in [0]:
+            if chunk in [1]:
                 nc.vector.tensor_scalar_max(*relu_views(1, chunk, bank), 0.0)
             else:
                 nc.scalar.activation(*relu_views(1, chunk, bank), ACT.Relu)
-        cast_w4(0)
+        cast_w4(0, 32)
         quant_h(1, 0)
         quant_w4(0)
-        quant_h(0, 0)
         quant_h(0, 2)
-        for chunk in range(6, 4):
-            hidden(1, chunk, on_vector=chunk in [0])
+        for chunk in range(7, 4):
+            hidden(1, chunk, on_vector=chunk in [1])
 
         diff0, minus0 = take(), take()
         for i, (nt, j, cols) in enumerate(blocks(0)):
@@ -358,19 +366,19 @@ def tile_list_candidate_expert_blend_kernel(
             mx(diff0[:, cols], w4_cols(nt), h_cols(1, j, SPAN), False, i == 1)
         for nt, j, cols in halves(0):
             mx(minus0[:, cols], w4_cols(nt), h_cols(1, j, SPAN), True, True)
-        for chunk in range(max(6, 2 * SPAN // CHUNK), S // CHUNK):
-            hidden(1, chunk, on_vector=chunk in [0])
+        for chunk in range(max(7, 2 * SPAN // CHUNK), S // CHUNK):
+            hidden(1, chunk, on_vector=chunk in [1])
         gated0 = held("gated0", 1)
-        nc.vector.tensor_tensor(gated0[:], diff0[:], gates[0], ALU.mult)
+        nc.vector.tensor_tensor(gated0[:], diff0[:], gates[0][:], ALU.mult)
         quant_h(1, 1)
+        quant_h(1, 2)
         blend0 = unit_buffer(0, "blend0")
         nc.vector.tensor_tensor(blend0[:], gated0[:], minus0[:], ALU.subtract)
-        cast_w4(1)
+        cast_w4(1, 64)
 
         diff1, minus1 = turned_banks(1)
         second1 = second_term(minus1)
         terms = {1: (second1, gated_term(1, nc.vector, diff1))}
-        quant_h(1, 2)
         quant_w4(1)
         quant_h(1, 3)
         weighted0 = [kept([P, SPAN], F32, "weighted0a"), kept([P, SPAN], F32, "weighted0b", "h_bf13")]

@@ -74,7 +74,7 @@ def tile_list_candidate_expert_blend_kernel(
         h_c = {key: kept([P, n * SPAN], U32, "h_c%d%d" % key, {(0, 0): "w1_raw10_0", (0, 2): "w1_bf11"}.get(key)) for key, n in h_spans.items()}
         h_s = {key: kept([P, n * SPAN], U8, "h_s%d%d" % key) for key, n in h_spans.items()}
         banks = [psum.tile([P, BANK], F32, name="bank%d" % b) for b in range(BANKS)]
-        cache = [kept([P, T2], F32, "cache%d" % nt) for nt in range(ROW_TILES)]
+        cache = [kept([P, T2], F32, "cache%d" % nt, {2: "w1_bf00"}.get(nt)) for nt in range(ROW_TILES)]
         identity = kept([P, P], F32, "identity")
         warm = kept([P, 2], F32, "warm")
 
@@ -82,7 +82,7 @@ def tile_list_candidate_expert_blend_kernel(
         nc.vector.memset(cache[ROW_TILES - 1][:], 0.0)
         nc.gpsimd.memset(w_s[:], 0)
         make_identity(nc, identity[:])
-        for nt in range(ROW_TILES - 1):
+        for nt in range(2):
             nc.gpsimd.memset(cache[nt][:], 0.0)
         nc.vector.memset(warm[:, 0:1], 0.0)
         nc.scalar.activation(warm[:, 1:2], warm[:, 0:1], ACT.Sigmoid)
@@ -90,9 +90,9 @@ def tile_list_candidate_expert_blend_kernel(
         def load_table(a):
             nc.sync.dma_start(out=tab_w[a][:], in_=tab_words[a].rearrange("p t i -> p (t i)").bitcast(I32))
 
-        def load_planes(dst, scales):
+        def load_planes(dst, scales, quads=range(QUADS)):
             rows = 4 * scales.shape[0]
-            for q in range(QUADS):
+            for q in quads:
                 nc.sync.dma_start(out=dst[32 * q : 32 * q + rows], in_=scales[:, 4 * q : 4 * q + 4, :].bitcast(I32))
 
         def load_wg(u):
@@ -113,13 +113,14 @@ def tile_list_candidate_expert_blend_kernel(
 
         load_table(0)
         nc.sync.dma_start(idx[:], offs)
-        load_planes(tab_s[:], tab_scales)
         load_w1(0, 0, 0)
-        load_planes(w_s[:, 1, :], w3_scales)
+        load_planes(tab_s[:], tab_scales)
         load_w1(0, 1, 0)
-        load_planes(w_s[:, 0, :], wg_scales)
+        load_planes(w_s[:, 1, :], w3_scales, (0, 1))
         load_table(1)
+        load_planes(w_s[:, 0, :], wg_scales)
         load_w1(1, 0, 0)
+        load_planes(w_s[:, 1, :], w3_scales, (2, 3))
         load_wg(0)
         load_w1(1, 1, 0)
         load_w1(1, 1, R // 2)
@@ -321,13 +322,14 @@ def tile_list_candidate_expert_blend_kernel(
                 scatter(nt1, j1, SPAN, weighted[:, cols1])
 
         gather(v_w[0], tab_w[0][:].bitcast(U32))
-        gather(v_s, tab_s[:].bitcast(U8))
         gates = {}
-        cast_w1(0, 0, 0, nc.vector.tensor_copy, 0, 48)
-        cast_w1(0, 0, 0, nc.scalar.copy, 48, 128)
+        cast_w1(0, 0, 0, nc.vector.tensor_copy, 0, 80)
+        cast_w1(0, 0, 0, nc.scalar.copy, 80, 128)
         quant_w1(0, 0)
-        cast_w1(0, 1, 0, nc.vector.tensor_copy, 0, 88)
-        cast_w1(0, 1, 0, nc.scalar.copy, 88, 128)
+        nc.gpsimd.memset(cache[2][:], 0.0)
+        gather(v_s, tab_s[:].bitcast(U8))
+        cast_w1(0, 1, 0, nc.vector.tensor_copy, 0, 56)
+        cast_w1(0, 1, 0, nc.scalar.copy, 56, 128)
         quant_w1(0, 1, 0, PACK // 2)
         quant_w1(0, 1, PACK // 2, PACK)
         gather(v_w[1], tab_w[1][:].bitcast(U32), SPAN)

@@ -56,7 +56,7 @@ def tile_list_candidate_expert_blend_kernel(
         v_w = [kept([P, S], U32, "v_w%d" % a) for a in range(PASSES)]
         v_s = kept([P, S], U8, "v_s")
         wg_w = [kept([P, PASSES, N // 2], I32, "wg_w%d" % u) for u in range(2)]
-        w_s = kept([P, 2, N // 4], I32, "w_s")
+        w_s = kept([P, PASSES + 1, N // 4], I32, "w_s")
         w3_w = kept([P, 2 * N // 4], I32, "w3_w")
         gain = kept([P, S], F32, "gain")
         w1_parts = {(0, 0, 0): R, (0, 1, 0): R, (1, 0, 0): R, (1, 1, 0): R // 2, (1, 1, R // 2): R // 2}
@@ -95,6 +95,11 @@ def tile_list_candidate_expert_blend_kernel(
             for q in quads:
                 nc.sync.dma_start(out=dst[32 * q : 32 * q + rows], in_=scales[:, 4 * q : 4 * q + 4, :].bitcast(I32))
 
+        def load_rows(first, scales, rows=range(4)):
+            planes = slice(first, first + scales.shape[0])
+            for r in rows:
+                nc.sync.dma_start(out=w_s[r:P:32, planes, :], in_=scales[:, r:16:4, :].rearrange("a q n -> q a n").bitcast(I32))
+
         def load_wg(u):
             cols = slice(u * (N // 2), (u + 1) * (N // 2))
             nc.sync.dma_start(out=wg_w[u][:], in_=wg_words[:, :, cols, :].rearrange("a p e i -> p a (e i)").bitcast(I32))
@@ -116,11 +121,11 @@ def tile_list_candidate_expert_blend_kernel(
         load_w1(0, 0, 0)
         load_planes(tab_s[:], tab_scales)
         load_w1(0, 1, 0)
-        load_planes(w_s[:, 1, :], w3_scales, (0, 1))
+        load_rows(PASSES, w3_scales, (0, 1))
         load_table(1)
-        load_planes(w_s[:, 0, :], wg_scales)
+        load_rows(0, wg_scales)
         load_w1(1, 0, 0)
-        load_planes(w_s[:, 1, :], w3_scales, (2, 3))
+        load_rows(PASSES, w3_scales, (2, 3))
         load_wg(0)
         load_w1(1, 1, 0)
         load_w1(1, 1, R // 2)
@@ -185,14 +190,14 @@ def tile_list_candidate_expert_blend_kernel(
 
         def w3_cols(nt):
             codes = w3_w[:].bitcast(U8)[:, 2 * nt * P : 2 * (nt + 1) * P].bitcast(FP4X4)
-            return codes, w_s[:, 1, :].bitcast(U8)[:, nt * P : (nt + 1) * P]
+            return codes, w_s[:, PASSES, :].bitcast(U8)[:, nt * P : (nt + 1) * P]
 
         def w4_cols(nt):
             return w4_c[:, nt * P : (nt + 1) * P].bitcast(FP8X4), w4_s[:, nt * P : (nt + 1) * P]
 
         def wg_cols(nt, a):
             codes = wg_w[nt // 2][:, a, nt % 2 * P : (nt % 2 + 1) * P].bitcast(FP8X4)
-            return codes, w_s[4 * a : P, 0, :].bitcast(U8)[:, nt * P : (nt + 1) * P]
+            return codes, w_s[:, a, :].bitcast(U8)[:, nt * P : (nt + 1) * P]
 
         def h_cols(e, j0, width):
             key, j = h_place(e, j0)
@@ -327,7 +332,7 @@ def tile_list_candidate_expert_blend_kernel(
         cast_w1(0, 0, 0, nc.scalar.copy, 80, 128)
         quant_w1(0, 0)
         nc.gpsimd.memset(cache[2][:], 0.0)
-        gather(v_s, tab_s[:].bitcast(U8))
+        gather(v_s, tab_s[:].bitcast(U8), SPAN)
         cast_w1(0, 1, 0, nc.vector.tensor_copy, 0, 56)
         cast_w1(0, 1, 0, nc.scalar.copy, 56, 128)
         quant_w1(0, 1, 0, PACK // 2)

@@ -28,8 +28,13 @@ SPAN = BANK // 2
 SPANS = S // SPAN
 ROW_TILES = N // P
 SUMMED_UNITS = 6
-EARLY_GATES = 4
-VECTOR_SHARE = 96
+EARLY_GATES = 2
+GATE_BUFS = 5
+FIRST_SHARE = 80
+SECOND_SHARE = 56
+W4_SHARE = 32
+OPENED = 7
+VECTOR_CHUNK = 1
 TERM_BUFS = 4
 WEIGHTED_BUFS = 6
 
@@ -71,7 +76,8 @@ def tile_list_candidate_expert_blend_kernel(
         w4_s = kept([P, N], U8, "w4_s")
         h_spans = {(0, 0): 2, (0, 2): 2, (1, 0): 1, (1, 1): 1, (1, 2): 1, (1, 3): 1}
         h_bf = {key: kept([P, n * SPAN, PACK], BF16, "h_bf%d%d" % key) for key, n in h_spans.items()}
-        h_c = {key: kept([P, n * SPAN], U32, "h_c%d%d" % key, {(0, 0): "w1_raw10_0", (0, 2): "w1_bf11"}.get(key)) for key, n in h_spans.items()}
+        h_tenancy = {(0, 0): "w1_raw10_0", (0, 2): "w1_bf11"}
+        h_c = {key: kept([P, n * SPAN], U32, "h_c%d%d" % key, h_tenancy.get(key)) for key, n in h_spans.items()}
         h_s = {key: kept([P, n * SPAN], U8, "h_s%d%d" % key) for key, n in h_spans.items()}
         banks = [psum.tile([P, BANK], F32, name="bank%d" % b) for b in range(BANKS)]
         cache = [kept([P, T2], F32, "cache%d" % nt, {2: "w1_bf00"}.get(nt)) for nt in range(ROW_TILES)]
@@ -90,12 +96,12 @@ def tile_list_candidate_expert_blend_kernel(
         def load_table(a):
             nc.sync.dma_start(out=tab_w[a][:], in_=tab_words[a].rearrange("p t i -> p (t i)").bitcast(I32))
 
-        def load_planes(dst, scales, quads=range(QUADS)):
+        def load_planes(dst, scales):
             rows = 4 * scales.shape[0]
-            for q in quads:
+            for q in range(QUADS):
                 nc.sync.dma_start(out=dst[32 * q : 32 * q + rows], in_=scales[:, 4 * q : 4 * q + 4, :].bitcast(I32))
 
-        def load_rows(first, scales, rows=range(4)):
+        def load_rows(first, scales, rows):
             planes = slice(first, first + scales.shape[0])
             for r in rows:
                 nc.sync.dma_start(out=w_s[r:P:32, planes, :], in_=scales[:, r:16:4, :].rearrange("a q n -> q a n").bitcast(I32))
@@ -123,10 +129,11 @@ def tile_list_candidate_expert_blend_kernel(
         load_w1(0, 1, 0)
         load_rows(PASSES, w3_scales, (0, 1))
         load_table(1)
-        load_rows(0, wg_scales)
+        load_rows(0, wg_scales, (0, 1))
         load_w1(1, 0, 0)
-        load_rows(PASSES, w3_scales, (2, 3))
+        load_rows(0, wg_scales, (2, 3))
         load_wg(0)
+        load_rows(PASSES, w3_scales, (2, 3))
         load_w1(1, 1, 0)
         load_w1(1, 1, R // 2)
         load_w4(0)
@@ -151,9 +158,9 @@ def tile_list_candidate_expert_blend_kernel(
                 j1 = j0 + width
                 nc.vector.tensor_copy(out=dst[:, j0:j1], in_=window.indirect(entries(idx, j0, j1)))
 
-        def cast_w1(e, a, c0, copy, m0=0, m1=None):
-            src = w1_raw[e, a, c0][:].rearrange("p j (m t) -> p m j t", t=PACK)[:, m0:m1]
-            dst = w1_bf[e, a][:].rearrange("p t m j -> p m j t")[:, c0 // PACK + m0 : c0 // PACK + m0 + src.shape[1]]
+        def cast_w1(e, a, c0, copy, m0=0, m1=None, t0=0, t1=PACK):
+            src = w1_raw[e, a, c0][:].rearrange("p j (m t) -> p m j t", t=PACK)[:, m0:m1, :, t0:t1]
+            dst = w1_bf[e, a][:].rearrange("p t m j -> p m j t")[:, c0 // PACK + m0 : c0 // PACK + m0 + src.shape[1], :, t0:t1]
             copy(dst, src)
 
         def quant_w1(e, a, t0=0, t1=PACK):
@@ -163,7 +170,7 @@ def tile_list_candidate_expert_blend_kernel(
                 in_=w1_bf[e, a][:, t0:t1].rearrange("p t m j -> p (t m j)"),
             )
 
-        def cast_w4(u, share):
+        def cast_w4(u, share=N // 2 // 4):
             dst = w4_bf[:, u * (N // 2) : (u + 1) * (N // 2), :].rearrange("p (c i) j -> p c j i", i=4)
             src = w4_raw[u][:].rearrange("p j (c i) -> p c j i", i=4)
             nc.vector.tensor_scalar_mul(dst[:, :share], src[:, :share], -1.0)
@@ -220,15 +227,18 @@ def tile_list_candidate_expert_blend_kernel(
             key, j = h_place(e, chunk * CHUNK)
             return h_bf[key][:, j : j + CHUNK, :], bank[:].rearrange("p (t n) -> p n t", t=PACK)
 
-        def hidden(e, chunk, on_vector=False):
+        def relu(e, chunk, bank):
+            if (e, chunk) == (1, VECTOR_CHUNK):
+                nc.vector.tensor_scalar_max(*relu_views(e, chunk, bank), 0.0)
+            else:
+                nc.scalar.activation(*relu_views(e, chunk, bank), ACT.Relu)
+
+        def hidden(e, chunk):
             bank = take()
             order = (1, 0) if e else (0, 1)
             for a in order:
                 hidden_pass(e, chunk, bank, a, order)
-            if on_vector:
-                nc.vector.tensor_scalar_max(*relu_views(e, chunk, bank), 0.0)
-            else:
-                nc.scalar.activation(*relu_views(e, chunk, bank), ACT.Relu)
+            relu(e, chunk, bank)
 
         units = [((0, s), (1, s)) for s in range(SPANS)] + [((nt, s), (nt, s + 1)) for s in (0, 2) for nt in (2, 3)]
         last = len(units) - 1
@@ -247,7 +257,7 @@ def tile_list_candidate_expert_blend_kernel(
                     weights, values = wg_cols(nt, a), v_cols(a, j, BANK // len(parts))
                     opens, closes = a == 0 and i == 0, a == PASSES - 1 and i == len(parts) - 1
                     mx(bank[:, cols], *((values, weights) if u else (weights, values)), opens, closes)
-            gate = held("gate", EARLY_GATES + 1)
+            gate = held("gate", GATE_BUFS)
             nc.scalar.activation(gate[:], bank[:], ACT.Sigmoid)
             return gate
 
@@ -328,43 +338,39 @@ def tile_list_candidate_expert_blend_kernel(
 
         gather(v_w[0], tab_w[0][:].bitcast(U32))
         gates = {}
-        cast_w1(0, 0, 0, nc.vector.tensor_copy, 0, 80)
-        cast_w1(0, 0, 0, nc.scalar.copy, 80, 128)
+        cast_w1(0, 0, 0, nc.vector.tensor_copy, 0, FIRST_SHARE)
+        cast_w1(0, 0, 0, nc.scalar.copy, FIRST_SHARE)
         quant_w1(0, 0)
         nc.gpsimd.memset(cache[2][:], 0.0)
         gather(v_s, tab_s[:].bitcast(U8), SPAN)
-        cast_w1(0, 1, 0, nc.vector.tensor_copy, 0, 56)
-        cast_w1(0, 1, 0, nc.scalar.copy, 56, 128)
+        cast_w1(0, 1, 0, nc.vector.tensor_copy, 0, SECOND_SHARE)
+        cast_w1(0, 1, 0, nc.scalar.copy, SECOND_SHARE)
         quant_w1(0, 1, 0, PACK // 2)
         quant_w1(0, 1, PACK // 2, PACK)
         gather(v_w[1], tab_w[1][:].bitcast(U32), SPAN)
-        cast_w1(1, 0, 0, nc.vector.tensor_copy, 0, 128)
+        cast_w1(1, 0, 0, nc.vector.tensor_copy)
         quant_w1(1, 0)
-        cast_w1(1, 1, 0, nc.vector.tensor_copy, 0, 64)
+        cast_w1(1, 1, 0, nc.vector.tensor_copy)
         for chunk in range(S // CHUNK):
-            hidden(0, chunk, on_vector=chunk in [])
+            hidden(0, chunk)
         quant_h(0, 0)
-        cast_w1(1, 1, 256, nc.vector.tensor_copy, 0, 64)
+        for t in range(0, PACK, PACK // 2):
+            cast_w1(1, 1, R // 2, nc.vector.tensor_copy, t0=t, t1=t + PACK // 2)
         quant_w1(1, 1, 0, PACK // 2)
         quant_w1(1, 1, PACK // 2, PACK)
 
-        for u in range(2):
+        for u in range(EARLY_GATES):
             gates[u] = gate_of(u)
-        first_banks = [take() for chunk in range(7)]
+        first_banks = [take() for chunk in range(OPENED)]
         for a in range(PASSES):
             for chunk, bank in enumerate(first_banks):
                 hidden_pass(1, chunk, bank, a)
         for chunk, bank in enumerate(first_banks):
-            if chunk in [1]:
-                nc.vector.tensor_scalar_max(*relu_views(1, chunk, bank), 0.0)
-            else:
-                nc.scalar.activation(*relu_views(1, chunk, bank), ACT.Relu)
-        cast_w4(0, 32)
+            relu(1, chunk, bank)
+        cast_w4(0, W4_SHARE)
         quant_h(1, 0)
         quant_w4(0)
         quant_h(0, 2)
-        for chunk in range(7, 4):
-            hidden(1, chunk, on_vector=chunk in [1])
 
         diff0, minus0 = take(), take()
         for i, (nt, j, cols) in enumerate(blocks(0)):
@@ -373,15 +379,15 @@ def tile_list_candidate_expert_blend_kernel(
             mx(diff0[:, cols], w4_cols(nt), h_cols(1, j, SPAN), False, i == 1)
         for nt, j, cols in halves(0):
             mx(minus0[:, cols], w4_cols(nt), h_cols(1, j, SPAN), True, True)
-        for chunk in range(max(7, 2 * SPAN // CHUNK), S // CHUNK):
-            hidden(1, chunk, on_vector=chunk in [1])
+        for chunk in range(OPENED, S // CHUNK):
+            hidden(1, chunk)
         gated0 = held("gated0", 1)
         nc.vector.tensor_tensor(gated0[:], diff0[:], gates[0][:], ALU.mult)
         quant_h(1, 1)
         quant_h(1, 2)
         blend0 = unit_buffer(0, "blend0")
         nc.vector.tensor_tensor(blend0[:], gated0[:], minus0[:], ALU.subtract)
-        cast_w4(1, 64)
+        cast_w4(1)
 
         diff1, minus1 = turned_banks(1)
         second1 = second_term(minus1)

from contextlib import ExitStack

import concourse.mybir as mybir
from concourse.masks import make_identity

K, H, R, N, T, S, T2, P = 1024, 1024, 512, 512, 2048, 1024, 2048, 128
FLOPS = 2 * S * (K * H + K * N + 2 * R * N)

F32 = mybir.dt.float32
BF16 = mybir.dt.bfloat16
I32 = mybir.dt.int32
U32 = mybir.dt.uint32
U16 = mybir.dt.uint16
U8 = mybir.dt.uint8
FP8X4 = mybir.dt.float8_e4m3fn_x4
FP4X4 = mybir.dt.float4_e2m1fn_x4
ACT = mybir.ActivationFunctionType
ALU = mybir.AluOpType

PACK = 4
PASSES = K // (P * PACK)
QUADS = 4
LIST_ROWS = 16
BANK = 512
BANKS = 8
CHUNK = BANK // PACK
SPAN = BANK // 2
SPANS = S // SPAN
ROW_TILES = N // P
SUMMED_UNITS = 6
EARLY_GATES = 2
GATE_BUFS = 5
FIRST_SHARE = 80
SECOND_SHARE = 56
W4_SHARE = 32
OPENED = 7
VECTOR_CHUNK = 1
TERM_BUFS = 4
WEIGHTED_BUFS = 6


def tile_list_candidate_expert_blend_kernel(
    tc, tab_words, tab_scales, offs, w1, wg_words, wg_scales, w3_words, w3_scales, w4, wgo, offs2, out
):
    nc = tc.nc
    with ExitStack() as ctx:
        keep = ctx.enter_context(tc.tile_pool(name="keep", bufs=1))
        ring = ctx.enter_context(tc.tile_pool(name="ring", bufs=1))
        psum = ctx.enter_context(tc.psum_pool(name="psum", bufs=1))

        def kept(shape, dtype, name, tag=None):
            return keep.tile(shape, dtype, name=name, tag=tag or name, align_bytes=64)

        def held(name, bufs):
            return ring.tile([P, BANK], F32, name=name, bufs=bufs)

        idx = keep.tile([P, S // LIST_ROWS], U16, name="idx")
        idx2 = keep.tile([P, S // LIST_ROWS], U16, name="idx2")
        tab_w = [kept([P, T], I32, "tab_w%d" % a) for a in range(PASSES)]
        tab_s = kept([P, T // 4], I32, "tab_s")
        v_w = [kept([P, S], U32, "v_w%d" % a) for a in range(PASSES)]
        v_s = kept([P, S], U8, "v_s")
        wg_w = [kept([P, PASSES, N // 2], I32, "wg_w%d" % u) for u in range(2)]
        w_s = kept([P, PASSES + 1, N // 4], I32, "w_s")
        w3_w = kept([P, 2 * N // 4], I32, "w3_w")
        gain = kept([P, S], F32, "gain")
        w1_parts = {(0, 0, 0): R, (0, 1, 0): R, (1, 0, 0): R, (1, 1, 0): R // 2, (1, 1, R // 2): R // 2}
        w1_raw = {part: kept([P, PACK, cols], F32, "w1_raw%d%d_%d" % part) for part, cols in w1_parts.items()}
        pieces = [(e, a) for e in range(2) for a in range(PASSES)]
        w1_bf = {ea: kept([P, PACK, P, PACK], BF16, "w1_bf%d%d" % ea) for ea in pieces}
        w1_c = {ea: kept([P, R], U32, "w1_c%d%d" % ea) for ea in pieces}
        w1_s = {ea: kept([P, R], U8, "w1_s%d%d" % ea) for ea in pieces}
        w4_raw = [kept([P, PACK, N // 2], F32, "w4_raw%d" % u) for u in range(2)]
        w4_bf = kept([P, N, PACK], BF16, "w4_bf")
        w4_c = kept([P, N], U32, "w4_c")
        w4_s = kept([P, N], U8, "w4_s")
        h_spans = {(0, 0): 2, (0, 2): 2, (1, 0): 1, (1, 1): 1, (1, 2): 1, (1, 3): 1}
        h_bf = {key: kept([P, n * SPAN, PACK], BF16, "h_bf%d%d" % key) for key, n in h_spans.items()}
        h_tenancy = {(0, 0): "w1_raw10_0", (0, 2): "w1_bf11"}
        h_c = {key: kept([P, n * SPAN], U32, "h_c%d%d" % key, h_tenancy.get(key)) for key, n in h_spans.items()}
        h_s = {key: kept([P, n * SPAN], U8, "h_s%d%d" % key) for key, n in h_spans.items()}
        banks = [psum.tile([P, BANK], F32, name="bank%d" % b) for b in range(BANKS)]
        cache = [kept([P, T2], F32, "cache%d" % nt, {2: "w1_bf00"}.get(nt)) for nt in range(ROW_TILES)]
        identity = kept([P, P], F32, "identity")
        warm = kept([P, 2], F32, "warm")

        nc.vector.memset(tab_s[:], 0)
        nc.vector.memset(cache[ROW_TILES - 1][:], 0.0)
        nc.gpsimd.memset(w_s[:], 0)
        make_identity(nc, identity[:])
        for nt in range(2):
            nc.gpsimd.memset(cache[nt][:], 0.0)
        nc.vector.memset(warm[:, 0:1], 0.0)
        nc.scalar.activation(warm[:, 1:2], warm[:, 0:1], ACT.Sigmoid)

        def load_table(a):
            nc.sync.dma_start(out=tab_w[a][:], in_=tab_words[a].rearrange("p t i -> p (t i)").bitcast(I32))

        def load_planes(dst, scales):
            rows = 4 * scales.shape[0]
            for q in range(QUADS):
                nc.sync.dma_start(out=dst[32 * q : 32 * q + rows], in_=scales[:, 4 * q : 4 * q + 4, :].bitcast(I32))

        def load_rows(first, scales, rows):
            planes = slice(first, first + scales.shape[0])
            for r in rows:
                nc.sync.dma_start(out=w_s[r:P:32, planes, :], in_=scales[:, r:16:4, :].rearrange("a q n -> q a n").bitcast(I32))

        def load_wg(u):
            cols = slice(u * (N // 2), (u + 1) * (N // 2))
            nc.sync.dma_start(out=wg_w[u][:], in_=wg_words[:, :, cols, :].rearrange("a p e i -> p a (e i)").bitcast(I32))

        def load_w4(u):
            cols = w4[:, u * (N // 2) : (u + 1) * (N // 2)]
            nc.sync.dma_start(out=w4_raw[u][:], in_=cols.rearrange("(p j) c -> p j c", j=PACK))

        def load_w1(e, a, c0):
            rows = w1[a * P * PACK : (a + 1) * P * PACK, e * R + c0 : e * R + c0 + w1_parts[e, a, c0]]
            nc.sync.dma_start(out=w1_raw[e, a, c0][:], in_=rows.rearrange("(p j) c -> p j c", j=PACK))

        def load_gain(half):
            cols = slice(half * (S // 2), (half + 1) * (S // 2))
            nc.sync.dma_start(out=gain[:, cols], in_=wgo[:, cols])

        load_table(0)
        nc.sync.dma_start(idx[:], offs)
        load_w1(0, 0, 0)
        load_planes(tab_s[:], tab_scales)
        load_w1(0, 1, 0)
        load_rows(PASSES, w3_scales, (0, 1))
        load_table(1)
        load_rows(0, wg_scales, (0, 1))
        load_w1(1, 0, 0)
        load_rows(0, wg_scales, (2, 3))
        load_wg(0)
        load_rows(PASSES, w3_scales, (2, 3))
        load_w1(1, 1, 0)
        load_w1(1, 1, R // 2)
        load_w4(0)
        nc.sync.dma_start(out=w3_w[:], in_=w3_words[0].bitcast(I32))
        load_w4(1)
        nc.sync.dma_start(idx2[:], offs2)
        load_gain(0)
        load_gain(1)
        load_wg(1)

        taken = []

        def take():
            taken.append(banks[len(taken) % BANKS])
            return taken[-1]

        def entries(lst, j0, j1):
            return lst[:, j0 // LIST_ROWS : j1 // LIST_ROWS]

        def gather(dst, window, width=S // 2):
            for j0 in range(0, S, width):
                j1 = j0 + width
                nc.vector.tensor_copy(out=dst[:, j0:j1], in_=window.indirect(entries(idx, j0, j1)))

        def cast_w1(e, a, c0, copy, m0=0, m1=None, t0=0, t1=PACK):
            src = w1_raw[e, a, c0][:].rearrange("p j (m t) -> p m j t", t=PACK)[:, m0:m1, :, t0:t1]
            dst = w1_bf[e, a][:].rearrange("p t m j -> p m j t")[:, c0 // PACK + m0 : c0 // PACK + m0 + src.shape[1], :, t0:t1]
            copy(dst, src)

        def quant_w1(e, a, t0=0, t1=PACK):
            nc.vector.quantize_mx(
                out=w1_c[e, a][:, t0 * P : t1 * P].bitcast(FP8X4),
                scales=w1_s[e, a][:, t0 * P : t1 * P],
                in_=w1_bf[e, a][:, t0:t1].rearrange("p t m j -> p (t m j)"),
            )

        def cast_w4(u, share=N // 2 // 4):
            dst = w4_bf[:, u * (N // 2) : (u + 1) * (N // 2), :].rearrange("p (c i) j -> p c j i", i=4)
            src = w4_raw[u][:].rearrange("p j (c i) -> p c j i", i=4)
            nc.vector.tensor_scalar_mul(dst[:, :share], src[:, :share], -1.0)
            if share < src.shape[1]:
                nc.scalar.mul(dst[:, share:], src[:, share:], -1.0)

        def quant_w4(u):
            cols = slice(u * (N // 2), (u + 1) * (N // 2))
            nc.vector.quantize_mx(
                out=w4_c[:, cols].bitcast(FP8X4), scales=w4_s[:, cols], in_=w4_bf[:, cols, :].rearrange("p c j -> p (c j)")
            )

        def quant_h(e, s):
            nc.vector.quantize_mx(
                out=h_c[e, s][:].bitcast(FP8X4), scales=h_s[e, s][:], in_=h_bf[e, s][:].rearrange("p n t -> p (n t)")
            )

        def h_place(e, j):
            s0 = max(s for expert, s in h_spans if expert == e and s * SPAN <= j)
            return (e, s0), j - s0 * SPAN

        def w1_cols(e, a, t):
            return w1_c[e, a][:, t * P : (t + 1) * P].bitcast(FP8X4), w1_s[e, a][:, t * P : (t + 1) * P]

        def w3_cols(nt):
            codes = w3_w[:].bitcast(U8)[:, 2 * nt * P : 2 * (nt + 1) * P].bitcast(FP4X4)
            return codes, w_s[:, PASSES, :].bitcast(U8)[:, nt * P : (nt + 1) * P]

        def w4_cols(nt):
            return w4_c[:, nt * P : (nt + 1) * P].bitcast(FP8X4), w4_s[:, nt * P : (nt + 1) * P]

        def wg_cols(nt, a):
            codes = wg_w[nt // 2][:, a, nt % 2 * P : (nt % 2 + 1) * P].bitcast(FP8X4)
            return codes, w_s[:, a, :].bitcast(U8)[:, nt * P : (nt + 1) * P]

        def h_cols(e, j0, width):
            key, j = h_place(e, j0)
            return h_c[key][:, j : j + width].bitcast(FP8X4), h_s[key][:, j : j + width]

        def v_cols(a, j0, width):
            return v_w[a][:, j0 : j0 + width].bitcast(FP8X4), v_s[4 * a : P, j0 : j0 + width]

        def mx(dst, stationary, moving, start, stop):
            nc.tensor.matmul_mx(
                out=dst, lhsT=stationary[0], lhsT_scale=stationary[1], rhs=moving[0], rhs_scale=moving[1], start=start, stop=stop
            )

        def hidden_pass(e, chunk, bank, a, order=(0, 1)):
            for t in range(PACK):
                opens, closes = a == order[0] and t == 0, a == order[-1] and t == PACK - 1
                mx(bank[:, t * CHUNK : (t + 1) * CHUNK], w1_cols(e, a, t), v_cols(a, chunk * CHUNK, CHUNK), opens, closes)

        def relu_views(e, chunk, bank):
            key, j = h_place(e, chunk * CHUNK)
            return h_bf[key][:, j : j + CHUNK, :], bank[:].rearrange("p (t n) -> p n t", t=PACK)

        def relu(e, chunk, bank):
            if (e, chunk) == (1, VECTOR_CHUNK):
                nc.vector.tensor_scalar_max(*relu_views(e, chunk, bank), 0.0)
            else:
                nc.scalar.activation(*relu_views(e, chunk, bank), ACT.Relu)

        def hidden(e, chunk):
            bank = take()
            order = (1, 0) if e else (0, 1)
            for a in order:
                hidden_pass(e, chunk, bank, a, order)
            relu(e, chunk, bank)

        units = [((0, s), (1, s)) for s in range(SPANS)] + [((nt, s), (nt, s + 1)) for s in (0, 2) for nt in (2, 3)]
        last = len(units) - 1

        def halves(u):
            return [(nt, s * SPAN, slice(i * SPAN, (i + 1) * SPAN)) for i, (nt, s) in enumerate(units[u])]

        def blocks(u):
            return [(nt, j + c, slice(cols.start + c, cols.start + c + P)) for nt, j, cols in halves(u) for c in range(0, SPAN, P)]

        def gate_of(u):
            bank = take()
            parts = blocks(u) if u else halves(u)
            for a in range(PASSES):
                for i, (nt, j, cols) in enumerate(parts):
                    weights, values = wg_cols(nt, a), v_cols(a, j, BANK // len(parts))
                    opens, closes = a == 0 and i == 0, a == PASSES - 1 and i == len(parts) - 1
                    mx(bank[:, cols], *((values, weights) if u else (weights, values)), opens, closes)
            gate = held("gate", GATE_BUFS)
            nc.scalar.activation(gate[:], bank[:], ACT.Sigmoid)
            return gate

        def turn_over(tiles):
            bank = take()
            for i, tile in enumerate(tiles):
                for c in range(0, BANK, P):
                    opens, closes = i == 0 and c == 0, i == len(tiles) - 1 and c == BANK - P
                    nc.tensor.matmul(bank[:, c : c + P], tile[:, c : c + P], identity[:], start=opens, stop=closes, is_transpose=True)
            return bank

        def copy_out(name, bufs, bank):
            tile = held(name, bufs)
            nc.scalar.copy(tile[:], bank[:])
            return tile

        def second_term(bank):
            tile = held("second", TERM_BUFS)
            nc.scalar.activation(tile[:], bank[:], ACT.Copy, scale=-1.0)
            return tile

        def turned_banks(u):
            diff = take()
            for nt, j, cols in blocks(u):
                mx(diff[:, cols], h_cols(0, j, P), w3_cols(nt), True, False)
                mx(diff[:, cols], h_cols(1, j, P), w4_cols(nt), False, True)
            minus = take()
            for nt, j, cols in blocks(u):
                mx(minus[:, cols], h_cols(1, j, P), w4_cols(nt), True, True)
            return diff, minus

        def upright_terms(u):
            terms = []
            for e, weights in enumerate((w3_cols, w4_cols)):
                bank = take()
                for nt, j, cols in halves(u):
                    mx(bank[:, cols], weights(nt), h_cols(e, j, SPAN), True, True)
                terms.append(copy_out("upright", 2 * (len(units) - SUMMED_UNITS), bank))
            return terms

        buffer_tags = ("w4_raw0", "h_bf11")

        def unit_buffer(u, name):
            return kept([P, BANK], F32, name, buffer_tags[u % 2])

        def gated_term(u, engine, diff):
            gated = unit_buffer(u, "gated")
            engine.tensor_tensor(gated[:], diff[:], gates[u][:], ALU.mult)
            return gated

        def scatter(nt, j, width, values, fused=False):
            window = cache[nt][:].indirect(entries(idx2, j, j + width))
            if fused:
                nc.vector.tensor_tensor(window, values, gain[:, j : j + width], ALU.mult)
            else:
                nc.vector.tensor_copy(out=window, in_=values)
            if j + width == S:
                nc.sync.dma_start(out=out[nt * P : (nt + 1) * P, :], in_=cache[nt][:])

        def finish(u, terms):
            bank = turn_over(terms)
            summed = unit_buffer(u, "summed")
            nc.scalar.copy(summed[:], bank[:])
            (nt0, j0, cols0), (nt1, j1, cols1) = halves(u)
            if u == last:
                scatter(nt0, j0, BANK, summed[:], fused=True)
                return
            weighted = held("weighted", WEIGHTED_BUFS)
            if nt0 == nt1:
                nc.gpsimd.tensor_tensor(weighted[:], summed[:], gain[:, j0 : j0 + BANK], ALU.mult)
                scatter(nt0, j0, BANK, weighted[:])
            else:
                both = gain[:, j0 : j0 + SPAN].unsqueeze(1).to_broadcast([P, 2, SPAN])
                by_half = "p (r j) -> p r j"
                nc.gpsimd.tensor_tensor(weighted[:].rearrange(by_half, r=2), summed[:].rearrange(by_half, r=2), both, ALU.mult)
                scatter(nt0, j0, SPAN, weighted[:, cols0])
                scatter(nt1, j1, SPAN, weighted[:, cols1])

        gather(v_w[0], tab_w[0][:].bitcast(U32))
        gates = {}
        cast_w1(0, 0, 0, nc.vector.tensor_copy, 0, FIRST_SHARE)
        cast_w1(0, 0, 0, nc.scalar.copy, FIRST_SHARE)
        quant_w1(0, 0)
        nc.gpsimd.memset(cache[2][:], 0.0)
        gather(v_s, tab_s[:].bitcast(U8), SPAN)
        cast_w1(0, 1, 0, nc.vector.tensor_copy, 0, SECOND_SHARE)
        cast_w1(0, 1, 0, nc.scalar.copy, SECOND_SHARE)
        quant_w1(0, 1, 0, PACK // 2)
        quant_w1(0, 1, PACK // 2, PACK)
        gather(v_w[1], tab_w[1][:].bitcast(U32), SPAN)
        cast_w1(1, 0, 0, nc.vector.tensor_copy)
        quant_w1(1, 0)
        cast_w1(1, 1, 0, nc.vector.tensor_copy)
        for chunk in range(S // CHUNK):
            hidden(0, chunk)
        quant_h(0, 0)
        for t in range(0, PACK, PACK // 2):
            cast_w1(1, 1, R // 2, nc.vector.tensor_copy, t0=t, t1=t + PACK // 2)
        quant_w1(1, 1, 0, PACK // 2)
        quant_w1(1, 1, PACK // 2, PACK)

        for u in range(EARLY_GATES):
            gates[u] = gate_of(u)
        first_banks = [take() for chunk in range(OPENED)]
        for a in range(PASSES):
            for chunk, bank in enumerate(first_banks):
                hidden_pass(1, chunk, bank, a)
        for chunk, bank in enumerate(first_banks):
            relu(1, chunk, bank)
        cast_w4(0, W4_SHARE)
        quant_h(1, 0)
        quant_w4(0)
        quant_h(0, 2)

        diff0, minus0 = take(), take()
        for i, (nt, j, cols) in enumerate(blocks(0)):
            mx(diff0[:, cols], w3_cols(nt), h_cols(0, j, P), i == 0, False)
        for i, (nt, j, cols) in enumerate(halves(0)):
            mx(diff0[:, cols], w4_cols(nt), h_cols(1, j, SPAN), False, i == 1)
        for nt, j, cols in halves(0):
            mx(minus0[:, cols], w4_cols(nt), h_cols(1, j, SPAN), True, True)
        for chunk in range(OPENED, S // CHUNK):
            hidden(1, chunk)
        gated0 = held("gated0", 1)
        nc.vector.tensor_tensor(gated0[:], diff0[:], gates[0][:], ALU.mult)
        quant_h(1, 1)
        quant_h(1, 2)
        blend0 = unit_buffer(0, "blend0")
        nc.vector.tensor_tensor(blend0[:], gated0[:], minus0[:], ALU.subtract)
        cast_w4(1)

        diff1, minus1 = turned_banks(1)
        second1 = second_term(minus1)
        terms = {1: (second1, gated_term(1, nc.vector, diff1))}
        quant_w4(1)
        quant_h(1, 3)
        weighted0 = [kept([P, SPAN], F32, "weighted0a"), kept([P, SPAN], F32, "weighted0b", "h_bf13")]
        for tile, (nt, j, cols) in zip(weighted0, halves(0)):
            nc.vector.tensor_tensor(tile[:], blend0[:, cols], gain[:, j : j + SPAN], ALU.mult)
        for tile, (nt, j, cols) in zip(weighted0, halves(0)):
            scatter(nt, j, SPAN, tile[:])

        upright = {}
        for u in range(2, len(units)):
            if u not in gates:
                gates[u] = gate_of(u)
            if u < SUMMED_UNITS:
                diff_bank, minus_bank = turned_banks(u)
                diff = copy_out("diff", TERM_BUFS, diff_bank)
            else:
                diff = copy_out("diff", TERM_BUFS, turn_over(upright[u]))
                minus_bank = turn_over(upright[u][1:])
            terms[u] = (second_term(minus_bank), gated_term(u, nc.gpsimd, diff))
            if SUMMED_UNITS <= u + 2 <= last:
                upright[u + 2] = upright_terms(u + 2)
            finish(u - 1, terms[u - 1])
        finish(last, terms[last])
